import numpy as np
import ml_dtypes


def mxq(x, axis, fmt="e4m3"):
    dtype, down = {"e4m3": (ml_dtypes.float8_e4m3fn, 7), "e5m2": (ml_dtypes.float8_e5m2, 14)}[fmt]
    v = np.moveaxis(np.asarray(x, np.float32).astype(ml_dtypes.bfloat16).astype(np.float64), axis, -1)
    blocks = v.reshape(v.shape[:-1] + (-1, 32))
    amax = np.abs(blocks).max(-1, keepdims=True)
    byte = np.maximum(np.where(amax > 0, np.frexp(amax)[1] - 1 + 127, 0) - down, 1)
    scale = np.exp2(byte - 127.0)
    codes = (blocks / scale).astype(np.float32).astype(dtype).astype(np.float64)
    return np.moveaxis((codes * scale).reshape(v.shape), -1, axis)


WIDE = False


def mx_kscale(k):
    if not WIDE:
        return np.ones(k)
    levels = np.array([10, -10, 5, -5, 0])
    if k % 512:
        return np.exp2(np.random.permutation(np.resize(levels, k // 32))).repeat(32)
    a = np.empty((k // 512, 16))
    for p in range(k // 512):
        a[p, :8] = np.random.permutation(np.resize(levels, 8))
        for g in range(8):
            far = levels[np.abs(levels - a[p, g]) >= 10]
            a[p, g + 8] = far[np.random.randint(len(far))]
    return np.exp2(a.ravel()).repeat(32)


def f64(x):
    return np.asarray(x).astype(np.float64)


def striped(idx):
    return np.tile(idx.reshape(-1, 16).T, (8, 1)).astype(np.uint16)


def unstriped(offs):
    return offs[:16].T.reshape(-1).astype(np.int64)


E2M1 = np.array([0.0, 0.5, 1.0, 1.5, 2.0, 3.0, 4.0, 6.0, -0.0, -0.5, -1.0, -1.5, -2.0, -3.0, -4.0, -6.0])


def pack_fp4(w):
    k, n = w.shape
    w = f64(np.asarray(w, np.float32).astype(ml_dtypes.bfloat16)).reshape(k // 32, 32, n)
    amax = np.abs(w).max(1)
    mant, ex = np.frexp(amax / 6.0)
    byte = np.clip(np.where(amax > 0, np.where(mant > 0.5, ex, ex - 1) + 127, 1), 1, 254)
    scaled = (w * np.exp2(127.0 - byte)[:, None, :]).reshape(k, n).astype(np.float32)
    c = np.ascontiguousarray(scaled.reshape(k // 512, 128, 4, n).transpose(0, 1, 3, 2)).astype(ml_dtypes.float4_e2m1fn).view(np.uint8) & 0xF
    words = (c[..., 0::2] | (c[..., 1::2] << 4)).reshape(k // 512, 128, 2 * n)
    return np.ascontiguousarray(words), np.ascontiguousarray(byte.astype(np.uint8).reshape(k // 512, 16, n))


def unpack_fp4(words, scales):
    g, _, n = scales.shape
    words = np.ascontiguousarray(words).reshape(g, 128, n, 2)
    nib = np.empty((g, 128, n, 4), np.uint8)
    nib[..., 0::2] = words & 0xF
    nib[..., 1::2] = words >> 4
    vals = E2M1[nib] * np.repeat(np.exp2(scales.astype(np.float64) - 127.0), 8, axis=1)[..., None]
    return vals.transpose(0, 1, 3, 2).reshape(g * 512, n)


def silu(v):
    return v / (1.0 + np.exp(-np.maximum(v, -700.0)))


K, T, H, N, J, U = 1024, 1024, 512, 128, 512, 2048


def setup_inputs():
    n = np.random.standard_normal
    s = mx_kscale(K)[:, None]
    u = mx_kscale(H)
    r = mx_kscale(J)[:, None]
    packed_xT = pack_fp4(n((K, T)) * s)
    return {
        "x_words": packed_xT[0],
        "x_scales": packed_xT[1],
        "aT": (n((J, U)) * r).astype(np.float32),
        "w1": (n((K, H)) / np.sqrt(K) / s * u).astype(np.float32),
        "w3": (n((J, H)) / np.sqrt(J) / r).astype(np.float32),
        "w2": (n((H, N)) / np.sqrt(2 * H) / u[:, None]).astype(np.float32),
        "pos1": striped(np.random.permutation(T)),
        "pos2": striped(np.random.permutation(T)),
    }


def reference(x_words, x_scales, aT, w1, w3, w2, pos1, pos2):
    xq = unpack_fp4(x_words, x_scales)
    h = silu(mxq(f64(w1), 0, "e4m3").T @ xq)
    f = mxq(f64(w3), 0, "e4m3").T @ mxq(f64(aT), 0, "e4m3")
    z = h[:, unstriped(pos1)] * f[:, :T] + h[:, unstriped(pos2)] * f[:, T:2 * T]
    return mxq(f64(w2), 0, "e4m3").T @ mxq(z, 0, "e4m3")

@@ -1,0 +1,258 @@
+from contextlib import ExitStack
+
+import concourse.mybir as mybir
+
+K, T, H, N, J, U = 1024, 1024, 512, 128, 512, 2048
+FLOPS = 2 * (K * H * T + J * H * U + H * N * T)
+
+F32 = mybir.dt.float32
+BF16 = mybir.dt.bfloat16
+I32 = mybir.dt.int32
+U32 = mybir.dt.uint32
+U16 = mybir.dt.uint16
+U8 = mybir.dt.uint8
+FP8X4 = mybir.dt.float8_e4m3fn_x4
+FP4X4 = mybir.dt.float4_e2m1fn_x4
+SILU = mybir.ActivationFunctionType.Silu
+MULT = mybir.AluOpType.mult
+ADD = mybir.AluOpType.add
+
+P = 128
+PACK = 4
+BANK = 512
+CHUNK = 256
+CHUNKS = T // CHUNK
+LISTS = 2
+
+
+def tile_picked_wdime_none_l_kernel(
+    tc, x_words, x_scales, aT, w1, w3, w2, pos1, pos2, out
+):
+    nc = tc.nc
+    with ExitStack() as ctx:
+        keep = ctx.enter_context(tc.tile_pool(name="keep", bufs=1))
+        ring = ctx.enter_context(tc.tile_pool(name="ring", bufs=2))
+        psum = ctx.enter_context(tc.psum_pool(name="psum", bufs=8))
+
+        def held(shape, dtype, name):
+            return keep.tile(shape, dtype, name=name, align_bytes=64)
+
+        w1_raw = [held([P, PACK, H], F32, "w1_raw%d" % g) for g in range(2)]
+        x_codes = [held([P, 2 * T], U8, "x_codes%d" % g) for g in range(2)]
+        x_plane = held([P, 2, T], U8, "x_plane")
+        w3_raw = held([P, PACK, H], F32, "w3_raw")
+        w2_raw = held([P, PACK, N], F32, "w2_raw")
+        a_raw = [[held([P, PACK, CHUNK], F32, "a_raw%d_%d" % (c, d)) for d in range(LISTS)] for c in range(CHUNKS)]
+        lists = [keep.tile([P, T // 16], U16, name="list%d" % d) for d in range(LISTS)]
+
+        def load_a(c, d):
+            cols = slice(d * T + c * CHUNK, d * T + (c + 1) * CHUNK)
+            nc.sync.dma_start(out=a_raw[c][d][:], in_=aT[:, cols].rearrange("(p j) n -> p j n", j=PACK))
+
+        def load_w1(g):
+            nc.sync.dma_start(out=w1_raw[g][:], in_=w1[g * 512:(g + 1) * 512, :].rearrange("(p j) n -> p j n", j=PACK))
+
+        def load_x(g):
+            nc.sync.dma_start(out=x_codes[g][:].bitcast(I32), in_=x_words[g].bitcast(I32))
+
+        nc.gpsimd.memset(x_plane[:].bitcast(I32), 0)
+        warm_in = held([P, 1], F32, "warm_in")
+        warm_out = held([P, 1], F32, "warm_out")
+        nc.vector.memset(warm_in[:], 0.0)
+        nc.scalar.activation(warm_out[:], warm_in[:], SILU)
+
+        nc.sync.dma_start(out=w3_raw[:], in_=w3.rearrange("(p j) n -> p j n", j=PACK))
+        load_a(0, 0)
+        load_w1(0)
+        for quad in range(4):
+            nc.sync.dma_start(
+                out=x_plane[32 * quad:32 * quad + 4, :, :].bitcast(I32),
+                in_=x_scales[:, 4 * quad:4 * quad + 4, :].rearrange("g r n -> r g n").bitcast(I32),
+            )
+        load_x(0)
+        load_w1(1)
+        load_x(1)
+        nc.sync.dma_start(lists[0][:], pos1)
+        nc.sync.dma_start(lists[1][:], pos2)
+        load_a(0, 1)
+        load_a(1, 0)
+        load_a(1, 1)
+        w2_rows = w2.rearrange("(q t i) n -> i q t n", t=PACK, i=4)
+        for i in range(4):
+            nc.sync.dma_start(out=w2_raw[i:P:4, :, :], in_=w2_rows[i])
+        for c in range(2, CHUNKS):
+            load_a(c, 0)
+            load_a(c, 1)
+
+        def copy_on(engine, out_ap, in_ap):
+            if engine == "vector":
+                nc.vector.tensor_copy(out=out_ap, in_=in_ap)
+            else:
+                nc.scalar.copy(out=out_ap, in_=in_ap)
+
+        def quantise(grouped, name):
+            width = grouped.shape[1]
+            codes = held([P, width], U32, name + "_codes")
+            plane = held([P, width], U8, name + "_plane")
+            nc.vector.quantize_mx(
+                out=codes[:].bitcast(FP8X4), scales=plane[:], in_=grouped[:].rearrange("p w j -> p (w j)")
+            )
+            return codes, plane
+
+        def cast_weights(engine, raw, t0, tiles, name):
+            grouped = held([P, tiles * P, PACK], BF16, name + "_bf")
+            src = raw[:].rearrange("p j (q t c i) -> p t q c j i", t=PACK, c=2, i=2)
+            dst = grouped[:].rearrange("p (t q c i) j -> p t q c j i", t=tiles, c=2, i=2)
+            for t in range(tiles):
+                copy_on(engine, dst[:, t], src[:, t0 + t])
+            return grouped
+
+        def cast_columns(engine, raw, name):
+            width = raw.shape[2]
+            grouped = held([P, width, PACK], BF16, name + "_bf")
+            copy_on(
+                engine,
+                grouped[:].rearrange("p (c i) j -> p c j i", i=2),
+                raw[:].rearrange("p j (c i) -> p c j i", i=2),
+            )
+            return grouped
+
+        h = [held([P, T], F32, "h%d" % t) for t in range(PACK)]
+        h_banks = {}
+
+        def first_layer_pass(g, t, codes, plane, at):
+            if g == 0:
+                h_banks[t] = [psum.tile([P, BANK], F32, name="bank", tag="bank") for half in range(2)]
+            for half in range(2):
+                nc.tensor.matmul_mx(
+                    out=h_banks[t][half][:],
+                    lhsT=codes[:, at * P:(at + 1) * P].bitcast(FP8X4),
+                    lhsT_scale=plane[:, at * P:(at + 1) * P],
+                    rhs=x_codes[g][:, 2 * half * BANK:2 * (half + 1) * BANK].bitcast(FP4X4),
+                    rhs_scale=x_plane[:, g, half * BANK:(half + 1) * BANK],
+                    start=(g == 0),
+                    stop=(g == 1),
+                )
+
+        def activate(t):
+            for half in range(2):
+                nc.scalar.activation(h[t][:, half * BANK:(half + 1) * BANK], h_banks[t][half][:], SILU)
+
+        w3_q = {}
+        a_q = {}
+        f = {}
+
+        def filters(c, d, u):
+            if (c, d) not in f:
+                f[(c, d)] = ring.tile([P, PACK, CHUNK], F32, name="f%d" % d, tag="f%d" % d, bufs=3)
+            bank = psum.tile([P, BANK], F32, name="bank", tag="bank")
+            w_codes, w_plane = w3_q[u]
+            a_codes, a_plane = a_q[(c, d)]
+            for e in range(2):
+                nc.tensor.matmul_mx(
+                    out=bank[:, e * CHUNK:(e + 1) * CHUNK],
+                    lhsT=w_codes[:, e * P:(e + 1) * P].bitcast(FP8X4),
+                    lhsT_scale=w_plane[:, e * P:(e + 1) * P],
+                    rhs=a_codes[:].bitcast(FP8X4),
+                    rhs_scale=a_plane[:],
+                    start=True,
+                    stop=True,
+                )
+            nc.scalar.copy(out=f[(c, d)][:, 2 * u:2 * u + 2, :].rearrange("p e n -> p (e n)"), in_=bank[:])
+
+        w3_bf0 = cast_weights("vector", w3_raw, 0, 2, "w3_0")
+        w3_bf1 = cast_weights("scalar", w3_raw, 2, 2, "w3_1")
+        w3_q[0] = quantise(w3_bf0, "w3_0")
+        a_bf00 = cast_columns("vector", a_raw[0][0], "a0_0")
+        w3_q[1] = quantise(w3_bf1, "w3_1")
+        a_q[(0, 0)] = quantise(a_bf00, "a0_0")
+        filters(0, 0, 0)
+        filters(0, 0, 1)
+
+        for g in range(2):
+            w1_bf = [
+                cast_weights("vector" if t < 2 else "scalar", w1_raw[g], t, 1, "w1_%d_%d" % (g, t)) for t in range(PACK)
+            ]
+            for t in range(PACK):
+                codes, plane = quantise(w1_bf[t], "w1_%d_%d" % (g, t))
+                first_layer_pass(g, t, codes, plane, 0)
+        activate(0)
+        activate(1)
+        a_q[(0, 1)] = quantise(cast_columns("vector", a_raw[0][1], "a0_1"), "a0_1")
+        activate(2)
+        filters(0, 1, 0)
+        activate(3)
+        filters(0, 1, 1)
+
+        def prepare(c):
+            for d in range(LISTS):
+                name = "a%d_%d" % (c, d)
+                a_q[(c, d)] = quantise(cast_columns("scalar", a_raw[c][d], name), name)
+
+        def all_filters(c):
+            for d in range(LISTS):
+                for u in range(2):
+                    filters(c, d, u)
+
+        prepare(1)
+        w2_q = quantise(cast_columns("scalar", w2_raw, "w2"), "w2")
+
+        pieces = [(c * CHUNK, CHUNK) for c in range(CHUNKS - 1)]
+        pieces = pieces + [(T - CHUNK, CHUNK // 2), (T - CHUNK // 2, CHUNK // 2)]
+
+        def gathers(v0, width, terms):
+            c, at = divmod(v0, CHUNK)
+            steps = [(d, t) for d in range(LISTS) for t in range(PACK)]
+            return [
+                (terms[d][:, t, :], h[t][:].indirect(lists[d][:, v0 // 16:(v0 + width) // 16]), f[(c, d)][:, t, at:at + width])
+                for d, t in steps
+            ]
+
+        def gather(step):
+            nc.vector.tensor_tensor(step[0], step[1], step[2], MULT)
+
+        def add_terms(v0, width, terms):
+            z = held([P, width, PACK], BF16, "z%d" % v0)
+            nc.vector.tensor_tensor(
+                z[:].rearrange("p (c i) t -> p c t i", i=2),
+                terms[0][:].rearrange("p t (c i) -> p c t i", i=2),
+                terms[1][:].rearrange("p t (c i) -> p c t i", i=2),
+                ADD,
+            )
+            return z
+
+        def project(v0, width, z):
+            codes, plane = quantise(z, "z%d" % v0)
+            bank = psum.tile([P, BANK], F32, name="bank", tag="bank")
+            nc.tensor.matmul_mx(
+                out=bank[:, 0:width],
+                lhsT=w2_q[0][:].bitcast(FP8X4),
+                lhsT_scale=w2_q[1][:],
+                rhs=codes[:].bitcast(FP8X4),
+                rhs_scale=plane[:],
+                start=True,
+                stop=True,
+            )
+            result = held([P, width], F32, "result%d" % v0)
+            nc.scalar.copy(out=result[:], in_=bank[:, 0:width])
+            nc.sync.dma_start(out=out[:, v0:v0 + width], in_=result[:])
+
+        last = None
+        for v0, width in pieces:
+            c, at = divmod(v0, CHUNK)
+            terms = [ring.tile([P, PACK, width], F32, name="term%d" % d, tag="term%d" % d, bufs=2) for d in range(LISTS)]
+            steps = gathers(v0, width, terms)
+            gather(steps[0])
+            if last is not None:
+                z = add_terms(*last)
+            gather(steps[1])
+            if last is not None:
+                project(last[0], last[1], z)
+            if at == 0 and c + 1 < CHUNKS:
+                all_filters(c + 1)
+                if c + 2 < CHUNKS:
+                    prepare(c + 2)
+            for step in steps[2:]:
+                gather(step)
+            last = (v0, width, terms)
+        project(last[0], last[1], add_terms(*last))

@@ -1,6 +1,7 @@
 from contextlib import ExitStack
 
 import concourse.mybir as mybir
+from concourse.masks import make_identity
 
 K, T, H, N, J, U = 1024, 1024, 512, 128, 512, 2048
 FLOPS = 2 * (K * H * T + J * H * U + H * N * T)
@@ -31,11 +32,13 @@ def tile_picked_wdime_none_l_kernel(
     nc = tc.nc
     with ExitStack() as ctx:
         keep = ctx.enter_context(tc.tile_pool(name="keep", bufs=1))
-        ring = ctx.enter_context(tc.tile_pool(name="ring", bufs=2))
-        psum = ctx.enter_context(tc.psum_pool(name="psum", bufs=8))
+        psum = ctx.enter_context(tc.psum_pool(name="psum", bufs=1))
 
-        def held(shape, dtype, name):
-            return keep.tile(shape, dtype, name=name, align_bytes=64)
+        def new_bank(role):
+            return psum.tile([P, BANK], F32, name=role, tag=role, bufs=4 if role == "filter" else 2)
+
+        def held(shape, dtype, name, slot=None):
+            return keep.tile(shape, dtype, name=name, tag=slot or name, align_bytes=64)
 
         w1_raw = [held([P, PACK, H], F32, "w1_raw%d" % g) for g in range(2)]
         x_codes = [held([P, 2 * T], U8, "x_codes%d" % g) for g in range(2)]
@@ -60,27 +63,27 @@ def tile_picked_wdime_none_l_kernel(
         warm_out = held([P, 1], F32, "warm_out")
         nc.vector.memset(warm_in[:], 0.0)
         nc.scalar.activation(warm_out[:], warm_in[:], SILU)
+        identity = held([P, P], F32, "identity")
+        make_identity(nc, identity[:])
 
         nc.sync.dma_start(out=w3_raw[:], in_=w3.rearrange("(p j) n -> p j n", j=PACK))
         load_a(0, 0)
-        load_w1(0)
         for quad in range(4):
             nc.sync.dma_start(
                 out=x_plane[32 * quad:32 * quad + 4, :, :].bitcast(I32),
                 in_=x_scales[:, 4 * quad:4 * quad + 4, :].rearrange("g r n -> r g n").bitcast(I32),
             )
+        load_a(0, 1)
+        load_w1(0)
         load_x(0)
         load_w1(1)
         load_x(1)
         nc.sync.dma_start(lists[0][:], pos1)
         nc.sync.dma_start(lists[1][:], pos2)
-        load_a(0, 1)
-        load_a(1, 0)
-        load_a(1, 1)
         w2_rows = w2.rearrange("(q t i) n -> i q t n", t=PACK, i=4)
         for i in range(4):
             nc.sync.dma_start(out=w2_raw[i:P:4, :, :], in_=w2_rows[i])
-        for c in range(2, CHUNKS):
+        for c in range(1, CHUNKS):
             load_a(c, 0)
             load_a(c, 1)
 
@@ -99,17 +102,17 @@ def tile_picked_wdime_none_l_kernel(
             )
             return codes, plane
 
-        def cast_weights(engine, raw, t0, tiles, name):
-            grouped = held([P, tiles * P, PACK], BF16, name + "_bf")
+        def cast_weights(engine, raw, t0, tiles, name, slot=None):
+            grouped = held([P, tiles * P, PACK], BF16, name + "_bf", slot)
             src = raw[:].rearrange("p j (q t c i) -> p t q c j i", t=PACK, c=2, i=2)
             dst = grouped[:].rearrange("p (t q c i) j -> p t q c j i", t=tiles, c=2, i=2)
             for t in range(tiles):
                 copy_on(engine, dst[:, t], src[:, t0 + t])
             return grouped
 
-        def cast_columns(engine, raw, name):
+        def cast_columns(engine, raw, name, slot=None):
             width = raw.shape[2]
-            grouped = held([P, width, PACK], BF16, name + "_bf")
+            grouped = held([P, width, PACK], BF16, name + "_bf", slot)
             copy_on(
                 engine,
                 grouped[:].rearrange("p (c i) j -> p c j i", i=2),
@@ -122,7 +125,7 @@ def tile_picked_wdime_none_l_kernel(
 
         def first_layer_pass(g, t, codes, plane, at):
             if g == 0:
-                h_banks[t] = [psum.tile([P, BANK], F32, name="bank", tag="bank") for half in range(2)]
+                h_banks[t] = [new_bank(role) for role in (("filter",) * 2, ("filter",) * 2, ("odd",) * 2, ("even",) * 2)[t]]
             for half in range(2):
                 nc.tensor.matmul_mx(
                     out=h_banks[t][half][:],
@@ -143,9 +146,8 @@ def tile_picked_wdime_none_l_kernel(
         f = {}
 
         def filters(c, d, u):
-            if (c, d) not in f:
-                f[(c, d)] = ring.tile([P, PACK, CHUNK], F32, name="f%d" % d, tag="f%d" % d, bufs=3)
-            bank = psum.tile([P, BANK], F32, name="bank", tag="bank")
+            f[(c, d, u)] = held([P, 2, CHUNK], F32, "f%d_%d_%d" % (c, d, u))
+            bank = new_bank("filter" if c > 0 else ("odd", "even")[d])
             w_codes, w_plane = w3_q[u]
             a_codes, a_plane = a_q[(c, d)]
             for e in range(2):
@@ -158,7 +160,7 @@ def tile_picked_wdime_none_l_kernel(
                     start=True,
                     stop=True,
                 )
-            nc.scalar.copy(out=f[(c, d)][:, 2 * u:2 * u + 2, :].rearrange("p e n -> p (e n)"), in_=bank[:])
+            nc.scalar.copy(out=f[(c, d, u)][:].rearrange("p e n -> p (e n)"), in_=bank[:])
 
         w3_bf0 = cast_weights("vector", w3_raw, 0, 2, "w3_0")
         w3_bf1 = cast_weights("scalar", w3_raw, 2, 2, "w3_1")
@@ -166,64 +168,93 @@ def tile_picked_wdime_none_l_kernel(
         a_bf00 = cast_columns("vector", a_raw[0][0], "a0_0")
         w3_q[1] = quantise(w3_bf1, "w3_1")
         a_q[(0, 0)] = quantise(a_bf00, "a0_0")
-        filters(0, 0, 0)
-        filters(0, 0, 1)
+        a_q[(0, 1)] = quantise(cast_columns("vector", a_raw[0][1], "a0_1"), "a0_1")
+        for d in range(LISTS):
+            filters(0, d, 0)
+            filters(0, d, 1)
 
-        for g in range(2):
-            w1_bf = [
-                cast_weights("vector" if t < 2 else "scalar", w1_raw[g], t, 1, "w1_%d_%d" % (g, t)) for t in range(PACK)
-            ]
-            for t in range(PACK):
-                codes, plane = quantise(w1_bf[t], "w1_%d_%d" % (g, t))
-                first_layer_pass(g, t, codes, plane, 0)
+        first = [quantise(cast_weights("vector", w1_raw[0], 2 * u, 2, "w1_0%d" % u), "w1_0%d" % u) for u in range(2)]
+        low = cast_weights("vector", w1_raw[1], 0, 2, "w1_1a")
+        high = cast_weights("scalar", w1_raw[1], 2, 2, "w1_1b")
+        second = [quantise(low[:, t * P:(t + 1) * P, :], "w1_1_%d" % t) for t in range(2)]
+        second.append(quantise(high, "w1_1b"))
+        first_layer_pass(0, 0, *first[0], 0)
+        first_layer_pass(0, 1, *first[0], 1)
+        first_layer_pass(1, 0, *second[0], 0)
+        first_layer_pass(0, 2, *first[1], 0)
+        first_layer_pass(1, 1, *second[1], 0)
+        first_layer_pass(0, 3, *first[1], 1)
+        first_layer_pass(1, 2, *second[2], 0)
+        first_layer_pass(1, 3, *second[2], 1)
         activate(0)
         activate(1)
-        a_q[(0, 1)] = quantise(cast_columns("vector", a_raw[0][1], "a0_1"), "a0_1")
         activate(2)
-        filters(0, 1, 0)
         activate(3)
-        filters(0, 1, 1)
 
-        def prepare(c):
-            for d in range(LISTS):
-                name = "a%d_%d" % (c, d)
-                a_q[(c, d)] = quantise(cast_columns("scalar", a_raw[c][d], name), name)
+        def prepare(c, d):
+            name = "a%d_%d" % (c, d)
+            slot = ("w1_1b_codes", "w1_1b_plane")[d] if c == 1 else "a%d_%d_codes" % (c - 1, d)
+            cast_slot[(c, d)] = slot
+            a_q[(c, d)] = quantise(cast_columns("scalar", a_raw[c][d], name, slot), name)
 
-        def all_filters(c):
-            for d in range(LISTS):
-                for u in range(2):
-                    filters(c, d, u)
+        terms = [[held([P, PACK, CHUNK], F32, "term%d_%d" % (c, d)) for d in range(LISTS)] for c in range(CHUNKS)]
+        cast_slot = {}
 
-        prepare(1)
-        w2_q = quantise(cast_columns("scalar", w2_raw, "w2"), "w2")
+        def gathers(c, d, tiles=range(PACK)):
+            offsets = lists[d][:, c * CHUNK // 16:(c + 1) * CHUNK // 16]
+            for t in tiles:
+                nc.vector.tensor_tensor(terms[c][d][:, t, :], h[t][:].indirect(offsets), f[(c, d, t // 2)][:, t % 2, :], MULT)
 
-        pieces = [(c * CHUNK, CHUNK) for c in range(CHUNKS - 1)]
-        pieces = pieces + [(T - CHUNK, CHUNK // 2), (T - CHUNK // 2, CHUNK // 2)]
-
-        def gathers(v0, width, terms):
-            c, at = divmod(v0, CHUNK)
-            steps = [(d, t) for d in range(LISTS) for t in range(PACK)]
-            return [
-                (terms[d][:, t, :], h[t][:].indirect(lists[d][:, v0 // 16:(v0 + width) // 16]), f[(c, d)][:, t, at:at + width])
-                for d, t in steps
-            ]
-
-        def gather(step):
-            nc.vector.tensor_tensor(step[0], step[1], step[2], MULT)
-
-        def add_terms(v0, width, terms):
-            z = held([P, width, PACK], BF16, "z%d" % v0)
+        def add_on_vector(summed, c, at, width):
             nc.vector.tensor_tensor(
-                z[:].rearrange("p (c i) t -> p c t i", i=2),
-                terms[0][:].rearrange("p t (c i) -> p c t i", i=2),
-                terms[1][:].rearrange("p t (c i) -> p c t i", i=2),
+                summed[:, at:at + width, :].rearrange("p (c i) t -> p c t i", i=2),
+                terms[c][0][:, :, at:at + width].rearrange("p t (c i) -> p c t i", i=2),
+                terms[c][1][:, :, at:at + width].rearrange("p t (c i) -> p c t i", i=2),
                 ADD,
             )
-            return z
 
-        def project(v0, width, z):
-            codes, plane = quantise(z, "z%d" % v0)
-            bank = psum.tile([P, BANK], F32, name="bank", tag="bank")
+        def add_on_tensor(c):
+            sums = [new_bank(("even", "odd")[c % 2]) for b in range(CHUNK // P)]
+            for t in range(PACK):
+                for b, bank in enumerate(sums):
+                    for d in range(LISTS):
+                        nc.tensor.matmul(
+                            bank[:, t * P:(t + 1) * P],
+                            lhsT=terms[c][d][:, t, b * P:(b + 1) * P],
+                            rhs=identity[:],
+                            start=(d == 0),
+                            stop=(d == LISTS - 1),
+                            is_transpose=True,
+                        )
+            return sums
+
+        def round_sums(c, sums):
+            rows = []
+            for b, bank in enumerate(sums):
+                row = held([P, 2, P, 2], BF16, "row%d_%d" % (c, b))
+                nc.scalar.copy(out=row[:], in_=bank[:].rearrange("v (u e p) -> v u p e", u=2, e=2))
+                rows.append(row)
+            return rows
+
+        def turn_back(c, rows):
+            bank = new_bank("odd")
+            for b, row in enumerate(rows):
+                words = row[:].rearrange("v u p e -> v (u p e)").bitcast(F32)
+                for u in range(2):
+                    at = (2 * b + u) * P
+                    nc.tensor.transpose(bank[:, at:at + P], words[:, u * P:(u + 1) * P], identity[:])
+            return bank
+
+        def lay_words(grouped, bank):
+            z_words = grouped.rearrange("p v t -> p (v t)").bitcast(F32)
+            nc.scalar.copy(
+                out=z_words.rearrange("p (b v u) -> p b v u", b=2, u=2),
+                in_=bank[:].rearrange("p (b u v) -> p b v u", b=2, u=2),
+            )
+
+        def project(v0, codes, plane):
+            width = codes.shape[1]
+            bank = new_bank("filter")
             nc.tensor.matmul_mx(
                 out=bank[:, 0:width],
                 lhsT=w2_q[0][:].bitcast(FP8X4),
@@ -237,22 +268,42 @@ def tile_picked_wdime_none_l_kernel(
             nc.scalar.copy(out=result[:], in_=bank[:, 0:width])
             nc.sync.dma_start(out=out[:, v0:v0 + width], in_=result[:])
 
-        last = None
-        for v0, width in pieces:
-            c, at = divmod(v0, CHUNK)
-            terms = [ring.tile([P, PACK, width], F32, name="term%d" % d, tag="term%d" % d, bufs=2) for d in range(LISTS)]
-            steps = gathers(v0, width, terms)
-            gather(steps[0])
-            if last is not None:
-                z = add_terms(*last)
-            gather(steps[1])
-            if last is not None:
-                project(last[0], last[1], z)
-            if at == 0 and c + 1 < CHUNKS:
-                all_filters(c + 1)
-                if c + 2 < CHUNKS:
-                    prepare(c + 2)
-            for step in steps[2:]:
-                gather(step)
-            last = (v0, width, terms)
-        project(last[0], last[1], add_terms(*last))
+        steps = [(c, d) for c in range(CHUNKS) for d in range(LISTS)]
+        w2_q = quantise(cast_columns("vector", w2_raw, "w2", "w1_1b_bf"), "w2")
+        prepare(*steps[2])
+        prepare(*steps[3])
+        for t in range(PACK):
+            for d in range(LISTS):
+                gathers(0, d, [t])
+        z_q = {}
+        sums = {}
+        for s in range(2, len(steps) - 1):
+            c, d = steps[s]
+            filters(c, d, 0)
+            filters(c, d, 1)
+            if s + 2 < len(steps):
+                prepare(*steps[s + 2])
+            if s == 2:
+                summed = held([P, CHUNK, PACK], BF16, "z0", cast_slot[(1, 0)])
+                add_on_vector(summed, 0, 0, CHUNK)
+                z_q[0] = quantise(summed, "z0")
+            elif d == 0:
+                sums[c - 1] = add_on_tensor(c - 1)
+            gathers(c, d)
+        last = CHUNKS - 1
+        turned = {1: turn_back(1, round_sums(1, sums[1]))}
+        filters(last, 1, 0)
+        filters(last, 1, 1)
+        turned[2] = turn_back(2, round_sums(2, sums[2]))
+        middle = held([P, 2 * CHUNK, PACK], BF16, "middle")
+        for c in (1, 2):
+            lay_words(middle[:, (c - 1) * CHUNK:c * CHUNK, :], turned[c])
+        z_q[CHUNK] = quantise(middle, "middle")
+        gathers(last, 1)
+        summed = held([P, CHUNK, PACK], BF16, "z_last", "middle")
+        for b in range(2):
+            add_on_vector(summed, last, b * P, P)
+        for b in range(2):
+            z_q[last * CHUNK + b * P] = quantise(summed[:, b * P:(b + 1) * P, :], "z%d_%d" % (last, b))
+        for v0 in sorted(z_q):
+            project(v0, *z_q[v0])

@@ -21,8 +21,7 @@ ADD = mybir.AluOpType.add
 P = 128
 PACK = 4
 BANK = 512
-CHUNK = 256
-CHUNKS = T // CHUNK
+WIDTHS = (256, 256, 256, 256)
 LISTS = 2
 
 
@@ -30,12 +29,14 @@ def tile_picked_wdime_none_l_kernel(
     tc, x_words, x_scales, aT, w1, w3, w2, pos1, pos2, out
 ):
     nc = tc.nc
+    starts = [sum(WIDTHS[:c]) for c in range(len(WIDTHS))]
     with ExitStack() as ctx:
         keep = ctx.enter_context(tc.tile_pool(name="keep", bufs=1))
         psum = ctx.enter_context(tc.psum_pool(name="psum", bufs=1))
+        depth = {"filter": 4, "sum": 2, "back": 2}
 
         def new_bank(role):
-            return psum.tile([P, BANK], F32, name=role, tag=role, bufs=4 if role == "filter" else 2)
+            return psum.tile([P, BANK], F32, name=role, tag=role, bufs=depth[role])
 
         def held(shape, dtype, name, slot=None):
             return keep.tile(shape, dtype, name=name, tag=slot or name, align_bytes=64)
@@ -45,18 +46,36 @@ def tile_picked_wdime_none_l_kernel(
         x_plane = held([P, 2, T], U8, "x_plane")
         w3_raw = held([P, PACK, H], F32, "w3_raw")
         w2_raw = held([P, PACK, N], F32, "w2_raw")
-        a_raw = [[held([P, PACK, CHUNK], F32, "a_raw%d_%d" % (c, d)) for d in range(LISTS)] for c in range(CHUNKS)]
+        a_raw = {(c, d): held([P, PACK, width], F32, "a_raw%d_%d" % (c, d)) for c, width in enumerate(WIDTHS) for d in range(LISTS)}
         lists = [keep.tile([P, T // 16], U16, name="list%d" % d) for d in range(LISTS)]
 
+        def load_rows(tile, rows):
+            nc.sync.dma_start(out=tile[:], in_=rows.rearrange("(p j) n -> p j n", j=PACK))
+
         def load_a(c, d):
-            cols = slice(d * T + c * CHUNK, d * T + (c + 1) * CHUNK)
-            nc.sync.dma_start(out=a_raw[c][d][:], in_=aT[:, cols].rearrange("(p j) n -> p j n", j=PACK))
+            load_rows(a_raw[(c, d)], aT[:, d * T + starts[c]:d * T + starts[c] + WIDTHS[c]])
 
         def load_w1(g):
-            nc.sync.dma_start(out=w1_raw[g][:], in_=w1[g * 512:(g + 1) * 512, :].rearrange("(p j) n -> p j n", j=PACK))
+            load_rows(w1_raw[g], w1[g * 512:(g + 1) * 512, :])
 
         def load_x(g):
             nc.sync.dma_start(out=x_codes[g][:].bitcast(I32), in_=x_words[g].bitcast(I32))
+
+        def load_scales():
+            for quad in range(4):
+                nc.sync.dma_start(
+                    out=x_plane[32 * quad:32 * quad + 4, :, :].bitcast(I32),
+                    in_=x_scales[:, 4 * quad:4 * quad + 4, :].rearrange("g r n -> r g n").bitcast(I32),
+                )
+
+        def load_lists():
+            nc.sync.dma_start(lists[0][:], pos1)
+            nc.sync.dma_start(lists[1][:], pos2)
+
+        def load_w2():
+            w2_rows = w2.rearrange("(q t i) n -> i q t n", t=PACK, i=4)
+            for i in range(4):
+                nc.sync.dma_start(out=w2_raw[i:P:4, :, :], in_=w2_rows[i])
 
         nc.gpsimd.memset(x_plane[:].bitcast(I32), 0)
         warm_in = held([P, 1], F32, "warm_in")
@@ -66,26 +85,22 @@ def tile_picked_wdime_none_l_kernel(
         identity = held([P, P], F32, "identity")
         make_identity(nc, identity[:])
 
-        nc.sync.dma_start(out=w3_raw[:], in_=w3.rearrange("(p j) n -> p j n", j=PACK))
-        load_a(0, 0)
-        for quad in range(4):
-            nc.sync.dma_start(
-                out=x_plane[32 * quad:32 * quad + 4, :, :].bitcast(I32),
-                in_=x_scales[:, 4 * quad:4 * quad + 4, :].rearrange("g r n -> r g n").bitcast(I32),
-            )
-        load_a(0, 1)
         load_w1(0)
+        load_scales()
         load_x(0)
         load_w1(1)
         load_x(1)
-        nc.sync.dma_start(lists[0][:], pos1)
-        nc.sync.dma_start(lists[1][:], pos2)
-        w2_rows = w2.rearrange("(q t i) n -> i q t n", t=PACK, i=4)
-        for i in range(4):
-            nc.sync.dma_start(out=w2_raw[i:P:4, :, :], in_=w2_rows[i])
-        for c in range(1, CHUNKS):
-            load_a(c, 0)
-            load_a(c, 1)
+        load_a(0, 0)
+        load_rows(w3_raw, w3)
+        load_lists()
+        load_a(0, 1)
+        load_a(1, 0)
+        load_a(1, 1)
+        load_a(2, 0)
+        load_a(2, 1)
+        load_w2()
+        load_a(3, 0)
+        load_a(3, 1)
 
         def copy_on(engine, out_ap, in_ap):
             if engine == "vector":
@@ -102,8 +117,8 @@ def tile_picked_wdime_none_l_kernel(
             )
             return codes, plane
 
-        def cast_weights(engine, raw, t0, tiles, name, slot=None):
-            grouped = held([P, tiles * P, PACK], BF16, name + "_bf", slot)
+        def cast_weights(engine, raw, t0, tiles, name, slot=None, into=None):
+            grouped = held([P, tiles * P, PACK], BF16, name + "_bf", slot) if into is None else into
             src = raw[:].rearrange("p j (q t c i) -> p t q c j i", t=PACK, c=2, i=2)
             dst = grouped[:].rearrange("p (t q c i) j -> p t q c j i", t=tiles, c=2, i=2)
             for t in range(tiles):
@@ -122,15 +137,26 @@ def tile_picked_wdime_none_l_kernel(
 
         h = [held([P, T], F32, "h%d" % t) for t in range(PACK)]
         h_banks = {}
+        w1_q = {}
+        w3_q = {}
+        a_bf = {}
+        a_q = {}
+        f = {}
 
-        def first_layer_pass(g, t, codes, plane, at):
+        def quantise_tiles(store, key, grouped, t0, name):
+            codes, plane = quantise(grouped, name)
+            for e in range(grouped.shape[1] // P):
+                store[key + (t0 + e,)] = (codes[:, e * P:(e + 1) * P], plane[:, e * P:(e + 1) * P])
+
+        def first_layer_pass(g, t):
             if g == 0:
-                h_banks[t] = [new_bank(role) for role in (("filter",) * 2, ("filter",) * 2, ("odd",) * 2, ("even",) * 2)[t]]
+                h_banks[t] = [new_bank(("filter", "filter", "sum", "back")[t]) for half in range(2)]
+            codes, plane = w1_q[(g, t)]
             for half in range(2):
                 nc.tensor.matmul_mx(
                     out=h_banks[t][half][:],
-                    lhsT=codes[:, at * P:(at + 1) * P].bitcast(FP8X4),
-                    lhsT_scale=plane[:, at * P:(at + 1) * P],
+                    lhsT=codes.bitcast(FP8X4),
+                    lhsT_scale=plane,
                     rhs=x_codes[g][:, 2 * half * BANK:2 * (half + 1) * BANK].bitcast(FP4X4),
                     rhs_scale=x_plane[:, g, half * BANK:(half + 1) * BANK],
                     start=(g == 0),
@@ -141,118 +167,94 @@ def tile_picked_wdime_none_l_kernel(
             for half in range(2):
                 nc.scalar.activation(h[t][:, half * BANK:(half + 1) * BANK], h_banks[t][half][:], SILU)
 
-        w3_q = {}
-        a_q = {}
-        f = {}
+        def cast_a(engine, c, d, slot=None):
+            a_bf[(c, d)] = cast_columns(engine, a_raw[(c, d)], "a%d_%d" % (c, d), slot)
 
-        def filters(c, d, u):
-            f[(c, d, u)] = held([P, 2, CHUNK], F32, "f%d_%d_%d" % (c, d, u))
-            bank = new_bank("filter" if c > 0 else ("odd", "even")[d])
-            w_codes, w_plane = w3_q[u]
+        def quantise_a(c, d):
+            a_q[(c, d)] = quantise(a_bf[(c, d)], "a%d_%d" % (c, d))
+
+        def filters(c, d, t0, tiles, engine="scalar", slot=None):
+            width = WIDTHS[c]
+            made = held([P, tiles, width], F32, "f%d_%d_%d" % (c, d, t0), slot)
+            bank = new_bank("filter")
             a_codes, a_plane = a_q[(c, d)]
-            for e in range(2):
+            for e in range(tiles):
+                w_codes, w_plane = w3_q[(t0 + e,)]
                 nc.tensor.matmul_mx(
-                    out=bank[:, e * CHUNK:(e + 1) * CHUNK],
-                    lhsT=w_codes[:, e * P:(e + 1) * P].bitcast(FP8X4),
-                    lhsT_scale=w_plane[:, e * P:(e + 1) * P],
+                    out=bank[:, e * width:(e + 1) * width],
+                    lhsT=w_codes.bitcast(FP8X4),
+                    lhsT_scale=w_plane,
                     rhs=a_codes[:].bitcast(FP8X4),
                     rhs_scale=a_plane[:],
                     start=True,
                     stop=True,
                 )
-            nc.scalar.copy(out=f[(c, d, u)][:].rearrange("p e n -> p (e n)"), in_=bank[:])
+                f[(c, d, t0 + e)] = made[:, e, :]
+            copy_on(engine, made[:].rearrange("p e n -> p (e n)"), bank[:, 0:tiles * width])
 
-        w3_bf0 = cast_weights("vector", w3_raw, 0, 2, "w3_0")
-        w3_bf1 = cast_weights("scalar", w3_raw, 2, 2, "w3_1")
-        w3_q[0] = quantise(w3_bf0, "w3_0")
-        a_bf00 = cast_columns("vector", a_raw[0][0], "a0_0")
-        w3_q[1] = quantise(w3_bf1, "w3_1")
-        a_q[(0, 0)] = quantise(a_bf00, "a0_0")
-        a_q[(0, 1)] = quantise(cast_columns("vector", a_raw[0][1], "a0_1"), "a0_1")
-        for d in range(LISTS):
-            filters(0, d, 0)
-            filters(0, d, 1)
+        def all_filters(c, d):
+            tiles = BANK // WIDTHS[c]
+            for t0 in range(0, PACK, tiles):
+                filters(c, d, t0, tiles)
 
-        first = [quantise(cast_weights("vector", w1_raw[0], 2 * u, 2, "w1_0%d" % u), "w1_0%d" % u) for u in range(2)]
-        low = cast_weights("vector", w1_raw[1], 0, 2, "w1_1a")
-        high = cast_weights("scalar", w1_raw[1], 2, 2, "w1_1b")
-        second = [quantise(low[:, t * P:(t + 1) * P, :], "w1_1_%d" % t) for t in range(2)]
-        second.append(quantise(high, "w1_1b"))
-        first_layer_pass(0, 0, *first[0], 0)
-        first_layer_pass(0, 1, *first[0], 1)
-        first_layer_pass(1, 0, *second[0], 0)
-        first_layer_pass(0, 2, *first[1], 0)
-        first_layer_pass(1, 1, *second[1], 0)
-        first_layer_pass(0, 3, *first[1], 1)
-        first_layer_pass(1, 2, *second[2], 0)
-        first_layer_pass(1, 3, *second[2], 1)
-        activate(0)
-        activate(1)
-        activate(2)
-        activate(3)
+        terms = {}
 
-        def prepare(c, d):
-            name = "a%d_%d" % (c, d)
-            slot = ("w1_1b_codes", "w1_1b_plane")[d] if c == 1 else "a%d_%d_codes" % (c - 1, d)
-            cast_slot[(c, d)] = slot
-            a_q[(c, d)] = quantise(cast_columns("scalar", a_raw[c][d], name, slot), name)
-
-        terms = [[held([P, PACK, CHUNK], F32, "term%d_%d" % (c, d)) for d in range(LISTS)] for c in range(CHUNKS)]
-        cast_slot = {}
-
-        def gathers(c, d, tiles=range(PACK)):
-            offsets = lists[d][:, c * CHUNK // 16:(c + 1) * CHUNK // 16]
+        def gathers(c, d, tiles=range(PACK), slot=None):
+            if (c, d) not in terms:
+                terms[(c, d)] = held([P, PACK, WIDTHS[c]], F32, "term%d_%d" % (c, d), slot)
+            offsets = lists[d][:, starts[c] // 16:(starts[c] + WIDTHS[c]) // 16]
             for t in tiles:
-                nc.vector.tensor_tensor(terms[c][d][:, t, :], h[t][:].indirect(offsets), f[(c, d, t // 2)][:, t % 2, :], MULT)
+                nc.vector.tensor_tensor(terms[(c, d)][:, t, :], h[t][:].indirect(offsets), f[(c, d, t)], MULT)
 
         def add_on_vector(summed, c, at, width):
             nc.vector.tensor_tensor(
-                summed[:, at:at + width, :].rearrange("p (c i) t -> p c t i", i=2),
-                terms[c][0][:, :, at:at + width].rearrange("p t (c i) -> p c t i", i=2),
-                terms[c][1][:, :, at:at + width].rearrange("p t (c i) -> p c t i", i=2),
+                summed.rearrange("p (c i) t -> p c t i", i=2),
+                terms[(c, 0)][:, :, at:at + width].rearrange("p t (c i) -> p c t i", i=2),
+                terms[(c, 1)][:, :, at:at + width].rearrange("p t (c i) -> p c t i", i=2),
                 ADD,
             )
 
-        def add_on_tensor(c):
-            sums = [new_bank(("even", "odd")[c % 2]) for b in range(CHUNK // P)]
+        sums = {}
+        rows = {}
+        turned = {}
+
+        def add_on_tensor(c, b):
+            bank = new_bank("sum")
+            sums[(c, b)] = bank
             for t in range(PACK):
-                for b, bank in enumerate(sums):
-                    for d in range(LISTS):
-                        nc.tensor.matmul(
-                            bank[:, t * P:(t + 1) * P],
-                            lhsT=terms[c][d][:, t, b * P:(b + 1) * P],
-                            rhs=identity[:],
-                            start=(d == 0),
-                            stop=(d == LISTS - 1),
-                            is_transpose=True,
-                        )
-            return sums
+                for d in range(LISTS):
+                    nc.tensor.matmul(
+                        bank[:, t * P:(t + 1) * P],
+                        lhsT=terms[(c, d)][:, t, b * P:(b + 1) * P],
+                        rhs=identity[:],
+                        start=(d == 0),
+                        stop=(d == LISTS - 1),
+                        is_transpose=True,
+                    )
 
-        def round_sums(c, sums):
-            rows = []
-            for b, bank in enumerate(sums):
-                row = held([P, 2, P, 2], BF16, "row%d_%d" % (c, b))
-                nc.scalar.copy(out=row[:], in_=bank[:].rearrange("v (u e p) -> v u p e", u=2, e=2))
-                rows.append(row)
-            return rows
+        def round_sum(c, b, slot=None):
+            rows[(c, b)] = held([P, 2, P, 2], BF16, "row%d_%d" % (c, b), slot)
+            nc.scalar.copy(out=rows[(c, b)][:], in_=sums[(c, b)][:].rearrange("v (u e p) -> v u p e", u=2, e=2))
 
-        def turn_back(c, rows):
-            bank = new_bank("odd")
-            for b, row in enumerate(rows):
-                words = row[:].rearrange("v u p e -> v (u p e)").bitcast(F32)
+        def turn_back(blocks):
+            bank = new_bank("back")
+            turned[blocks[0]] = bank
+            for i, block in enumerate(blocks):
+                words = rows[block][:].rearrange("v u p e -> v (u p e)").bitcast(F32)
                 for u in range(2):
-                    at = (2 * b + u) * P
+                    at = (2 * i + u) * P
                     nc.tensor.transpose(bank[:, at:at + P], words[:, u * P:(u + 1) * P], identity[:])
-            return bank
 
-        def lay_words(grouped, bank):
+        def lay_words(grouped, first, count):
             z_words = grouped.rearrange("p v t -> p (v t)").bitcast(F32)
             nc.scalar.copy(
-                out=z_words.rearrange("p (b v u) -> p b v u", b=2, u=2),
-                in_=bank[:].rearrange("p (b u v) -> p b v u", b=2, u=2),
+                out=z_words.rearrange("p (b v u) -> p b v u", b=count, u=2),
+                in_=turned[first][:, 0:count * 2 * P].rearrange("p (b u v) -> p b v u", b=count, u=2),
             )
 
-        def project(v0, codes, plane):
+        w2_q = []
+
+        def project(v0, codes, plane, engine="scalar"):
             width = codes.shape[1]
             bank = new_bank("filter")
             nc.tensor.matmul_mx(
@@ -265,45 +267,90 @@ def tile_picked_wdime_none_l_kernel(
                 stop=True,
             )
             result = held([P, width], F32, "result%d" % v0)
-            nc.scalar.copy(out=result[:], in_=bank[:, 0:width])
+            copy_on(engine, result[:], bank[:, 0:width])
             nc.sync.dma_start(out=out[:, v0:v0 + width], in_=result[:])
 
-        steps = [(c, d) for c in range(CHUNKS) for d in range(LISTS)]
-        w2_q = quantise(cast_columns("vector", w2_raw, "w2", "w1_1b_bf"), "w2")
-        prepare(*steps[2])
-        prepare(*steps[3])
+        low = cast_weights("vector", w1_raw[0], 0, 2, "w1_0a")
+        high = held([P, 4 * P, PACK], BF16, "w1_high_bf")
+        cast_weights("scalar", w1_raw[0], 2, 2, "", into=high[:, 0:2 * P, :])
+        quantise_tiles(w1_q, (0,), low, 0, "w1_0a")
+        low = cast_weights("vector", w1_raw[1], 0, 2, "w1_1a")
+        cast_weights("scalar", w1_raw[1], 2, 2, "", into=high[:, 2 * P:4 * P, :])
+        for t in range(2):
+            quantise_tiles(w1_q, (1,), low[:, t * P:(t + 1) * P, :], t, "w1_1_%d" % t)
+        high_q = {}
+        quantise_tiles(high_q, (), high, 0, "w1_high")
+        for g in range(2):
+            for e in range(2):
+                w1_q[(g, 2 + e)] = high_q[(2 * g + e,)]
         for t in range(PACK):
-            for d in range(LISTS):
-                gathers(0, d, [t])
-        z_q = {}
-        sums = {}
-        for s in range(2, len(steps) - 1):
-            c, d = steps[s]
-            filters(c, d, 0)
-            filters(c, d, 1)
-            if s + 2 < len(steps):
-                prepare(*steps[s + 2])
-            if s == 2:
-                summed = held([P, CHUNK, PACK], BF16, "z0", cast_slot[(1, 0)])
-                add_on_vector(summed, 0, 0, CHUNK)
-                z_q[0] = quantise(summed, "z0")
-            elif d == 0:
-                sums[c - 1] = add_on_tensor(c - 1)
-            gathers(c, d)
-        last = CHUNKS - 1
-        turned = {1: turn_back(1, round_sums(1, sums[1]))}
-        filters(last, 1, 0)
-        filters(last, 1, 1)
-        turned[2] = turn_back(2, round_sums(2, sums[2]))
-        middle = held([P, 2 * CHUNK, PACK], BF16, "middle")
-        for c in (1, 2):
-            lay_words(middle[:, (c - 1) * CHUNK:c * CHUNK, :], turned[c])
-        z_q[CHUNK] = quantise(middle, "middle")
-        gathers(last, 1)
-        summed = held([P, CHUNK, PACK], BF16, "z_last", "middle")
+            first_layer_pass(0, t)
+            first_layer_pass(1, t)
+        cast_a("vector", 0, 0)
+        quantise_a(0, 0)
+        for t in range(3):
+            activate(t)
+        for u in range(2):
+            quantise_tiles(w3_q, (), cast_weights("vector", w3_raw, 2 * u, 2, "w3_%d" % u), 2 * u, "w3_%d" % u)
+        filters(0, 0, 0, 2)
+        activate(3)
+        filters(0, 0, 2, 2)
+        cast_a("vector", 0, 1, "w3_0_bf")
+        quantise_a(0, 1)
+
+        cast_a("scalar", 1, 0)
+        gathers(0, 0)
+        quantise_a(1, 0)
+        all_filters(0, 1)
+        cast_a("scalar", 1, 1)
+        gathers(0, 1)
+        quantise_a(1, 1)
+        all_filters(1, 0)
+        cast_a("scalar", 2, 0)
+        gathers(1, 0)
+        quantise_a(2, 0)
+        all_filters(1, 1)
+        add_on_tensor(0, 0)
+        add_on_tensor(0, 1)
+        cast_a("scalar", 2, 1)
+        gathers(1, 1)
+        quantise_a(2, 1)
+        all_filters(2, 0)
+        round_sum(0, 0)
+        cast_a("scalar", 3, 0)
+        gathers(2, 0)
+        quantise_a(3, 0)
+        all_filters(2, 1)
+        round_sum(0, 1)
+        cast_a("scalar", 3, 1)
+        add_on_tensor(1, 0)
+        add_on_tensor(1, 1)
+        turn_back([(0, 0), (0, 1)])
+        gathers(2, 1)
+        quantise_a(3, 1)
+        all_filters(3, 0)
+        round_sum(1, 0)
+        round_sum(1, 1)
+        early = held([P, 512, PACK], BF16, "early")
+        late = held([P, 256, PACK], BF16, "late")
+        turn_back([(1, 0), (1, 1)])
+        lay_words(early[:, 0:256, :], (0, 0), 2)
+        w2_q.extend(quantise(cast_columns("scalar", w2_raw, "w2"), "w2"))
+        lay_words(early[:, 256:512, :], (1, 0), 2)
+        gathers(3, 0)
+        early_q = quantise(early, "early")
+        all_filters(3, 1)
+        add_on_tensor(2, 0)
+        add_on_tensor(2, 1)
+        round_sum(2, 0)
+        round_sum(2, 1)
+        turn_back([(2, 0), (2, 1)])
+        project(0, *early_q)
+        lay_words(late[:], (2, 0), 2)
+        gathers(3, 1)
+        project(512, *quantise(late, "late"))
+        last = held([P, 256, PACK], BF16, "last", "late")
         for b in range(2):
-            add_on_vector(summed, last, b * P, P)
+            add_on_vector(last[:, b * P:(b + 1) * P, :], 3, b * P, P)
         for b in range(2):
-            z_q[last * CHUNK + b * P] = quantise(summed[:, b * P:(b + 1) * P, :], "z%d_%d" % (last, b))
-        for v0 in sorted(z_q):
-            project(v0, *z_q[v0])
+            project(768 + b * P, *quantise(last[:, b * P:(b + 1) * P, :], "last%d" % b))

@@ -33,7 +33,7 @@ def tile_picked_wdime_none_l_kernel(
     with ExitStack() as ctx:
         keep = ctx.enter_context(tc.tile_pool(name="keep", bufs=1))
         psum = ctx.enter_context(tc.psum_pool(name="psum", bufs=1))
-        depth = {"filter": 4, "sum": 2, "back": 2}
+        depth = {"filter": 5, "sum": 2, "back": 1}
 
         def new_bank(role):
             return psum.tile([P, BANK], F32, name=role, tag=role, bufs=depth[role])
@@ -117,12 +117,12 @@ def tile_picked_wdime_none_l_kernel(
             )
             return codes, plane
 
-        def cast_weights(engine, raw, t0, tiles, name, slot=None, into=None):
+        def cast_weights(engine, raw, t0, tiles, name, slot=None, into=None, step=2):
             grouped = held([P, tiles * P, PACK], BF16, name + "_bf", slot) if into is None else into
-            src = raw[:].rearrange("p j (q t c i) -> p t q c j i", t=PACK, c=2, i=2)
-            dst = grouped[:].rearrange("p (t q c i) j -> p t q c j i", t=tiles, c=2, i=2)
-            for t in range(tiles):
-                copy_on(engine, dst[:, t], src[:, t0 + t])
+            src = raw[:].rearrange("p j (q t i) -> p t q j i", t=PACK, i=4)
+            dst = grouped[:].rearrange("p (t q i) j -> p t q j i", t=tiles, i=4)
+            for t in range(0, tiles, step):
+                copy_on(engine, dst[:, t:t + step], src[:, t0 + t:t0 + t + step])
             return grouped
 
         def cast_columns(engine, raw, name, slot=None):
@@ -150,7 +150,7 @@ def tile_picked_wdime_none_l_kernel(
 
         def first_layer_pass(g, t):
             if g == 0:
-                h_banks[t] = [new_bank(("filter", "filter", "sum", "back")[t]) for half in range(2)]
+                h_banks[t] = [new_bank(role) for role in (("filter", "filter"), ("filter", "filter"), ("sum", "sum"), ("back", "filter"))[t]]
             codes, plane = w1_q[(g, t)]
             for half in range(2):
                 nc.tensor.matmul_mx(
@@ -254,9 +254,9 @@ def tile_picked_wdime_none_l_kernel(
 
         w2_q = []
 
-        def project(v0, codes, plane, engine="scalar"):
+        def project(v0, codes, plane, engine="scalar", role="filter"):
             width = codes.shape[1]
-            bank = new_bank("filter")
+            bank = new_bank(role)
             nc.tensor.matmul_mx(
                 out=bank[:, 0:width],
                 lhsT=w2_q[0][:].bitcast(FP8X4),
@@ -270,11 +270,25 @@ def tile_picked_wdime_none_l_kernel(
             copy_on(engine, result[:], bank[:, 0:width])
             nc.sync.dma_start(out=out[:, v0:v0 + width], in_=result[:])
 
+        def cast_both(c, d):
+            if d == 0:
+                a_bf[c] = held([P, 2 * WIDTHS[c], PACK], BF16, "a%d_bf" % c)
+            nc.scalar.copy(
+                out=a_bf[c][:, d * WIDTHS[c]:(d + 1) * WIDTHS[c], :].rearrange("p (c i) j -> p c j i", i=2),
+                in_=a_raw[(c, d)][:].rearrange("p j (c i) -> p c j i", i=2),
+            )
+
+        def quantise_both(c):
+            codes, plane = quantise(a_bf[c], "a%d" % c)
+            for d in range(LISTS):
+                cols = slice(d * WIDTHS[c], (d + 1) * WIDTHS[c])
+                a_q[(c, d)] = (codes[:, cols], plane[:, cols])
+
         low = cast_weights("vector", w1_raw[0], 0, 2, "w1_0a")
         high = held([P, 4 * P, PACK], BF16, "w1_high_bf")
         cast_weights("scalar", w1_raw[0], 2, 2, "", into=high[:, 0:2 * P, :])
         quantise_tiles(w1_q, (0,), low, 0, "w1_0a")
-        low = cast_weights("vector", w1_raw[1], 0, 2, "w1_1a")
+        low = cast_weights("vector", w1_raw[1], 0, 2, "w1_1a", step=1)
         cast_weights("scalar", w1_raw[1], 2, 2, "", into=high[:, 2 * P:4 * P, :])
         for t in range(2):
             quantise_tiles(w1_q, (1,), low[:, t * P:(t + 1) * P, :], t, "w1_1_%d" % t)
@@ -298,7 +312,7 @@ def tile_picked_wdime_none_l_kernel(
         cast_a("vector", 0, 1, "w3_0_bf")
         quantise_a(0, 1)
 
-        cast_a("scalar", 1, 0)
+        cast_a("scalar", 1, 0, "a0_0_codes")
         gathers(0, 0)
         quantise_a(1, 0)
         all_filters(0, 1)
@@ -306,47 +320,46 @@ def tile_picked_wdime_none_l_kernel(
         gathers(0, 1)
         quantise_a(1, 1)
         all_filters(1, 0)
-        cast_a("scalar", 2, 0)
+        cast_both(2, 0)
+        cast_both(2, 1)
         gathers(1, 0)
-        quantise_a(2, 0)
+        quantise_both(2)
         all_filters(1, 1)
         add_on_tensor(0, 0)
         add_on_tensor(0, 1)
-        cast_a("scalar", 2, 1)
-        gathers(1, 1)
-        quantise_a(2, 1)
-        all_filters(2, 0)
+        cast_both(3, 0)
         round_sum(0, 0)
-        cast_a("scalar", 3, 0)
-        gathers(2, 0)
-        quantise_a(3, 0)
-        all_filters(2, 1)
+        gathers(1, 1)
+        all_filters(2, 0)
+        cast_both(3, 1)
         round_sum(0, 1)
-        cast_a("scalar", 3, 1)
+        gathers(2, 0)
+        quantise_both(3)
+        all_filters(2, 1)
         add_on_tensor(1, 0)
         add_on_tensor(1, 1)
         turn_back([(0, 0), (0, 1)])
-        gathers(2, 1)
-        quantise_a(3, 1)
-        all_filters(3, 0)
-        round_sum(1, 0)
-        round_sum(1, 1)
         early = held([P, 512, PACK], BF16, "early")
         late = held([P, 256, PACK], BF16, "late")
-        turn_back([(1, 0), (1, 1)])
-        lay_words(early[:, 0:256, :], (0, 0), 2)
         w2_q.extend(quantise(cast_columns("scalar", w2_raw, "w2"), "w2"))
+        round_sum(1, 0)
+        lay_words(early[:, 0:256, :], (0, 0), 2)
+        gathers(2, 1)
+        all_filters(3, 0)
+        round_sum(1, 1)
+        turn_back([(1, 0), (1, 1)])
         lay_words(early[:, 256:512, :], (1, 0), 2)
         gathers(3, 0)
         early_q = quantise(early, "early")
-        all_filters(3, 1)
+        filters(3, 1, 0, 2, slot="row1_1")
+        filters(3, 1, 2, 2)
         add_on_tensor(2, 0)
         add_on_tensor(2, 1)
         round_sum(2, 0)
         round_sum(2, 1)
         turn_back([(2, 0), (2, 1)])
-        project(0, *early_q)
         lay_words(late[:], (2, 0), 2)
+        project(0, *early_q, role="back")
         gathers(3, 1)
         project(512, *quantise(late, "late"))
         last = held([P, 256, PACK], BF16, "last", "late")

@@ -20,62 +20,49 @@ ADD = mybir.AluOpType.add
 
 P = 128
 PACK = 4
+PASS = P * PACK
 BANK = 512
-WIDTHS = (256, 256, 256, 256)
+CHUNK = 256
+CHUNKS = T // CHUNK
 LISTS = 2
+PER_COLUMN = 16
+BANKS = {"filter": 5, "sum": 2, "back": 1}
+FIRST_LAYER_BANKS = (("filter", "filter"), ("filter", "filter"), ("sum", "sum"), ("back", "filter"))
 
 
 def tile_picked_wdime_none_l_kernel(
     tc, x_words, x_scales, aT, w1, w3, w2, pos1, pos2, out
 ):
     nc = tc.nc
-    starts = [sum(WIDTHS[:c]) for c in range(len(WIDTHS))]
     with ExitStack() as ctx:
         keep = ctx.enter_context(tc.tile_pool(name="keep", bufs=1))
         psum = ctx.enter_context(tc.psum_pool(name="psum", bufs=1))
-        depth = {"filter": 5, "sum": 2, "back": 1}
 
         def new_bank(role):
-            return psum.tile([P, BANK], F32, name=role, tag=role, bufs=depth[role])
+            return psum.tile([P, BANK], F32, name=role, tag=role, bufs=BANKS[role])
 
-        def held(shape, dtype, name, slot=None):
-            return keep.tile(shape, dtype, name=name, tag=slot or name, align_bytes=64)
+        def held(shape, dtype, name, takes_over=None):
+            return keep.tile(shape, dtype, name=name, tag=takes_over or name, align_bytes=64)
 
-        w1_raw = [held([P, PACK, H], F32, "w1_raw%d" % g) for g in range(2)]
-        x_codes = [held([P, 2 * T], U8, "x_codes%d" % g) for g in range(2)]
-        x_plane = held([P, 2, T], U8, "x_plane")
+        w1_raw = [held([P, PACK, H], F32, "w1_raw%d" % g) for g in range(K // PASS)]
+        x_codes = [held([P, 2 * T], U8, "x_codes%d" % g) for g in range(K // PASS)]
+        x_plane = held([P, K // PASS, T], U8, "x_plane")
         w3_raw = held([P, PACK, H], F32, "w3_raw")
         w2_raw = held([P, PACK, N], F32, "w2_raw")
-        a_raw = {(c, d): held([P, PACK, width], F32, "a_raw%d_%d" % (c, d)) for c, width in enumerate(WIDTHS) for d in range(LISTS)}
-        lists = [keep.tile([P, T // 16], U16, name="list%d" % d) for d in range(LISTS)]
+        a_raw = {(c, d): held([P, PACK, CHUNK], F32, "a_raw%d_%d" % (c, d)) for c in range(CHUNKS) for d in range(LISTS)}
+        lists = [keep.tile([P, T // PER_COLUMN], U16, name="list%d" % d) for d in range(LISTS)]
 
         def load_rows(tile, rows):
             nc.sync.dma_start(out=tile[:], in_=rows.rearrange("(p j) n -> p j n", j=PACK))
 
         def load_a(c, d):
-            load_rows(a_raw[(c, d)], aT[:, d * T + starts[c]:d * T + starts[c] + WIDTHS[c]])
+            load_rows(a_raw[(c, d)], aT[:, d * T + c * CHUNK:d * T + (c + 1) * CHUNK])
 
         def load_w1(g):
-            load_rows(w1_raw[g], w1[g * 512:(g + 1) * 512, :])
+            load_rows(w1_raw[g], w1[g * PASS:(g + 1) * PASS, :])
 
         def load_x(g):
             nc.sync.dma_start(out=x_codes[g][:].bitcast(I32), in_=x_words[g].bitcast(I32))
-
-        def load_scales():
-            for quad in range(4):
-                nc.sync.dma_start(
-                    out=x_plane[32 * quad:32 * quad + 4, :, :].bitcast(I32),
-                    in_=x_scales[:, 4 * quad:4 * quad + 4, :].rearrange("g r n -> r g n").bitcast(I32),
-                )
-
-        def load_lists():
-            nc.sync.dma_start(lists[0][:], pos1)
-            nc.sync.dma_start(lists[1][:], pos2)
-
-        def load_w2():
-            w2_rows = w2.rearrange("(q t i) n -> i q t n", t=PACK, i=4)
-            for i in range(4):
-                nc.sync.dma_start(out=w2_raw[i:P:4, :, :], in_=w2_rows[i])
 
         nc.gpsimd.memset(x_plane[:].bitcast(I32), 0)
         warm_in = held([P, 1], F32, "warm_in")
@@ -86,284 +73,264 @@ def tile_picked_wdime_none_l_kernel(
         make_identity(nc, identity[:])
 
         load_w1(0)
-        load_scales()
+        for quad in range(4):
+            nc.sync.dma_start(
+                out=x_plane[32 * quad:32 * quad + 4, :, :].bitcast(I32),
+                in_=x_scales[:, 4 * quad:4 * quad + 4, :].rearrange("g r n -> r g n").bitcast(I32),
+            )
         load_x(0)
         load_w1(1)
         load_x(1)
+        nc.sync.dma_start(lists[0][:], pos1)
+        nc.sync.dma_start(lists[1][:], pos2)
         load_a(0, 0)
         load_rows(w3_raw, w3)
-        load_lists()
         load_a(0, 1)
-        load_a(1, 0)
-        load_a(1, 1)
-        load_a(2, 0)
-        load_a(2, 1)
-        load_w2()
-        load_a(3, 0)
-        load_a(3, 1)
+        for c in (1, 2):
+            for d in range(LISTS):
+                load_a(c, d)
+        w2_rows = w2.rearrange("(q t r) n -> r q t n", t=PACK, r=4)
+        for r in range(4):
+            nc.sync.dma_start(out=w2_raw[r:P:4, :, :], in_=w2_rows[r])
+        for d in range(LISTS):
+            load_a(3, d)
 
-        def copy_on(engine, out_ap, in_ap):
-            if engine == "vector":
-                nc.vector.tensor_copy(out=out_ap, in_=in_ap)
-            else:
-                nc.scalar.copy(out=out_ap, in_=in_ap)
+        copy = {"vector": nc.vector.tensor_copy, "scalar": nc.scalar.copy}
+
+        def round_weights(engine, raw, t0, tiles, grouped):
+            copy[engine](
+                out=grouped.rearrange("p (t q r) j -> p t q j r", t=tiles, r=4),
+                in_=raw[:].rearrange("p j (q t r) -> p t q j r", t=PACK, r=4)[:, t0:t0 + tiles],
+            )
+
+        def round_columns(engine, raw, grouped):
+            copy[engine](
+                out=grouped.rearrange("p (c e) j -> p c j e", e=2),
+                in_=raw[:].rearrange("p j (c e) -> p c j e", e=2),
+            )
 
         def quantise(grouped, name):
             width = grouped.shape[1]
             codes = held([P, width], U32, name + "_codes")
             plane = held([P, width], U8, name + "_plane")
-            nc.vector.quantize_mx(
-                out=codes[:].bitcast(FP8X4), scales=plane[:], in_=grouped[:].rearrange("p w j -> p (w j)")
-            )
+            nc.vector.quantize_mx(out=codes[:].bitcast(FP8X4), scales=plane[:], in_=grouped.rearrange("p w j -> p (w j)"))
             return codes, plane
 
-        def cast_weights(engine, raw, t0, tiles, name, slot=None, into=None, step=2):
-            grouped = held([P, tiles * P, PACK], BF16, name + "_bf", slot) if into is None else into
-            src = raw[:].rearrange("p j (q t i) -> p t q j i", t=PACK, i=4)
-            dst = grouped[:].rearrange("p (t q i) j -> p t q j i", t=tiles, i=4)
-            for t in range(0, tiles, step):
-                copy_on(engine, dst[:, t:t + step], src[:, t0 + t:t0 + t + step])
-            return grouped
+        def parts(operand, width):
+            codes, plane = operand
+            return [(codes[:, at:at + width], plane[:, at:at + width]) for at in range(0, codes.shape[1], width)]
 
-        def cast_columns(engine, raw, name, slot=None):
-            width = raw.shape[2]
-            grouped = held([P, width, PACK], BF16, name + "_bf", slot)
-            copy_on(
-                engine,
-                grouped[:].rearrange("p (c i) j -> p c j i", i=2),
-                raw[:].rearrange("p j (c i) -> p c j i", i=2),
+        def multiply(result, stationary, moving):
+            nc.tensor.matmul_mx(
+                out=result,
+                lhsT=stationary[0].bitcast(FP8X4),
+                lhsT_scale=stationary[1],
+                rhs=moving[0].bitcast(FP8X4),
+                rhs_scale=moving[1],
+                start=True,
+                stop=True,
             )
-            return grouped
+
+        a_bf = {}
+        a_q = {}
+
+        def round_piece(engine, c, d, takes_over=None):
+            a_bf[(c, d)] = held([P, CHUNK, PACK], BF16, "a%d_%d_bf" % (c, d), takes_over)
+            round_columns(engine, a_raw[(c, d)], a_bf[(c, d)][:])
+
+        def quantise_piece(c, d):
+            a_q[(c, d)] = parts(quantise(a_bf[(c, d)][:], "a%d_%d" % (c, d)), CHUNK)[0]
+
+        def round_beside(c, d, takes_over=None):
+            if d == 0:
+                a_bf[c] = held([P, LISTS * CHUNK, PACK], BF16, "a%d_bf" % c, takes_over)
+            round_columns("scalar", a_raw[(c, d)], a_bf[c][:, d * CHUNK:(d + 1) * CHUNK, :])
+
+        def quantise_chunk(c):
+            for d, piece in enumerate(parts(quantise(a_bf[c][:], "a%d" % c), CHUNK)):
+                a_q[(c, d)] = piece
 
         h = [held([P, T], F32, "h%d" % t) for t in range(PACK)]
         h_banks = {}
-        w1_q = {}
-        w3_q = {}
-        a_bf = {}
-        a_q = {}
+        w3_q = []
         f = {}
-
-        def quantise_tiles(store, key, grouped, t0, name):
-            codes, plane = quantise(grouped, name)
-            for e in range(grouped.shape[1] // P):
-                store[key + (t0 + e,)] = (codes[:, e * P:(e + 1) * P], plane[:, e * P:(e + 1) * P])
-
-        def first_layer_pass(g, t):
-            if g == 0:
-                h_banks[t] = [new_bank(role) for role in (("filter", "filter"), ("filter", "filter"), ("sum", "sum"), ("back", "filter"))[t]]
-            codes, plane = w1_q[(g, t)]
-            for half in range(2):
-                nc.tensor.matmul_mx(
-                    out=h_banks[t][half][:],
-                    lhsT=codes.bitcast(FP8X4),
-                    lhsT_scale=plane,
-                    rhs=x_codes[g][:, 2 * half * BANK:2 * (half + 1) * BANK].bitcast(FP4X4),
-                    rhs_scale=x_plane[:, g, half * BANK:(half + 1) * BANK],
-                    start=(g == 0),
-                    stop=(g == 1),
-                )
+        terms = {}
 
         def activate(t):
             for half in range(2):
                 nc.scalar.activation(h[t][:, half * BANK:(half + 1) * BANK], h_banks[t][half][:], SILU)
 
-        def cast_a(engine, c, d, slot=None):
-            a_bf[(c, d)] = cast_columns(engine, a_raw[(c, d)], "a%d_%d" % (c, d), slot)
-
-        def quantise_a(c, d):
-            a_q[(c, d)] = quantise(a_bf[(c, d)], "a%d_%d" % (c, d))
-
-        def filters(c, d, t0, tiles, engine="scalar", slot=None):
-            width = WIDTHS[c]
-            made = held([P, tiles, width], F32, "f%d_%d_%d" % (c, d, t0), slot)
-            bank = new_bank("filter")
-            a_codes, a_plane = a_q[(c, d)]
+        def filters(c, d, t0, tiles=2, role="filter", takes_over=None):
+            made = held([P, tiles, CHUNK], F32, "f%d_%d_%d" % (c, d, t0), takes_over)
+            bank = new_bank(role)
             for e in range(tiles):
-                w_codes, w_plane = w3_q[(t0 + e,)]
-                nc.tensor.matmul_mx(
-                    out=bank[:, e * width:(e + 1) * width],
-                    lhsT=w_codes.bitcast(FP8X4),
-                    lhsT_scale=w_plane,
-                    rhs=a_codes[:].bitcast(FP8X4),
-                    rhs_scale=a_plane[:],
-                    start=True,
-                    stop=True,
-                )
+                multiply(bank[:, e * CHUNK:(e + 1) * CHUNK], w3_q[t0 + e], a_q[(c, d)])
                 f[(c, d, t0 + e)] = made[:, e, :]
-            copy_on(engine, made[:].rearrange("p e n -> p (e n)"), bank[:, 0:tiles * width])
+            nc.scalar.copy(out=made[:].rearrange("p e n -> p (e n)"), in_=bank[:, 0:tiles * CHUNK])
 
-        def all_filters(c, d):
-            tiles = BANK // WIDTHS[c]
-            for t0 in range(0, PACK, tiles):
-                filters(c, d, t0, tiles)
+        def all_filters(c, d, role="filter"):
+            for t0 in (0, 2):
+                filters(c, d, t0, role=role)
 
-        terms = {}
+        def offsets(c, d):
+            return lists[d][:, c * CHUNK // PER_COLUMN:(c + 1) * CHUNK // PER_COLUMN]
 
-        def gathers(c, d, tiles=range(PACK), slot=None):
+        def gathers(c, d, tiles=range(PACK)):
             if (c, d) not in terms:
-                terms[(c, d)] = held([P, PACK, WIDTHS[c]], F32, "term%d_%d" % (c, d), slot)
-            offsets = lists[d][:, starts[c] // 16:(starts[c] + WIDTHS[c]) // 16]
+                terms[(c, d)] = held([P, PACK, CHUNK], F32, "term%d_%d" % (c, d))
             for t in tiles:
-                nc.vector.tensor_tensor(terms[(c, d)][:, t, :], h[t][:].indirect(offsets), f[(c, d, t)], MULT)
-
-        def add_on_vector(summed, c, at, width):
-            nc.vector.tensor_tensor(
-                summed.rearrange("p (c i) t -> p c t i", i=2),
-                terms[(c, 0)][:, :, at:at + width].rearrange("p t (c i) -> p c t i", i=2),
-                terms[(c, 1)][:, :, at:at + width].rearrange("p t (c i) -> p c t i", i=2),
-                ADD,
-            )
+                nc.vector.tensor_tensor(terms[(c, d)][:, t, :], h[t][:].indirect(offsets(c, d)), f[(c, d, t)], MULT)
 
         sums = {}
         rows = {}
         turned = {}
 
-        def add_on_tensor(c, b):
-            bank = new_bank("sum")
-            sums[(c, b)] = bank
-            for t in range(PACK):
-                for d in range(LISTS):
-                    nc.tensor.matmul(
-                        bank[:, t * P:(t + 1) * P],
-                        lhsT=terms[(c, d)][:, t, b * P:(b + 1) * P],
-                        rhs=identity[:],
-                        start=(d == 0),
-                        stop=(d == LISTS - 1),
-                        is_transpose=True,
-                    )
+        def add_on_tensor(c):
+            for b in range(CHUNK // P):
+                sums[(c, b)] = new_bank("sum")
+                for t in range(PACK):
+                    for d in range(LISTS):
+                        nc.tensor.matmul(
+                            sums[(c, b)][:, t * P:(t + 1) * P],
+                            lhsT=terms[(c, d)][:, t, b * P:(b + 1) * P],
+                            rhs=identity[:],
+                            start=(d == 0),
+                            stop=(d == LISTS - 1),
+                            is_transpose=True,
+                        )
 
-        def round_sum(c, b, slot=None):
-            rows[(c, b)] = held([P, 2, P, 2], BF16, "row%d_%d" % (c, b), slot)
+        def round_sum(c, b):
+            rows[(c, b)] = held([P, 2, P, 2], BF16, "row%d_%d" % (c, b))
             nc.scalar.copy(out=rows[(c, b)][:], in_=sums[(c, b)][:].rearrange("v (u e p) -> v u p e", u=2, e=2))
 
-        def turn_back(blocks):
-            bank = new_bank("back")
-            turned[blocks[0]] = bank
-            for i, block in enumerate(blocks):
-                words = rows[block][:].rearrange("v u p e -> v (u p e)").bitcast(F32)
+        def turn_back(c):
+            turned[c] = new_bank("back")
+            for b in range(CHUNK // P):
+                pairs = rows[(c, b)][:].rearrange("v u p e -> v (u p e)").bitcast(F32)
                 for u in range(2):
-                    at = (2 * i + u) * P
-                    nc.tensor.transpose(bank[:, at:at + P], words[:, u * P:(u + 1) * P], identity[:])
+                    at = (2 * b + u) * P
+                    nc.tensor.transpose(turned[c][:, at:at + P], pairs[:, u * P:(u + 1) * P], identity[:])
 
-        def lay_words(grouped, first, count):
-            z_words = grouped.rearrange("p v t -> p (v t)").bitcast(F32)
+        def lay_pairs(c, grouped):
             nc.scalar.copy(
-                out=z_words.rearrange("p (b v u) -> p b v u", b=count, u=2),
-                in_=turned[first][:, 0:count * 2 * P].rearrange("p (b u v) -> p b v u", b=count, u=2),
+                out=grouped.rearrange("p v t -> p (v t)").bitcast(F32).rearrange("p (b v u) -> p b v u", b=2, u=2),
+                in_=turned[c][:].rearrange("p (b u v) -> p b v u", b=2, u=2),
             )
 
-        w2_q = []
-
-        def project(v0, codes, plane, engine="scalar", role="filter"):
-            width = codes.shape[1]
+        def project(v0, z_q, role="filter"):
+            width = z_q[0].shape[1]
             bank = new_bank(role)
-            nc.tensor.matmul_mx(
-                out=bank[:, 0:width],
-                lhsT=w2_q[0][:].bitcast(FP8X4),
-                lhsT_scale=w2_q[1][:],
-                rhs=codes[:].bitcast(FP8X4),
-                rhs_scale=plane[:],
-                start=True,
-                stop=True,
-            )
+            multiply(bank[:, 0:width], parts(w2_q, N)[0], parts(z_q, width)[0])
             result = held([P, width], F32, "result%d" % v0)
-            copy_on(engine, result[:], bank[:, 0:width])
+            nc.scalar.copy(out=result[:], in_=bank[:, 0:width])
             nc.sync.dma_start(out=out[:, v0:v0 + width], in_=result[:])
 
-        def cast_both(c, d):
-            if d == 0:
-                a_bf[c] = held([P, 2 * WIDTHS[c], PACK], BF16, "a%d_bf" % c)
-            nc.scalar.copy(
-                out=a_bf[c][:, d * WIDTHS[c]:(d + 1) * WIDTHS[c], :].rearrange("p (c i) j -> p c j i", i=2),
-                in_=a_raw[(c, d)][:].rearrange("p j (c i) -> p c j i", i=2),
-            )
+        picked = held([P, CHUNK], F32, "picked")
 
-        def quantise_both(c):
-            codes, plane = quantise(a_bf[c], "a%d" % c)
-            for d in range(LISTS):
-                cols = slice(d * WIDTHS[c], (d + 1) * WIDTHS[c])
-                a_q[(c, d)] = (codes[:, cols], plane[:, cols])
-
-        low = cast_weights("vector", w1_raw[0], 0, 2, "w1_0a")
+        low = held([P, 2 * P, PACK], BF16, "w1_0a_bf")
+        round_weights("vector", w1_raw[0], 0, 2, low[:])
         high = held([P, 4 * P, PACK], BF16, "w1_high_bf")
-        cast_weights("scalar", w1_raw[0], 2, 2, "", into=high[:, 0:2 * P, :])
-        quantise_tiles(w1_q, (0,), low, 0, "w1_0a")
-        low = cast_weights("vector", w1_raw[1], 0, 2, "w1_1a", step=1)
-        cast_weights("scalar", w1_raw[1], 2, 2, "", into=high[:, 2 * P:4 * P, :])
+        round_weights("scalar", w1_raw[0], 2, 2, high[:, 0:2 * P, :])
+        w1_q = [parts(quantise(low[:], "w1_0a"), P), []]
+        low = held([P, 2 * P, PACK], BF16, "w1_1a_bf")
         for t in range(2):
-            quantise_tiles(w1_q, (1,), low[:, t * P:(t + 1) * P, :], t, "w1_1_%d" % t)
-        high_q = {}
-        quantise_tiles(high_q, (), high, 0, "w1_high")
-        for g in range(2):
-            for e in range(2):
-                w1_q[(g, 2 + e)] = high_q[(2 * g + e,)]
+            round_weights("vector", w1_raw[1], t, 1, low[:, t * P:(t + 1) * P, :])
+        round_weights("scalar", w1_raw[1], 2, 2, high[:, 2 * P:4 * P, :])
+        for t in range(2):
+            w1_q[1].extend(parts(quantise(low[:, t * P:(t + 1) * P, :], "w1_1_%d" % t), P))
+        high_q = parts(quantise(high[:], "w1_high"), P)
+        for g in range(K // PASS):
+            w1_q[g].extend(high_q[2 * g:2 * g + 2])
         for t in range(PACK):
-            first_layer_pass(0, t)
-            first_layer_pass(1, t)
-        cast_a("vector", 0, 0)
-        quantise_a(0, 0)
-        for t in range(3):
-            activate(t)
-        for u in range(2):
-            quantise_tiles(w3_q, (), cast_weights("vector", w3_raw, 2 * u, 2, "w3_%d" % u), 2 * u, "w3_%d" % u)
-        filters(0, 0, 0, 2)
-        activate(3)
-        filters(0, 0, 2, 2)
-        cast_a("vector", 0, 1, "w3_0_bf")
-        quantise_a(0, 1)
+            h_banks[t] = [new_bank(role) for role in FIRST_LAYER_BANKS[t]]
+            for g in range(K // PASS):
+                for half in range(2):
+                    nc.tensor.matmul_mx(
+                        out=h_banks[t][half][:],
+                        lhsT=w1_q[g][t][0].bitcast(FP8X4),
+                        lhsT_scale=w1_q[g][t][1],
+                        rhs=x_codes[g][:, 2 * half * BANK:2 * (half + 1) * BANK].bitcast(FP4X4),
+                        rhs_scale=x_plane[:, g, half * BANK:(half + 1) * BANK],
+                        start=(g == 0),
+                        stop=(g == K // PASS - 1),
+                    )
 
-        cast_a("scalar", 1, 0, "a0_0_codes")
-        gathers(0, 0)
-        quantise_a(1, 0)
+        round_piece("vector", 0, 0)
+        quantise_piece(0, 0)
+        for t in range(PACK - 1):
+            activate(t)
+        nc.vector.tensor_copy(out=picked[:], in_=h[0][:].indirect(offsets(0, 0)))
+        for u in range(2):
+            w3_bf = held([P, 2 * P, PACK], BF16, "w3_%d_bf" % u)
+            round_weights("vector", w3_raw, 2 * u, 2, w3_bf[:])
+            w3_q.extend(parts(quantise(w3_bf[:], "w3_%d" % u), P))
+        bank = new_bank("filter")
+        multiply(bank[:, 0:CHUNK], w3_q[0], a_q[(0, 0)])
+        terms[(0, 0)] = held([P, PACK, CHUNK], F32, "term0_0")
+        nc.vector.tensor_tensor(terms[(0, 0)][:, 0, :], bank[:, 0:CHUNK], picked[:], MULT)
+        filters(0, 0, 1, tiles=1)
+        activate(PACK - 1)
+        filters(0, 0, 2)
+        round_piece("vector", 0, 1, takes_over="w3_0_bf")
+        quantise_piece(0, 1)
+
+        round_piece("scalar", 1, 0, takes_over="a0_0_codes")
+        gathers(0, 0, range(1, PACK))
+        quantise_piece(1, 0)
         all_filters(0, 1)
-        cast_a("scalar", 1, 1)
+        round_piece("scalar", 1, 1, takes_over="a0_1_codes")
         gathers(0, 1)
-        quantise_a(1, 1)
-        all_filters(1, 0)
-        cast_both(2, 0)
-        cast_both(2, 1)
+        quantise_piece(1, 1)
+        all_filters(1, 0, role="sum")
+        round_beside(2, 0, takes_over="a1_0_codes")
+        round_beside(2, 1)
         gathers(1, 0)
-        quantise_both(2)
+        quantise_chunk(2)
         all_filters(1, 1)
-        add_on_tensor(0, 0)
-        add_on_tensor(0, 1)
-        cast_both(3, 0)
+        add_on_tensor(0)
+        round_beside(3, 0, takes_over="a1_1_codes")
         round_sum(0, 0)
         gathers(1, 1)
         all_filters(2, 0)
-        cast_both(3, 1)
+        round_beside(3, 1)
         round_sum(0, 1)
         gathers(2, 0)
-        quantise_both(3)
+        quantise_chunk(3)
         all_filters(2, 1)
-        add_on_tensor(1, 0)
-        add_on_tensor(1, 1)
-        turn_back([(0, 0), (0, 1)])
-        early = held([P, 512, PACK], BF16, "early")
-        late = held([P, 256, PACK], BF16, "late")
-        w2_q.extend(quantise(cast_columns("scalar", w2_raw, "w2"), "w2"))
+        add_on_tensor(1)
+        turn_back(0)
+        early = held([P, 2 * CHUNK, PACK], BF16, "early")
+        late = held([P, CHUNK, PACK], BF16, "late")
+        w2_bf = held([P, N, PACK], BF16, "w2_bf")
+        round_columns("scalar", w2_raw, w2_bf[:])
+        w2_q = quantise(w2_bf[:], "w2")
         round_sum(1, 0)
-        lay_words(early[:, 0:256, :], (0, 0), 2)
+        lay_pairs(0, early[:, 0:CHUNK, :])
         gathers(2, 1)
         all_filters(3, 0)
         round_sum(1, 1)
-        turn_back([(1, 0), (1, 1)])
-        lay_words(early[:, 256:512, :], (1, 0), 2)
+        turn_back(1)
+        lay_pairs(1, early[:, CHUNK:2 * CHUNK, :])
         gathers(3, 0)
-        early_q = quantise(early, "early")
-        filters(3, 1, 0, 2, slot="row1_1")
-        filters(3, 1, 2, 2)
-        add_on_tensor(2, 0)
-        add_on_tensor(2, 1)
+        early_q = quantise(early[:], "early")
+        filters(3, 1, 0, takes_over="row1_1")
+        filters(3, 1, 2)
+        add_on_tensor(2)
         round_sum(2, 0)
         round_sum(2, 1)
-        turn_back([(2, 0), (2, 1)])
-        lay_words(late[:], (2, 0), 2)
-        project(0, *early_q, role="back")
+        turn_back(2)
+        lay_pairs(2, late[:])
+        project(0, early_q, role="back")
         gathers(3, 1)
-        project(512, *quantise(late, "late"))
-        last = held([P, 256, PACK], BF16, "last", "late")
-        for b in range(2):
-            add_on_vector(last[:, b * P:(b + 1) * P, :], 3, b * P, P)
-        for b in range(2):
-            project(768 + b * P, *quantise(last[:, b * P:(b + 1) * P, :], "last%d" % b))
+        project(2 * CHUNK, quantise(late[:], "late"))
+
+        last = held([P, CHUNK, PACK], BF16, "last", takes_over="late")
+        for b in range(CHUNK // P):
+            nc.vector.tensor_tensor(
+                last[:, b * P:(b + 1) * P, :].rearrange("p (c e) t -> p c t e", e=2),
+                terms[(3, 0)][:, :, b * P:(b + 1) * P].rearrange("p t (c e) -> p c t e", e=2),
+                terms[(3, 1)][:, :, b * P:(b + 1) * P].rearrange("p t (c e) -> p c t e", e=2),
+                ADD,
+            )
+        for b in range(CHUNK // P):
+            project(3 * CHUNK + b * P, quantise(last[:, b * P:(b + 1) * P, :], "last%d" % b))

@@ -26,8 +26,6 @@ CHUNK = 256
 CHUNKS = T // CHUNK
 LISTS = 2
 PER_COLUMN = 16
-BANKS = {"filter": 5, "sum": 2, "back": 1}
-FIRST_LAYER_BANKS = (("filter", "filter"), ("filter", "filter"), ("sum", "sum"), ("back", "filter"))
 
 
 def tile_picked_wdime_none_l_kernel(
@@ -38,8 +36,8 @@ def tile_picked_wdime_none_l_kernel(
         keep = ctx.enter_context(tc.tile_pool(name="keep", bufs=1))
         psum = ctx.enter_context(tc.psum_pool(name="psum", bufs=1))
 
-        def new_bank(role):
-            return psum.tile([P, BANK], F32, name=role, tag=role, bufs=BANKS[role])
+        def new_bank(number):
+            return psum.tile([P, BANK], F32, name="bank%d" % number, tag="bank%d" % number)
 
         def held(shape, dtype, name, takes_over=None):
             return keep.tile(shape, dtype, name=name, tag=takes_over or name, align_bytes=64)
@@ -73,11 +71,9 @@ def tile_picked_wdime_none_l_kernel(
         make_identity(nc, identity[:])
 
         load_w1(0)
-        for quad in range(4):
-            nc.sync.dma_start(
-                out=x_plane[32 * quad:32 * quad + 4, :, :].bitcast(I32),
-                in_=x_scales[:, 4 * quad:4 * quad + 4, :].rearrange("g r n -> r g n").bitcast(I32),
-            )
+        scale_rows = x_scales.rearrange("g (quad r) n -> r quad g n", r=4)
+        for r in range(4):
+            nc.sync.dma_start(out=x_plane[r:P:32, :, :].bitcast(I32), in_=scale_rows[r].bitcast(I32))
         load_x(0)
         load_w1(1)
         load_x(1)
@@ -154,23 +150,31 @@ def tile_picked_wdime_none_l_kernel(
         h_banks = {}
         w3_q = []
         f = {}
+        f_banks = {}
         terms = {}
 
         def activate(t):
             for half in range(2):
                 nc.scalar.activation(h[t][:, half * BANK:(half + 1) * BANK], h_banks[t][half][:], SILU)
 
-        def filters(c, d, t0, tiles=2, role="filter", takes_over=None):
-            made = held([P, tiles, CHUNK], F32, "f%d_%d_%d" % (c, d, t0), takes_over)
-            bank = new_bank(role)
+        def multiply_filters(c, d, t0, role, tiles=2):
+            f_banks[(c, d, t0)] = new_bank(role)
             for e in range(tiles):
-                multiply(bank[:, e * CHUNK:(e + 1) * CHUNK], w3_q[t0 + e], a_q[(c, d)])
-                f[(c, d, t0 + e)] = made[:, e, :]
-            nc.scalar.copy(out=made[:].rearrange("p e n -> p (e n)"), in_=bank[:, 0:tiles * CHUNK])
+                multiply(f_banks[(c, d, t0)][:, e * CHUNK:(e + 1) * CHUNK], w3_q[t0 + e], a_q[(c, d)])
 
-        def all_filters(c, d, role="filter"):
-            for t0 in (0, 2):
-                filters(c, d, t0, role=role)
+        def copy_filters(c, d, t0, tiles=2, takes_over=None):
+            made = held([P, tiles, CHUNK], F32, "f%d_%d_%d" % (c, d, t0), takes_over)
+            for e in range(tiles):
+                f[(c, d, t0 + e)] = made[:, e, :]
+            nc.scalar.copy(out=made[:].rearrange("p e n -> p (e n)"), in_=f_banks[(c, d, t0)][:, 0:tiles * CHUNK])
+
+        def filters(c, d, t0, role, tiles=2):
+            multiply_filters(c, d, t0, role, tiles)
+            copy_filters(c, d, t0, tiles)
+
+        def all_filters(c, d, roles):
+            for u in range(2):
+                filters(c, d, 2 * u, roles[u])
 
         def offsets(c, d):
             return lists[d][:, c * CHUNK // PER_COLUMN:(c + 1) * CHUNK // PER_COLUMN]
@@ -185,10 +189,11 @@ def tile_picked_wdime_none_l_kernel(
         rows = {}
         turned = {}
 
-        def add_on_tensor(c):
+        def add_on_tensor(c, roles):
             for b in range(CHUNK // P):
-                sums[(c, b)] = new_bank("sum")
-                for t in range(PACK):
+                sums[(c, b)] = new_bank(roles[b])
+            for t in range(PACK):
+                for b in range(CHUNK // P):
                     for d in range(LISTS):
                         nc.tensor.matmul(
                             sums[(c, b)][:, t * P:(t + 1) * P],
@@ -203,8 +208,8 @@ def tile_picked_wdime_none_l_kernel(
             rows[(c, b)] = held([P, 2, P, 2], BF16, "row%d_%d" % (c, b))
             nc.scalar.copy(out=rows[(c, b)][:], in_=sums[(c, b)][:].rearrange("v (u e p) -> v u p e", u=2, e=2))
 
-        def turn_back(c):
-            turned[c] = new_bank("back")
+        def turn_back(c, role):
+            turned[c] = new_bank(role)
             for b in range(CHUNK // P):
                 pairs = rows[(c, b)][:].rearrange("v u p e -> v (u p e)").bitcast(F32)
                 for u in range(2):
@@ -217,12 +222,15 @@ def tile_picked_wdime_none_l_kernel(
                 in_=turned[c][:].rearrange("p (b u v) -> p b v u", b=2, u=2),
             )
 
-        def project(v0, z_q, role="filter"):
-            width = z_q[0].shape[1]
+        def project(v0, z_qs, role, engine="scalar"):
             bank = new_bank(role)
-            multiply(bank[:, 0:width], parts(w2_q, N)[0], parts(z_q, width)[0])
+            width = 0
+            for z_q in z_qs:
+                columns = z_q[0].shape[1]
+                multiply(bank[:, width:width + columns], parts(w2_q, N)[0], parts(z_q, columns)[0])
+                width = width + columns
             result = held([P, width], F32, "result%d" % v0)
-            nc.scalar.copy(out=result[:], in_=bank[:, 0:width])
+            copy[engine](out=result[:], in_=bank[:, 0:width])
             nc.sync.dma_start(out=out[:, v0:v0 + width], in_=result[:])
 
         picked = held([P, CHUNK], F32, "picked")
@@ -242,7 +250,7 @@ def tile_picked_wdime_none_l_kernel(
         for g in range(K // PASS):
             w1_q[g].extend(high_q[2 * g:2 * g + 2])
         for t in range(PACK):
-            h_banks[t] = [new_bank(role) for role in FIRST_LAYER_BANKS[t]]
+            h_banks[t] = [new_bank(2 * t + half) for half in range(2)]
             for g in range(K // PASS):
                 for half in range(2):
                     nc.tensor.matmul_mx(
@@ -264,73 +272,74 @@ def tile_picked_wdime_none_l_kernel(
             w3_bf = held([P, 2 * P, PACK], BF16, "w3_%d_bf" % u)
             round_weights("vector", w3_raw, 2 * u, 2, w3_bf[:])
             w3_q.extend(parts(quantise(w3_bf[:], "w3_%d" % u), P))
-        bank = new_bank("filter")
+        bank = new_bank(0)
         multiply(bank[:, 0:CHUNK], w3_q[0], a_q[(0, 0)])
         terms[(0, 0)] = held([P, PACK, CHUNK], F32, "term0_0")
         nc.vector.tensor_tensor(terms[(0, 0)][:, 0, :], bank[:, 0:CHUNK], picked[:], MULT)
-        filters(0, 0, 1, tiles=1)
+        filters(0, 0, 1, 1, tiles=1)
         activate(PACK - 1)
-        filters(0, 0, 2)
+        filters(0, 0, 2, 2)
         round_piece("vector", 0, 1, takes_over="w3_0_bf")
         quantise_piece(0, 1)
-
         round_piece("scalar", 1, 0, takes_over="a0_0_codes")
         gathers(0, 0, range(1, PACK))
         quantise_piece(1, 0)
-        all_filters(0, 1)
+        all_filters(0, 1, (3, 4))
         round_piece("scalar", 1, 1, takes_over="a0_1_codes")
         gathers(0, 1)
         quantise_piece(1, 1)
-        all_filters(1, 0, role="sum")
+        all_filters(1, 0, (5, 6))
         round_beside(2, 0, takes_over="a1_0_codes")
         round_beside(2, 1)
         gathers(1, 0)
         quantise_chunk(2)
-        all_filters(1, 1)
-        add_on_tensor(0)
+        all_filters(1, 1, (7, 0))
+        add_on_tensor(0, (5, 6))
         round_beside(3, 0, takes_over="a1_1_codes")
-        round_sum(0, 0)
         gathers(1, 1)
-        all_filters(2, 0)
+        all_filters(2, 0, (1, 2))
         round_beside(3, 1)
-        round_sum(0, 1)
         gathers(2, 0)
         quantise_chunk(3)
-        all_filters(2, 1)
-        add_on_tensor(1)
-        turn_back(0)
-        early = held([P, 2 * CHUNK, PACK], BF16, "early")
-        late = held([P, CHUNK, PACK], BF16, "late")
-        w2_bf = held([P, N, PACK], BF16, "w2_bf")
+        all_filters(2, 1, (3, 4))
+        add_on_tensor(1, (7, 0))
+        round_sum(0, 0)
+        round_sum(0, 1)
+        w2_bf = held([P, N, PACK], BF16, "w2_bf", takes_over="f2_0_0")
         round_columns("scalar", w2_raw, w2_bf[:])
-        w2_q = quantise(w2_bf[:], "w2")
-        round_sum(1, 0)
-        lay_pairs(0, early[:, 0:CHUNK, :])
         gathers(2, 1)
-        all_filters(3, 0)
+        all_filters(3, 0, (1, 2))
+        filters(3, 1, 0, 3)
+        multiply_filters(3, 1, 2, 4)
+        turn_back(0, 6)
+        add_on_tensor(2, (1, 2))
+        z = [held([P, CHUNK, PACK], BF16, "z%d" % c) for c in range(CHUNKS - 1)]
+        round_sum(1, 0)
         round_sum(1, 1)
-        turn_back(1)
-        lay_pairs(1, early[:, CHUNK:2 * CHUNK, :])
-        gathers(3, 0)
-        early_q = quantise(early[:], "early")
-        filters(3, 1, 0, takes_over="row1_1")
-        filters(3, 1, 2)
-        add_on_tensor(2)
+        turn_back(1, 5)
+        lay_pairs(0, z[0][:])
+        copy_filters(3, 1, 2, takes_over="row0_1")
         round_sum(2, 0)
         round_sum(2, 1)
-        turn_back(2)
-        lay_pairs(2, late[:])
-        project(0, early_q, role="back")
-        gathers(3, 1)
-        project(2 * CHUNK, quantise(late[:], "late"))
-
-        last = held([P, CHUNK, PACK], BF16, "last", takes_over="late")
-        for b in range(CHUNK // P):
+        turn_back(2, 7)
+        lay_pairs(1, z[1][:])
+        lay_pairs(2, z[2][:])
+        w2_q = quantise(w2_bf[:], "w2")
+        gathers(3, 0)
+        gathers(3, 1, (0, 1))
+        project(0, [quantise(z[0][:], "z0")], 5)
+        gathers(3, 1, (2, 3))
+        project(CHUNK, [quantise(z[1][:], "z1")], 6)
+        last = held([P, CHUNK, PACK], BF16, "last", takes_over="z0_codes")
+        def add_on_vector(b):
             nc.vector.tensor_tensor(
                 last[:, b * P:(b + 1) * P, :].rearrange("p (c e) t -> p c t e", e=2),
                 terms[(3, 0)][:, :, b * P:(b + 1) * P].rearrange("p t (c e) -> p c t e", e=2),
                 terms[(3, 1)][:, :, b * P:(b + 1) * P].rearrange("p t (c e) -> p c t e", e=2),
                 ADD,
             )
+        add_on_vector(0)
+        project(2 * CHUNK, [quantise(z[2][:], "z2")], 4)
+        add_on_vector(1)
         for b in range(CHUNK // P):
-            project(3 * CHUNK + b * P, quantise(last[:, b * P:(b + 1) * P, :], "last%d" % b))
+            project(3 * CHUNK + b * P, [quantise(last[:, b * P:(b + 1) * P, :], "last%d" % b)], (3, 0)[b])

@@ -82,14 +82,15 @@ def tile_picked_wdime_none_l_kernel(
         load_a(0, 0)
         load_rows(w3_raw, w3)
         load_a(0, 1)
-        for c in (1, 2):
-            for d in range(LISTS):
-                load_a(c, d)
+        for d in range(LISTS):
+            load_a(1, d)
+        for c in (2, 3):
+            load_a(c, 0)
         w2_rows = w2.rearrange("(q t r) n -> r q t n", t=PACK, r=4)
         for r in range(4):
             nc.sync.dma_start(out=w2_raw[r:P:4, :, :], in_=w2_rows[r])
-        for d in range(LISTS):
-            load_a(3, d)
+        for c in (2, 3):
+            load_a(c, 1)
 
         copy = {"vector": nc.vector.tensor_copy, "scalar": nc.scalar.copy}
 
@@ -138,13 +139,14 @@ def tile_picked_wdime_none_l_kernel(
             a_q[(c, d)] = parts(quantise(a_bf[(c, d)][:], "a%d_%d" % (c, d)), CHUNK)[0]
 
         def round_beside(c, d, takes_over=None):
-            if d == 0:
-                a_bf[c] = held([P, LISTS * CHUNK, PACK], BF16, "a%d_bf" % c, takes_over)
-            round_columns("scalar", a_raw[(c, d)], a_bf[c][:, d * CHUNK:(d + 1) * CHUNK, :])
+            if c == 2:
+                a_bf[d] = held([P, 2 * CHUNK, PACK], BF16, "a_late%d_bf" % d, takes_over)
+            round_columns("scalar", a_raw[(c, d)], a_bf[d][:, (c - 2) * CHUNK:(c - 1) * CHUNK, :])
 
-        def quantise_chunk(c):
-            for d, piece in enumerate(parts(quantise(a_bf[c][:], "a%d" % c), CHUNK)):
-                a_q[(c, d)] = piece
+        def quantise_late(d):
+            both = quantise(a_bf[d][:], "a_late%d" % d)
+            a_q[d] = parts(both, 2 * CHUNK)[0]
+            a_q[(2, d)], a_q[(3, d)] = parts(both, CHUNK)
 
         h = [held([P, T], F32, "h%d" % t) for t in range(PACK)]
         h_banks = {}
@@ -176,6 +178,20 @@ def tile_picked_wdime_none_l_kernel(
             for u in range(2):
                 filters(c, d, 2 * u, roles[u])
 
+        def wide_filter(t, role):
+            bank = new_bank(role)
+            multiply(bank[:], w3_q[t], a_q[0])
+            f[t] = held([P, 2 * CHUNK], F32, "f_wide%d" % t)
+            nc.scalar.copy(out=f[t][:], in_=bank[:])
+
+        def wide_gathers(tiles):
+            for t in tiles:
+                nc.vector.tensor_tensor(wide[:, t, :], h[t][:].indirect(lists[0][:, 2 * CHUNK // PER_COLUMN:]), f[t][:], MULT)
+
+        wide = held([P, PACK, 2 * CHUNK], F32, "wide")
+        terms[(2, 0)] = wide[:, :, 0:CHUNK]
+        terms[(3, 0)] = wide[:, :, CHUNK:2 * CHUNK]
+
         def offsets(c, d):
             return lists[d][:, c * CHUNK // PER_COLUMN:(c + 1) * CHUNK // PER_COLUMN]
 
@@ -190,31 +206,32 @@ def tile_picked_wdime_none_l_kernel(
         turned = {}
 
         def add_on_tensor(c, roles):
-            for b in range(CHUNK // P):
-                sums[(c, b)] = new_bank(roles[b])
-            for t in range(PACK):
-                for b in range(CHUNK // P):
-                    for d in range(LISTS):
-                        nc.tensor.matmul(
-                            sums[(c, b)][:, t * P:(t + 1) * P],
-                            lhsT=terms[(c, d)][:, t, b * P:(b + 1) * P],
-                            rhs=identity[:],
-                            start=(d == 0),
-                            stop=(d == LISTS - 1),
-                            is_transpose=True,
-                        )
+            for u in range(2):
+                sums[(c, u)] = new_bank(roles[u])
+                for e in range(2):
+                    for b in range(CHUNK // P):
+                        at = (2 * b + e) * P
+                        for d in range(LISTS):
+                            nc.tensor.matmul(
+                                sums[(c, u)][:, at:at + P],
+                                lhsT=terms[(c, d)][:, 2 * u + e, b * P:(b + 1) * P],
+                                rhs=identity[:],
+                                start=(d == 0),
+                                stop=(d == LISTS - 1),
+                                is_transpose=True,
+                            )
 
-        def round_sum(c, b):
-            rows[(c, b)] = held([P, 2, P, 2], BF16, "row%d_%d" % (c, b))
-            nc.scalar.copy(out=rows[(c, b)][:], in_=sums[(c, b)][:].rearrange("v (u e p) -> v u p e", u=2, e=2))
+        def round_sum(c, u):
+            rows[(c, u)] = held([P, 2, P, 2], BF16, "row%d_%d" % (c, u))
+            nc.scalar.copy(out=rows[(c, u)][:], in_=sums[(c, u)][:].rearrange("v (b e p) -> v b p e", b=2, e=2))
 
         def turn_back(c, role):
             turned[c] = new_bank(role)
-            for b in range(CHUNK // P):
-                pairs = rows[(c, b)][:].rearrange("v u p e -> v (u p e)").bitcast(F32)
-                for u in range(2):
+            for u in range(2):
+                pairs = rows[(c, u)][:].rearrange("v b p e -> v (b p e)").bitcast(F32)
+                for b in range(CHUNK // P):
                     at = (2 * b + u) * P
-                    nc.tensor.transpose(turned[c][:, at:at + P], pairs[:, u * P:(u + 1) * P], identity[:])
+                    nc.tensor.transpose(turned[c][:, at:at + P], pairs[:, b * P:(b + 1) * P], identity[:])
 
         def lay_pairs(c, grouped):
             nc.scalar.copy(
@@ -289,34 +306,38 @@ def tile_picked_wdime_none_l_kernel(
         gathers(0, 1)
         quantise_piece(1, 1)
         all_filters(1, 0, (5, 6))
+        add_on_tensor(0, (3, 4))
         round_beside(2, 0, takes_over="a1_0_codes")
-        round_beside(2, 1)
+        round_beside(3, 0)
         gathers(1, 0)
-        quantise_chunk(2)
+        quantise_late(0)
         all_filters(1, 1, (7, 0))
-        add_on_tensor(0, (5, 6))
-        round_beside(3, 0, takes_over="a1_1_codes")
+        round_beside(2, 1, takes_over="a1_1_codes")
         gathers(1, 1)
-        all_filters(2, 0, (1, 2))
+        wide_filter(0, 1)
+        wide_filter(1, 2)
         round_beside(3, 1)
-        gathers(2, 0)
-        quantise_chunk(3)
-        all_filters(2, 1, (3, 4))
+        wide_gathers((0, 1))
+        quantise_late(1)
+        wide_filter(2, 5)
+        wide_filter(3, 6)
         add_on_tensor(1, (7, 0))
         round_sum(0, 0)
         round_sum(0, 1)
-        w2_bf = held([P, N, PACK], BF16, "w2_bf", takes_over="f2_0_0")
+        w2_bf = held([P, N, PACK], BF16, "w2_bf", takes_over="f_wide0")
         round_columns("scalar", w2_raw, w2_bf[:])
+        wide_gathers((2, 3))
+        all_filters(2, 1, (1, 2))
+        filters(3, 1, 0, 5)
+        multiply_filters(3, 1, 2, 6)
+        turn_back(0, 4)
+        w2_q = quantise(w2_bf[:], "w2")
         gathers(2, 1)
-        all_filters(3, 0, (1, 2))
-        filters(3, 1, 0, 3)
-        multiply_filters(3, 1, 2, 4)
-        turn_back(0, 6)
         add_on_tensor(2, (1, 2))
         z = [held([P, CHUNK, PACK], BF16, "z%d" % c) for c in range(CHUNKS - 1)]
         round_sum(1, 0)
         round_sum(1, 1)
-        turn_back(1, 5)
+        turn_back(1, 3)
         lay_pairs(0, z[0][:])
         copy_filters(3, 1, 2, takes_over="row0_1")
         round_sum(2, 0)
@@ -324,12 +345,10 @@ def tile_picked_wdime_none_l_kernel(
         turn_back(2, 7)
         lay_pairs(1, z[1][:])
         lay_pairs(2, z[2][:])
-        w2_q = quantise(w2_bf[:], "w2")
-        gathers(3, 0)
         gathers(3, 1, (0, 1))
-        project(0, [quantise(z[0][:], "z0")], 5)
+        project(0, [quantise(z[0][:], "z0")], 2)
         gathers(3, 1, (2, 3))
-        project(CHUNK, [quantise(z[1][:], "z1")], 6)
+        project(CHUNK, [quantise(z[1][:], "z1")], 4)
         last = held([P, CHUNK, PACK], BF16, "last", takes_over="z0_codes")
         def add_on_vector(b):
             nc.vector.tensor_tensor(
@@ -339,7 +358,7 @@ def tile_picked_wdime_none_l_kernel(
                 ADD,
             )
         add_on_vector(0)
-        project(2 * CHUNK, [quantise(z[2][:], "z2")], 4)
+        project(2 * CHUNK, [quantise(z[2][:], "z2")], 6)
         add_on_vector(1)
         for b in range(CHUNK // P):
-            project(3 * CHUNK + b * P, [quantise(last[:, b * P:(b + 1) * P, :], "last%d" % b)], (3, 0)[b])
+            project(3 * CHUNK + b * P, [quantise(last[:, b * P:(b + 1) * P, :], "last%d" % b)], (5, 0)[b])

@@ -1,7 +1,6 @@
 from contextlib import ExitStack
 
 import concourse.mybir as mybir
-from concourse.masks import make_identity
 
 K, T, H, N, J, U = 1024, 1024, 512, 128, 512, 2048
 FLOPS = 2 * (K * H * T + J * H * U + H * N * T)
@@ -14,6 +13,7 @@ U16 = mybir.dt.uint16
 U8 = mybir.dt.uint8
 FP8X4 = mybir.dt.float8_e4m3fn_x4
 FP4X4 = mybir.dt.float4_e2m1fn_x4
+COPY = mybir.ActivationFunctionType.Copy
 SILU = mybir.ActivationFunctionType.Silu
 MULT = mybir.AluOpType.mult
 ADD = mybir.AluOpType.add
@@ -47,14 +47,15 @@ def tile_picked_wdime_none_l_kernel(
         x_plane = held([P, K // PASS, T], U8, "x_plane")
         w3_raw = held([P, PACK, H], F32, "w3_raw")
         w2_raw = held([P, PACK, N], F32, "w2_raw")
-        a_raw = {(c, d): held([P, PACK, CHUNK], F32, "a_raw%d_%d" % (c, d)) for c in range(CHUNKS) for d in range(LISTS)}
         lists = [keep.tile([P, T // PER_COLUMN], U16, name="list%d" % d) for d in range(LISTS)]
+        a_raw = {}
 
         def load_rows(tile, rows):
             nc.sync.dma_start(out=tile[:], in_=rows.rearrange("(p j) n -> p j n", j=PACK))
 
-        def load_a(c, d):
-            load_rows(a_raw[(c, d)], aT[:, d * T + c * CHUNK:d * T + (c + 1) * CHUNK])
+        def load_a(d, v0, width):
+            a_raw[(d, v0)] = held([P, PACK, width], F32, "a_raw%d_%d" % (d, v0))
+            load_rows(a_raw[(d, v0)], aT[:, d * T + v0:d * T + v0 + width])
 
         def load_w1(g):
             load_rows(w1_raw[g], w1[g * PASS:(g + 1) * PASS, :])
@@ -67,8 +68,6 @@ def tile_picked_wdime_none_l_kernel(
         warm_out = held([P, 1], F32, "warm_out")
         nc.vector.memset(warm_in[:], 0.0)
         nc.scalar.activation(warm_out[:], warm_in[:], SILU)
-        identity = held([P, P], F32, "identity")
-        make_identity(nc, identity[:])
 
         load_w1(0)
         scale_rows = x_scales.rearrange("g (quad r) n -> r quad g n", r=4)
@@ -79,18 +78,17 @@ def tile_picked_wdime_none_l_kernel(
         load_x(1)
         nc.sync.dma_start(lists[0][:], pos1)
         nc.sync.dma_start(lists[1][:], pos2)
-        load_a(0, 0)
+        load_a(0, 0, CHUNK)
         load_rows(w3_raw, w3)
-        load_a(0, 1)
-        for d in range(LISTS):
-            load_a(1, d)
-        for c in (2, 3):
-            load_a(c, 0)
+        load_a(0, CHUNK, CHUNK)
+        load_a(1, 0, BANK)
+        load_a(0, BANK, BANK)
+        load_a(1, BANK, CHUNK)
         w2_rows = w2.rearrange("(q t r) n -> r q t n", t=PACK, r=4)
         for r in range(4):
             nc.sync.dma_start(out=w2_raw[r:P:4, :, :], in_=w2_rows[r])
-        for c in (2, 3):
-            load_a(c, 1)
+        load_a(1, BANK + CHUNK, CHUNK)
+
 
         copy = {"vector": nc.vector.tensor_copy, "scalar": nc.scalar.copy}
 
@@ -106,11 +104,14 @@ def tile_picked_wdime_none_l_kernel(
                 in_=raw[:].rearrange("p j (c e) -> p c j e", e=2),
             )
 
+        def quantise_into(codes, plane, grouped):
+            nc.vector.quantize_mx(out=codes.bitcast(FP8X4), scales=plane, in_=grouped.rearrange("p w j -> p (w j)"))
+
         def quantise(grouped, name):
             width = grouped.shape[1]
             codes = held([P, width], U32, name + "_codes")
             plane = held([P, width], U8, name + "_plane")
-            nc.vector.quantize_mx(out=codes[:].bitcast(FP8X4), scales=plane[:], in_=grouped.rearrange("p w j -> p (w j)"))
+            quantise_into(codes[:], plane[:], grouped)
             return codes, plane
 
         def parts(operand, width):
@@ -129,128 +130,67 @@ def tile_picked_wdime_none_l_kernel(
             )
 
         a_bf = {}
-        a_q = {}
+        a_codes = [held([P, T], U32, "a_codes%d" % d) for d in range(LISTS)]
+        a_plane = [held([P, T], U8, "a_plane%d" % d) for d in range(LISTS)]
 
-        def round_piece(engine, c, d, takes_over=None):
-            a_bf[(c, d)] = held([P, CHUNK, PACK], BF16, "a%d_%d_bf" % (c, d), takes_over)
-            round_columns(engine, a_raw[(c, d)], a_bf[(c, d)][:])
+        def round_piece(engine, d, v0, takes_over=None):
+            width = a_raw[(d, v0)].shape[2]
+            a_bf[(d, v0)] = held([P, width, PACK], BF16, "a%d_%d_bf" % (d, v0), takes_over)
+            round_columns(engine, a_raw[(d, v0)], a_bf[(d, v0)][:])
 
-        def quantise_piece(c, d):
-            a_q[(c, d)] = parts(quantise(a_bf[(c, d)][:], "a%d_%d" % (c, d)), CHUNK)[0]
-
-        def round_beside(c, d, takes_over=None):
-            if c == 2:
-                a_bf[d] = held([P, 2 * CHUNK, PACK], BF16, "a_late%d_bf" % d, takes_over)
-            round_columns("scalar", a_raw[(c, d)], a_bf[d][:, (c - 2) * CHUNK:(c - 1) * CHUNK, :])
-
-        def quantise_late(d):
-            both = quantise(a_bf[d][:], "a_late%d" % d)
-            a_q[d] = parts(both, 2 * CHUNK)[0]
-            a_q[(2, d)], a_q[(3, d)] = parts(both, CHUNK)
+        def quantise_piece(d, v0):
+            width = a_bf[(d, v0)].shape[1]
+            quantise_into(a_codes[d][:, v0:v0 + width], a_plane[d][:, v0:v0 + width], a_bf[(d, v0)][:])
 
         h = [held([P, T], F32, "h%d" % t) for t in range(PACK)]
         h_banks = {}
         w3_q = []
         f = {}
-        f_banks = {}
+        picked = {}
         terms = {}
 
         def activate(t):
             for half in range(2):
                 nc.scalar.activation(h[t][:, half * BANK:(half + 1) * BANK], h_banks[t][half][:], SILU)
 
-        def multiply_filters(c, d, t0, role, tiles=2):
-            f_banks[(c, d, t0)] = new_bank(role)
-            for e in range(tiles):
-                multiply(f_banks[(c, d, t0)][:, e * CHUNK:(e + 1) * CHUNK], w3_q[t0 + e], a_q[(c, d)])
-
-        def copy_filters(c, d, t0, tiles=2, takes_over=None):
-            made = held([P, tiles, CHUNK], F32, "f%d_%d_%d" % (c, d, t0), takes_over)
-            for e in range(tiles):
-                f[(c, d, t0 + e)] = made[:, e, :]
-            nc.scalar.copy(out=made[:].rearrange("p e n -> p (e n)"), in_=f_banks[(c, d, t0)][:, 0:tiles * CHUNK])
-
-        def filters(c, d, t0, role, tiles=2):
-            multiply_filters(c, d, t0, role, tiles)
-            copy_filters(c, d, t0, tiles)
-
-        def all_filters(c, d, roles):
-            for u in range(2):
-                filters(c, d, 2 * u, roles[u])
-
-        def wide_filter(t, role):
+        def filters(d, v0, width, t0, role):
             bank = new_bank(role)
-            multiply(bank[:], w3_q[t], a_q[0])
-            f[t] = held([P, 2 * CHUNK], F32, "f_wide%d" % t)
-            nc.scalar.copy(out=f[t][:], in_=bank[:])
+            for e in range(BANK // width):
+                f[(d, v0, t0 + e)] = bank[:, e * width:(e + 1) * width]
+                multiply(f[(d, v0, t0 + e)], w3_q[t0 + e], (a_codes[d][:, v0:v0 + width], a_plane[d][:, v0:v0 + width]))
 
-        def wide_gathers(tiles):
-            for t in tiles:
-                nc.vector.tensor_tensor(wide[:, t, :], h[t][:].indirect(lists[0][:, 2 * CHUNK // PER_COLUMN:]), f[t][:], MULT)
+        def gather(engine, d, v0, width, t, into=None):
+            picked[(d, v0, t)] = held([P, width], F32, "picked%d_%d_%d" % (d, v0, t))[:] if into is None else into
+            window = h[t][:].indirect(lists[d][:, v0 // PER_COLUMN:(v0 + width) // PER_COLUMN])
+            if engine == "vector":
+                nc.vector.tensor_copy(out=picked[(d, v0, t)], in_=window)
+            else:
+                nc.scalar.activation(picked[(d, v0, t)], window, COPY)
 
-        wide = held([P, PACK, 2 * CHUNK], F32, "wide")
-        terms[(2, 0)] = wide[:, :, 0:CHUNK]
-        terms[(3, 0)] = wide[:, :, CHUNK:2 * CHUNK]
+        def weigh(d, v0, width, t, takes_over=None):
+            if (d, v0) not in terms:
+                terms[(d, v0)] = held([P, PACK, width], F32, "term%d_%d" % (d, v0), takes_over)
+            nc.vector.tensor_tensor(terms[(d, v0)][:, t, :], f[(d, v0, t)], picked[(d, v0, t)], MULT)
 
-        def offsets(c, d):
-            return lists[d][:, c * CHUNK // PER_COLUMN:(c + 1) * CHUNK // PER_COLUMN]
-
-        def gathers(c, d, tiles=range(PACK)):
-            if (c, d) not in terms:
-                terms[(c, d)] = held([P, PACK, CHUNK], F32, "term%d_%d" % (c, d))
-            for t in tiles:
-                nc.vector.tensor_tensor(terms[(c, d)][:, t, :], h[t][:].indirect(offsets(c, d)), f[(c, d, t)], MULT)
-
-        sums = {}
-        rows = {}
-        turned = {}
-
-        def add_on_tensor(c, roles):
-            for u in range(2):
-                sums[(c, u)] = new_bank(roles[u])
-                for e in range(2):
-                    for b in range(CHUNK // P):
-                        at = (2 * b + e) * P
-                        for d in range(LISTS):
-                            nc.tensor.matmul(
-                                sums[(c, u)][:, at:at + P],
-                                lhsT=terms[(c, d)][:, 2 * u + e, b * P:(b + 1) * P],
-                                rhs=identity[:],
-                                start=(d == 0),
-                                stop=(d == LISTS - 1),
-                                is_transpose=True,
-                            )
-
-        def round_sum(c, u):
-            rows[(c, u)] = held([P, 2, P, 2], BF16, "row%d_%d" % (c, u))
-            nc.scalar.copy(out=rows[(c, u)][:], in_=sums[(c, u)][:].rearrange("v (b e p) -> v b p e", b=2, e=2))
-
-        def turn_back(c, role):
-            turned[c] = new_bank(role)
-            for u in range(2):
-                pairs = rows[(c, u)][:].rearrange("v b p e -> v (b p e)").bitcast(F32)
-                for b in range(CHUNK // P):
-                    at = (2 * b + u) * P
-                    nc.tensor.transpose(turned[c][:, at:at + P], pairs[:, b * P:(b + 1) * P], identity[:])
-
-        def lay_pairs(c, grouped):
-            nc.scalar.copy(
-                out=grouped.rearrange("p v t -> p (v t)").bitcast(F32).rearrange("p (b v u) -> p b v u", b=2, u=2),
-                in_=turned[c][:].rearrange("p (b u v) -> p b v u", b=2, u=2),
+        def add(z, first, second):
+            nc.vector.tensor_tensor(
+                z.rearrange("p (c e) t -> p c t e", e=2),
+                first.rearrange("p t (c e) -> p c t e", e=2),
+                second.rearrange("p t (c e) -> p c t e", e=2),
+                ADD,
             )
 
-        def project(v0, z_qs, role, engine="scalar"):
-            bank = new_bank(role)
-            width = 0
-            for z_q in z_qs:
-                columns = z_q[0].shape[1]
-                multiply(bank[:, width:width + columns], parts(w2_q, N)[0], parts(z_q, columns)[0])
-                width = width + columns
-            result = held([P, width], F32, "result%d" % v0)
-            copy[engine](out=result[:], in_=bank[:, 0:width])
-            nc.sync.dma_start(out=out[:, v0:v0 + width], in_=result[:])
+        banks = {}
 
-        picked = held([P, CHUNK], F32, "picked")
+        def project(v0, z_q, role):
+            banks[v0] = new_bank(role)
+            width = z_q[0].shape[1]
+            multiply(banks[v0][:, 0:width], parts(w2_q, N)[0], parts(z_q, width)[0])
+
+        def store(v0, width):
+            result = held([P, width], F32, "result%d" % v0)
+            nc.scalar.copy(out=result[:], in_=banks[v0][:, 0:width])
+            nc.sync.dma_start(out=out[:, v0:v0 + width], in_=result[:])
 
         low = held([P, 2 * P, PACK], BF16, "w1_0a_bf")
         round_weights("vector", w1_raw[0], 0, 2, low[:])
@@ -282,83 +222,75 @@ def tile_picked_wdime_none_l_kernel(
 
         round_piece("vector", 0, 0)
         quantise_piece(0, 0)
-        for t in range(PACK - 1):
+        for t in range(PACK):
             activate(t)
-        nc.vector.tensor_copy(out=picked[:], in_=h[0][:].indirect(offsets(0, 0)))
+        gather("vector", 0, 0, BANK, 0)
+        w3_bf = [held([P, 2 * P, PACK], BF16, "w3_%d_bf" % u) for u in range(2)]
         for u in range(2):
-            w3_bf = held([P, 2 * P, PACK], BF16, "w3_%d_bf" % u)
-            round_weights("vector", w3_raw, 2 * u, 2, w3_bf[:])
-            w3_q.extend(parts(quantise(w3_bf[:], "w3_%d" % u), P))
-        bank = new_bank(0)
-        multiply(bank[:, 0:CHUNK], w3_q[0], a_q[(0, 0)])
-        terms[(0, 0)] = held([P, PACK, CHUNK], F32, "term0_0")
-        nc.vector.tensor_tensor(terms[(0, 0)][:, 0, :], bank[:, 0:CHUNK], picked[:], MULT)
-        filters(0, 0, 1, 1, tiles=1)
-        activate(PACK - 1)
-        filters(0, 0, 2, 2)
-        round_piece("vector", 0, 1, takes_over="w3_0_bf")
-        quantise_piece(0, 1)
-        round_piece("scalar", 1, 0, takes_over="a0_0_codes")
-        gathers(0, 0, range(1, PACK))
+            round_weights("vector", w3_raw, 2 * u, 2, w3_bf[u][:])
+        for u in range(2):
+            w3_q.extend(parts(quantise(w3_bf[u][:], "w3_%d" % u), P))
+        round_piece("vector", 0, CHUNK)
+        quantise_piece(0, CHUNK)
+        for t in range(1, PACK):
+            gather("scalar", 0, 0, BANK, t)
+        for t in range(PACK):
+            gather("scalar", 1, 0, BANK, t)
+        for t in range(PACK):
+            filters(0, 0, BANK, t, t)
+        round_piece("vector", 1, 0)
+        weigh(0, 0, BANK, 0, "w1_raw0")
         quantise_piece(1, 0)
-        all_filters(0, 1, (3, 4))
-        round_piece("scalar", 1, 1, takes_over="a0_1_codes")
-        gathers(0, 1)
-        quantise_piece(1, 1)
-        all_filters(1, 0, (5, 6))
-        add_on_tensor(0, (3, 4))
-        round_beside(2, 0, takes_over="a1_0_codes")
-        round_beside(3, 0)
-        gathers(1, 0)
-        quantise_late(0)
-        all_filters(1, 1, (7, 0))
-        round_beside(2, 1, takes_over="a1_1_codes")
-        gathers(1, 1)
-        wide_filter(0, 1)
-        wide_filter(1, 2)
-        round_beside(3, 1)
-        wide_gathers((0, 1))
-        quantise_late(1)
-        wide_filter(2, 5)
-        wide_filter(3, 6)
-        add_on_tensor(1, (7, 0))
-        round_sum(0, 0)
-        round_sum(0, 1)
-        w2_bf = held([P, N, PACK], BF16, "w2_bf", takes_over="f_wide0")
+        for t in range(PACK):
+            filters(1, 0, BANK, t, PACK + t)
+        for t in range(1, PACK):
+            weigh(0, 0, BANK, t)
+        round_piece("vector", 0, BANK)
+        weigh(1, 0, BANK, 0, "w1_raw1")
+        quantise_piece(0, BANK)
+        for t in range(PACK):
+            filters(0, BANK, BANK, t, t)
+        for t in range(1, PACK):
+            weigh(1, 0, BANK, t)
+        w2_bf = held([P, N, PACK], BF16, "w2_bf")
         round_columns("scalar", w2_raw, w2_bf[:])
-        wide_gathers((2, 3))
-        all_filters(2, 1, (1, 2))
-        filters(3, 1, 0, 5)
-        multiply_filters(3, 1, 2, 6)
-        turn_back(0, 4)
+        round_piece("scalar", 1, BANK + CHUNK)
+        late = held([P, 2 * PACK * BANK], F32, "late", "a_raw1_768")
+        late0 = late[:, 0:PACK * BANK]
+        for t in range(PACK):
+            gather("scalar", 0, BANK, BANK, t, late0[:, t * BANK:(t + 1) * BANK])
+        late1 = late[:, PACK * BANK:]
+        for c in range(2):
+            for t in range(PACK):
+                at = (c * PACK + t) * CHUNK
+                gather("scalar", 1, BANK + c * CHUNK, CHUNK, t, late1[:, at:at + CHUNK])
+        z0 = held([P, BANK, PACK], BF16, "z0")
+        add(z0[:], terms[(0, 0)][:], terms[(1, 0)][:])
+        round_piece("vector", 1, BANK)
         w2_q = quantise(w2_bf[:], "w2")
-        gathers(2, 1)
-        add_on_tensor(2, (1, 2))
-        z = [held([P, CHUNK, PACK], BF16, "z%d" % c) for c in range(CHUNKS - 1)]
-        round_sum(1, 0)
-        round_sum(1, 1)
-        turn_back(1, 3)
-        lay_pairs(0, z[0][:])
-        copy_filters(3, 1, 2, takes_over="row0_1")
-        round_sum(2, 0)
-        round_sum(2, 1)
-        turn_back(2, 7)
-        lay_pairs(1, z[1][:])
-        lay_pairs(2, z[2][:])
-        gathers(3, 1, (0, 1))
-        project(0, [quantise(z[0][:], "z0")], 2)
-        gathers(3, 1, (2, 3))
-        project(CHUNK, [quantise(z[1][:], "z1")], 4)
-        last = held([P, CHUNK, PACK], BF16, "last", takes_over="z0_codes")
-        def add_on_vector(b):
-            nc.vector.tensor_tensor(
-                last[:, b * P:(b + 1) * P, :].rearrange("p (c e) t -> p c t e", e=2),
-                terms[(3, 0)][:, :, b * P:(b + 1) * P].rearrange("p t (c e) -> p c t e", e=2),
-                terms[(3, 1)][:, :, b * P:(b + 1) * P].rearrange("p t (c e) -> p c t e", e=2),
-                ADD,
-            )
-        add_on_vector(0)
-        project(2 * CHUNK, [quantise(z[2][:], "z2")], 6)
-        add_on_vector(1)
-        for b in range(CHUNK // P):
-            project(3 * CHUNK + b * P, [quantise(last[:, b * P:(b + 1) * P, :], "last%d" % b)], (5, 0)[b])
+        project(0, quantise(z0[:], "z0"), 4)
+        quantise_piece(1, BANK)
+        quantise_piece(1, BANK + CHUNK)
+        for u in range(2):
+            filters(1, BANK, CHUNK, 2 * u, 5 + u)
+        for t in range(PACK):
+            weigh(0, BANK, BANK, t, "w3_raw")
+        for u in range(2):
+            filters(1, BANK + CHUNK, CHUNK, 2 * u, (7, 0)[u])
+        for t in range(PACK):
+            weigh(1, BANK, CHUNK, t)
+        z2 = held([P, CHUNK, PACK], BF16, "z2")
+        add(z2[:], terms[(0, BANK)][:, :, 0:CHUNK], terms[(1, BANK)][:])
+        for t in range(2):
+            weigh(1, BANK + CHUNK, CHUNK, t)
+        project(BANK, quantise(z2[:], "z2"), 1)
+        for t in range(2, PACK):
+            weigh(1, BANK + CHUNK, CHUNK, t)
+        store(0, BANK)
+        store(BANK, CHUNK)
+        last = held([P, CHUNK, PACK], BF16, "last")
+        for b in range(2):
+            add(last[:, b * P:(b + 1) * P, :], terms[(0, BANK)][:, :, CHUNK + b * P:CHUNK + (b + 1) * P], terms[(1, BANK + CHUNK)][:, :, b * P:(b + 1) * P])
+        for b in range(2):
+            project(BANK + CHUNK + b * P, quantise(last[:, b * P:(b + 1) * P, :], "last%d" % b), 2 + b)
+            store(BANK + CHUNK + b * P, P)

@@ -80,14 +80,14 @@ def tile_picked_wdime_none_l_kernel(
         nc.sync.dma_start(lists[1][:], pos2)
         load_a(0, 0, CHUNK)
         load_rows(w3_raw, w3)
-        load_a(0, CHUNK, CHUNK)
         load_a(1, 0, BANK)
+        load_a(0, CHUNK, CHUNK)
         load_a(0, BANK, BANK)
-        load_a(1, BANK, CHUNK)
+        load_a(1, BANK + CHUNK, CHUNK)
         w2_rows = w2.rearrange("(q t r) n -> r q t n", t=PACK, r=4)
         for r in range(4):
             nc.sync.dma_start(out=w2_raw[r:P:4, :, :], in_=w2_rows[r])
-        load_a(1, BANK + CHUNK, CHUNK)
+        load_a(1, BANK, CHUNK)
 
 
         copy = {"vector": nc.vector.tensor_copy, "scalar": nc.scalar.copy}
@@ -104,12 +104,19 @@ def tile_picked_wdime_none_l_kernel(
                 in_=raw[:].rearrange("p j (c e) -> p c j e", e=2),
             )
 
+        def round_on_gpsimd(raw, grouped):
+            nc.gpsimd.tensor_scalar(
+                grouped.rearrange("p (c e) j -> p c j e", e=2),
+                raw[:].rearrange("p j (c e) -> p c j e", e=2),
+                1.0, 0.0, MULT, ADD,
+            )
+
         def quantise_into(codes, plane, grouped):
             nc.vector.quantize_mx(out=codes.bitcast(FP8X4), scales=plane, in_=grouped.rearrange("p w j -> p (w j)"))
 
-        def quantise(grouped, name):
+        def quantise(grouped, name, takes_over=None):
             width = grouped.shape[1]
-            codes = held([P, width], U32, name + "_codes")
+            codes = held([P, width], U32, name + "_codes", takes_over)
             plane = held([P, width], U8, name + "_plane")
             quantise_into(codes[:], plane[:], grouped)
             return codes, plane
@@ -130,6 +137,7 @@ def tile_picked_wdime_none_l_kernel(
             )
 
         a_bf = {}
+        a_q = {}
         a_codes = [held([P, T], U32, "a_codes%d" % d) for d in range(LISTS)]
         a_plane = [held([P, T], U8, "a_plane%d" % d) for d in range(LISTS)]
 
@@ -146,37 +154,42 @@ def tile_picked_wdime_none_l_kernel(
         h_banks = {}
         w3_q = []
         f = {}
-        picked = {}
+        picked = [held([P, LISTS * T], F32, "picked%d" % t) for t in range(PACK)]
         terms = {}
 
         def activate(t):
             for half in range(2):
                 nc.scalar.activation(h[t][:, half * BANK:(half + 1) * BANK], h_banks[t][half][:], SILU)
 
-        def filters(d, v0, width, t0, role):
-            bank = new_bank(role)
-            for e in range(BANK // width):
-                f[(d, v0, t0 + e)] = bank[:, e * width:(e + 1) * width]
-                multiply(f[(d, v0, t0 + e)], w3_q[t0 + e], (a_codes[d][:, v0:v0 + width], a_plane[d][:, v0:v0 + width]))
+        def filters(c, t, role):
+            f[(c, t)] = new_bank(role)
+            for e in range(LISTS):
+                d = 1 - e if c == 0 else e
+                v0 = c * CHUNK
+                multiply(f[(c, t)][:, e * CHUNK:(e + 1) * CHUNK], w3_q[t], a_q.get((d, v0)) or (a_codes[d][:, v0:v0 + CHUNK], a_plane[d][:, v0:v0 + CHUNK]))
 
-        def gather(engine, d, v0, width, t, into=None):
-            picked[(d, v0, t)] = held([P, width], F32, "picked%d_%d_%d" % (d, v0, t))[:] if into is None else into
+        def gather(engine, d, v0, width, t, into):
             window = h[t][:].indirect(lists[d][:, v0 // PER_COLUMN:(v0 + width) // PER_COLUMN])
             if engine == "vector":
-                nc.vector.tensor_copy(out=picked[(d, v0, t)], in_=window)
+                nc.vector.tensor_copy(out=into, in_=window)
             else:
-                nc.scalar.activation(picked[(d, v0, t)], window, COPY)
+                nc.scalar.activation(into, window, COPY)
 
-        def weigh(d, v0, width, t, takes_over=None):
-            if (d, v0) not in terms:
-                terms[(d, v0)] = held([P, PACK, width], F32, "term%d_%d" % (d, v0), takes_over)
-            nc.vector.tensor_tensor(terms[(d, v0)][:, t, :], f[(d, v0, t)], picked[(d, v0, t)], MULT)
-
-        def add(z, first, second):
+        def weigh(c, t, takes_over=None):
+            if c not in terms:
+                terms[c] = held([P, LISTS, PACK, CHUNK], F32, "term%d" % c, takes_over)[:]
             nc.vector.tensor_tensor(
+                terms[c][:, :, t, :],
+                f[(c, t)][:].rearrange("p (e v) -> p e v", e=LISTS),
+                picked[t][:, c * BANK:(c + 1) * BANK].rearrange("p (e v) -> p e v", e=LISTS),
+                MULT,
+            )
+
+        def add(engine, z, c, v0, width):
+            engine.tensor_tensor(
                 z.rearrange("p (c e) t -> p c t e", e=2),
-                first.rearrange("p t (c e) -> p c t e", e=2),
-                second.rearrange("p t (c e) -> p c t e", e=2),
+                terms[c][:, 0, :, v0:v0 + width].rearrange("p t (c e) -> p c t e", e=2),
+                terms[c][:, 1, :, v0:v0 + width].rearrange("p t (c e) -> p c t e", e=2),
                 ADD,
             )
 
@@ -185,7 +198,7 @@ def tile_picked_wdime_none_l_kernel(
         def project(v0, z_q, role):
             banks[v0] = new_bank(role)
             width = z_q[0].shape[1]
-            multiply(banks[v0][:, 0:width], parts(w2_q, N)[0], parts(z_q, width)[0])
+            multiply(banks[v0][:, 0:width], w2_q, z_q)
 
         def store(v0, width):
             result = held([P, width], F32, "result%d" % v0)
@@ -224,73 +237,76 @@ def tile_picked_wdime_none_l_kernel(
         quantise_piece(0, 0)
         for t in range(PACK):
             activate(t)
-        gather("vector", 0, 0, BANK, 0)
+        gather("vector", 0, 0, BANK, 0, picked[0][:, CHUNK:CHUNK + BANK])
         w3_bf = [held([P, 2 * P, PACK], BF16, "w3_%d_bf" % u) for u in range(2)]
         for u in range(2):
             round_weights("vector", w3_raw, 2 * u, 2, w3_bf[u][:])
         for u in range(2):
             w3_q.extend(parts(quantise(w3_bf[u][:], "w3_%d" % u), P))
-        round_piece("vector", 0, CHUNK)
-        quantise_piece(0, CHUNK)
-        for t in range(1, PACK):
-            gather("scalar", 0, 0, BANK, t)
         for t in range(PACK):
-            gather("scalar", 1, 0, BANK, t)
+            if t > 0:
+                gather("scalar", 0, 0, BANK, t, picked[t][:, CHUNK:CHUNK + BANK])
+            gather("scalar", 1, 0, CHUNK, t, picked[t][:, 0:CHUNK])
         for t in range(PACK):
-            filters(0, 0, BANK, t, t)
+            gather("scalar", 1, CHUNK, CHUNK, t, picked[t][:, CHUNK + BANK:2 * BANK])
+        for c in (2, 3):
+            for t in range(PACK):
+                for d in range(LISTS):
+                    gather("scalar", d, c * CHUNK, CHUNK, t, picked[t][:, c * BANK + d * CHUNK:c * BANK + (d + 1) * CHUNK])
         round_piece("vector", 1, 0)
-        weigh(0, 0, BANK, 0, "w1_raw0")
+        round_piece("vector", 0, CHUNK)
         quantise_piece(1, 0)
-        for t in range(PACK):
-            filters(1, 0, BANK, t, PACK + t)
-        for t in range(1, PACK):
-            weigh(0, 0, BANK, t)
-        round_piece("vector", 0, BANK)
-        weigh(1, 0, BANK, 0, "w1_raw1")
-        quantise_piece(0, BANK)
-        for t in range(PACK):
-            filters(0, BANK, BANK, t, t)
-        for t in range(1, PACK):
-            weigh(1, 0, BANK, t)
-        w2_bf = held([P, N, PACK], BF16, "w2_bf")
-        round_columns("scalar", w2_raw, w2_bf[:])
-        round_piece("scalar", 1, BANK + CHUNK)
-        late = held([P, 2 * PACK * BANK], F32, "late", "a_raw1_768")
-        late0 = late[:, 0:PACK * BANK]
-        for t in range(PACK):
-            gather("scalar", 0, BANK, BANK, t, late0[:, t * BANK:(t + 1) * BANK])
-        late1 = late[:, PACK * BANK:]
+        quantise_piece(0, CHUNK)
         for c in range(2):
             for t in range(PACK):
-                at = (c * PACK + t) * CHUNK
-                gather("scalar", 1, BANK + c * CHUNK, CHUNK, t, late1[:, at:at + CHUNK])
-        z0 = held([P, BANK, PACK], BF16, "z0")
-        add(z0[:], terms[(0, 0)][:], terms[(1, 0)][:])
-        round_piece("vector", 1, BANK)
-        w2_q = quantise(w2_bf[:], "w2")
-        project(0, quantise(z0[:], "z0"), 4)
-        quantise_piece(1, BANK)
-        quantise_piece(1, BANK + CHUNK)
-        for u in range(2):
-            filters(1, BANK, CHUNK, 2 * u, 5 + u)
+                filters(c, t, PACK * c + t)
+        round_piece("vector", 0, BANK)
+        early = held([P, 2, LISTS, PACK, CHUNK], F32, "early", "a_raw0_512")
+        terms[0] = early[:, 0]
+        terms[1] = early[:, 1]
+        weigh(0, 0)
+        quantise_piece(0, BANK)
+        late_bf = held([P, CHUNK + N, PACK], BF16, "late_bf", "a0_512_bf")
+        round_on_gpsimd(a_raw[(1, BANK + CHUNK)], late_bf[:, 0:CHUNK, :])
+        round_on_gpsimd(w2_raw, late_bf[:, CHUNK:, :])
+        for t in range(1, PACK):
+            weigh(0, t)
+        mixed_bf = held([P, 2 * CHUNK, PACK], BF16, "mixed_bf")
+        add(nc.gpsimd, mixed_bf[:, 0:CHUNK, :], 0, 0, CHUNK)
         for t in range(PACK):
-            weigh(0, BANK, BANK, t, "w3_raw")
-        for u in range(2):
-            filters(1, BANK + CHUNK, CHUNK, 2 * u, (7, 0)[u])
+            weigh(1, t)
+        round_columns("vector", a_raw[(1, BANK)], mixed_bf[:, CHUNK:, :])
+        z0_q, a_q[(1, BANK)] = parts(quantise(mixed_bf[:], "mixed"), CHUNK)
         for t in range(PACK):
-            weigh(1, BANK, CHUNK, t)
-        z2 = held([P, CHUNK, PACK], BF16, "z2")
-        add(z2[:], terms[(0, BANK)][:, :, 0:CHUNK], terms[(1, BANK)][:])
-        for t in range(2):
-            weigh(1, BANK + CHUNK, CHUNK, t)
-        project(BANK, quantise(z2[:], "z2"), 1)
-        for t in range(2, PACK):
-            weigh(1, BANK + CHUNK, CHUNK, t)
+            filters(2, t, t)
+        late_codes, late_plane = quantise(late_bf[:], "late", "mixed_bf")
+        a_q[(1, BANK + CHUNK)] = (late_codes[:, 0:CHUNK], late_plane[:, 0:CHUNK])
+        w2_q = (late_codes[:, CHUNK:], late_plane[:, CHUNK:])
+        for t in range(PACK):
+            filters(3, t, PACK + t)
+        z_codes = held([P, T], U32, "z_codes")
+        z_plane = held([P, T], U8, "z_plane")
+
+        def quantise_z(z, v0, width):
+            quantise_into(z_codes[:, v0:v0 + width], z_plane[:, v0:v0 + width], z)
+
+        for c in (1, 2):
+            z = held([P, CHUNK, PACK], BF16, "z%d" % c, "a0_512_bf")
+            add(nc.gpsimd, z[:], c, 0, CHUNK)
+            for t in range(PACK):
+                weigh(c + 1, t, ("w1_raw0", "a_raw0_512")[c - 1])
+            quantise_z(z[:], c * CHUNK, CHUNK)
+        banks[0] = new_bank(0)
+        multiply(banks[0][:, 0:CHUNK], w2_q, z0_q)
+        multiply(banks[0][:, CHUNK:], w2_q, (z_codes[:, CHUNK:BANK], z_plane[:, CHUNK:BANK]))
+        project(BANK, (z_codes[:, BANK:BANK + CHUNK], z_plane[:, BANK:BANK + CHUNK]), 1)
         store(0, BANK)
         store(BANK, CHUNK)
         last = held([P, CHUNK, PACK], BF16, "last")
         for b in range(2):
-            add(last[:, b * P:(b + 1) * P, :], terms[(0, BANK)][:, :, CHUNK + b * P:CHUNK + (b + 1) * P], terms[(1, BANK + CHUNK)][:, :, b * P:(b + 1) * P])
+            add(nc.vector, last[:, b * P:(b + 1) * P, :], 3, b * P, P)
         for b in range(2):
-            project(BANK + CHUNK + b * P, quantise(last[:, b * P:(b + 1) * P, :], "last%d" % b), 2 + b)
-            store(BANK + CHUNK + b * P, P)
+            v0 = BANK + CHUNK + b * P
+            quantise_z(last[:, b * P:(b + 1) * P, :], v0, P)
+            project(v0, (z_codes[:, v0:v0 + P], z_plane[:, v0:v0 + P]), 2 + b)
+            store(v0, P)

@@ -106,8 +106,8 @@ def tile_picked_wdime_none_l_kernel(
 
         def round_on_gpsimd(raw, grouped):
             nc.gpsimd.tensor_scalar(
-                grouped.rearrange("p (c e) j -> p c j e", e=2),
-                raw[:].rearrange("p j (c e) -> p c j e", e=2),
+                grouped,
+                raw[:].rearrange("p j c -> p c j"),
                 1.0, 0.0, MULT, ADD,
             )
 
@@ -154,7 +154,12 @@ def tile_picked_wdime_none_l_kernel(
         h_banks = {}
         w3_q = []
         f = {}
-        picked = [held([P, LISTS * T], F32, "picked%d" % t) for t in range(PACK)]
+        picked = [held([P, BANK], F32, "picked%d" % t) for t in range(PACK)]
+        wide = held([P, PACK, BANK], F32, "wide")
+        found = {(0, 0): wide[:, :, 0:CHUNK], (1, 0): wide[:, :, CHUNK:]}
+        for c, d in ((0, 1), (1, 1), (2, 0), (2, 1)):
+            found[(c, d)] = held([P, PACK, CHUNK], F32, "found%d_%d" % (c, d))[:]
+        woven = {}
         terms = {}
 
         def activate(t):
@@ -181,7 +186,7 @@ def tile_picked_wdime_none_l_kernel(
             nc.vector.tensor_tensor(
                 terms[c][:, :, t, :],
                 f[(c, t)][:].rearrange("p (e v) -> p e v", e=LISTS),
-                picked[t][:, c * BANK:(c + 1) * BANK].rearrange("p (e v) -> p e v", e=LISTS),
+                picked[t][:].rearrange("p (e v) -> p e v", e=LISTS),
                 MULT,
             )
 
@@ -191,6 +196,29 @@ def tile_picked_wdime_none_l_kernel(
                 terms[c][:, 0, :, v0:v0 + width].rearrange("p t (c e) -> p c t e", e=2),
                 terms[c][:, 1, :, v0:v0 + width].rearrange("p t (c e) -> p c t e", e=2),
                 ADD,
+            )
+
+        def add_on_gpsimd(z, c):
+            nc.gpsimd.tensor_tensor(z, woven[c][:, 0], woven[c][:, 1], ADD)
+
+        def strip_filters(c, d, b, role):
+            f[(c, d, b)] = new_bank(role)
+            v0 = c * CHUNK
+            codes, plane = a_q.get((d, v0)) or (a_codes[d][:, v0:v0 + CHUNK], a_plane[d][:, v0:v0 + CHUNK])
+            for t in range(PACK):
+                multiply(f[(c, d, b)][:, t * P:(t + 1) * P], w3_q[t], (codes[:, b * P:(b + 1) * P], plane[:, b * P:(b + 1) * P]))
+
+        def chunk_filters(c, role):
+            for d in range(LISTS):
+                for b in range(2):
+                    strip_filters(c, d, b, role + 2 * d + b)
+
+        def weave(c, d, b):
+            nc.vector.tensor_tensor(
+                woven[c][:, d, b * P:(b + 1) * P, :].rearrange("p (c e) t -> p c t e", e=2),
+                f[(c, d, b)][:].rearrange("p (t c e) -> p c t e", t=PACK, e=2),
+                found[(c, d)][:, :, b * P:(b + 1) * P].rearrange("p t (c e) -> p c t e", e=2),
+                MULT,
             )
 
         banks = {}
@@ -237,48 +265,45 @@ def tile_picked_wdime_none_l_kernel(
         quantise_piece(0, 0)
         for t in range(PACK):
             activate(t)
-        gather("vector", 0, 0, BANK, 0, picked[0][:, CHUNK:CHUNK + BANK])
+        gather("vector", 0, 0, BANK, 0, wide[:, 0, :])
         w3_bf = [held([P, 2 * P, PACK], BF16, "w3_%d_bf" % u) for u in range(2)]
         for u in range(2):
             round_weights("vector", w3_raw, 2 * u, 2, w3_bf[u][:])
         for u in range(2):
             w3_q.extend(parts(quantise(w3_bf[u][:], "w3_%d" % u), P))
-        for t in range(PACK):
-            if t > 0:
-                gather("scalar", 0, 0, BANK, t, picked[t][:, CHUNK:CHUNK + BANK])
-            gather("scalar", 1, 0, CHUNK, t, picked[t][:, 0:CHUNK])
-        for t in range(PACK):
-            gather("scalar", 1, CHUNK, CHUNK, t, picked[t][:, CHUNK + BANK:2 * BANK])
-        for c in (2, 3):
+        for t in range(1, PACK):
+            gather("scalar", 0, 0, BANK, t, wide[:, t, :])
+        for c, d in ((0, 1), (1, 1), (2, 0), (2, 1)):
             for t in range(PACK):
-                for d in range(LISTS):
-                    gather("scalar", d, c * CHUNK, CHUNK, t, picked[t][:, c * BANK + d * CHUNK:c * BANK + (d + 1) * CHUNK])
+                gather("scalar", d, c * CHUNK, CHUNK, t, found[(c, d)][:, t, :])
+        for t in range(PACK):
+            for d in range(LISTS):
+                gather("scalar", d, 3 * CHUNK, CHUNK, t, picked[t][:, d * CHUNK:(d + 1) * CHUNK])
         round_piece("vector", 1, 0)
         round_piece("vector", 0, CHUNK)
         quantise_piece(1, 0)
         quantise_piece(0, CHUNK)
         for c in range(2):
-            for t in range(PACK):
-                filters(c, t, PACK * c + t)
+            chunk_filters(c, PACK * c)
         round_piece("vector", 0, BANK)
-        early = held([P, 2, LISTS, PACK, CHUNK], F32, "early", "a_raw0_512")
-        terms[0] = early[:, 0]
-        terms[1] = early[:, 1]
-        weigh(0, 0)
+        early = held([P, 2, LISTS, CHUNK, PACK], F32, "early", "a_raw0_512")
+        woven[0] = early[:, 0]
+        woven[1] = early[:, 1]
+        weave(0, 0, 0)
         quantise_piece(0, BANK)
         late_bf = held([P, CHUNK + N, PACK], BF16, "late_bf", "a0_512_bf")
         round_on_gpsimd(a_raw[(1, BANK + CHUNK)], late_bf[:, 0:CHUNK, :])
         round_on_gpsimd(w2_raw, late_bf[:, CHUNK:, :])
-        for t in range(1, PACK):
-            weigh(0, t)
+        for d, b in ((0, 1), (1, 0), (1, 1)):
+            weave(0, d, b)
         mixed_bf = held([P, 2 * CHUNK, PACK], BF16, "mixed_bf")
-        add(nc.gpsimd, mixed_bf[:, 0:CHUNK, :], 0, 0, CHUNK)
-        for t in range(PACK):
-            weigh(1, t)
+        add_on_gpsimd(mixed_bf[:, 0:CHUNK, :], 0)
+        for d in range(LISTS):
+            for b in range(2):
+                weave(1, d, b)
         round_columns("vector", a_raw[(1, BANK)], mixed_bf[:, CHUNK:, :])
         z0_q, a_q[(1, BANK)] = parts(quantise(mixed_bf[:], "mixed"), CHUNK)
-        for t in range(PACK):
-            filters(2, t, t)
+        chunk_filters(2, 0)
         late_codes, late_plane = quantise(late_bf[:], "late", "mixed_bf")
         a_q[(1, BANK + CHUNK)] = (late_codes[:, 0:CHUNK], late_plane[:, 0:CHUNK])
         w2_q = (late_codes[:, CHUNK:], late_plane[:, CHUNK:])
@@ -292,9 +317,15 @@ def tile_picked_wdime_none_l_kernel(
 
         for c in (1, 2):
             z = held([P, CHUNK, PACK], BF16, "z%d" % c, "a0_512_bf")
-            add(nc.gpsimd, z[:], c, 0, CHUNK)
-            for t in range(PACK):
-                weigh(c + 1, t, ("w1_raw0", "a_raw0_512")[c - 1])
+            add_on_gpsimd(z[:], c)
+            if c == 1:
+                woven[2] = held([P, LISTS, CHUNK, PACK], F32, "woven2", "w1_raw0")[:]
+                for d in range(LISTS):
+                    for b in range(2):
+                        weave(2, d, b)
+            else:
+                for t in range(PACK):
+                    weigh(3, t, "a_raw0_512")
             quantise_z(z[:], c * CHUNK, CHUNK)
         banks[0] = new_bank(0)
         multiply(banks[0][:, 0:CHUNK], w2_q, z0_q)

@@ -198,8 +198,8 @@ def tile_picked_wdime_none_l_kernel(
                 ADD,
             )
 
-        def add_on_gpsimd(z, c):
-            nc.gpsimd.tensor_tensor(z, woven[c][:, 0], woven[c][:, 1], ADD)
+        def add_on_gpsimd(z, c, width=CHUNK):
+            nc.gpsimd.tensor_tensor(z, woven[c][:, 0, 0:width, :], woven[c][:, 1, 0:width, :], ADD)
 
         def strip_filters(c, d, b, role):
             f[(c, d, b)] = new_bank(role)
@@ -266,6 +266,7 @@ def tile_picked_wdime_none_l_kernel(
         for t in range(PACK):
             activate(t)
         gather("vector", 0, 0, BANK, 0, wide[:, 0, :])
+        gather("vector", 1, 0, CHUNK, 0, found[(0, 1)][:, 0, :])
         w3_bf = [held([P, 2 * P, PACK], BF16, "w3_%d_bf" % u) for u in range(2)]
         for u in range(2):
             round_weights("vector", w3_raw, 2 * u, 2, w3_bf[u][:])
@@ -274,7 +275,7 @@ def tile_picked_wdime_none_l_kernel(
         for t in range(1, PACK):
             gather("scalar", 0, 0, BANK, t, wide[:, t, :])
         for c, d in ((0, 1), (1, 1), (2, 0), (2, 1)):
-            for t in range(PACK):
+            for t in range(1 if c == 0 else 0, PACK):
                 gather("scalar", d, c * CHUNK, CHUNK, t, found[(c, d)][:, t, :])
         for t in range(PACK):
             for d in range(LISTS):
@@ -315,24 +316,23 @@ def tile_picked_wdime_none_l_kernel(
         def quantise_z(z, v0, width):
             quantise_into(z_codes[:, v0:v0 + width], z_plane[:, v0:v0 + width], z)
 
-        for c in (1, 2):
-            z = held([P, CHUNK, PACK], BF16, "z%d" % c, "a0_512_bf")
-            add_on_gpsimd(z[:], c)
-            if c == 1:
-                woven[2] = held([P, LISTS, CHUNK, PACK], F32, "woven2", "w1_raw0")[:]
-                for d in range(LISTS):
-                    for b in range(2):
-                        weave(2, d, b)
-            else:
-                for t in range(PACK):
-                    weigh(3, t, "a_raw0_512")
-            quantise_z(z[:], c * CHUNK, CHUNK)
-        banks[0] = new_bank(0)
-        multiply(banks[0][:, 0:CHUNK], w2_q, z0_q)
-        multiply(banks[0][:, CHUNK:], w2_q, (z_codes[:, CHUNK:BANK], z_plane[:, CHUNK:BANK]))
-        project(BANK, (z_codes[:, BANK:BANK + CHUNK], z_plane[:, BANK:BANK + CHUNK]), 1)
-        store(0, BANK)
-        store(BANK, CHUNK)
+        z = held([P, 2 * CHUNK, PACK], BF16, "z12", "a0_512_bf")
+        add_on_gpsimd(z[:, 0:CHUNK, :], 1)
+        woven[2] = held([P, LISTS, CHUNK, PACK], F32, "woven2", "w1_raw0")[:]
+        for d in range(LISTS):
+            for b in range(2):
+                weave(2, d, b)
+        add_on_gpsimd(z[:, CHUNK:CHUNK + P, :], 2, P)
+        for t in range(2):
+            weigh(3, t, "w1_raw1")
+        nc.vector.tensor_tensor(z[:, CHUNK + P:, :], woven[2][:, 0, P:, :], woven[2][:, 1, P:, :], ADD)
+        weigh(3, 2)
+        quantise_z(z[:], CHUNK, 2 * CHUNK)
+        weigh(3, PACK - 1)
+        project(0, z0_q, 0)
+        project(CHUNK, (z_codes[:, CHUNK:CHUNK + BANK], z_plane[:, CHUNK:CHUNK + BANK]), 1)
+        store(0, CHUNK)
+        store(CHUNK, BANK)
         last = held([P, CHUNK, PACK], BF16, "last")
         for b in range(2):
             add(nc.vector, last[:, b * P:(b + 1) * P, :], 3, b * P, P)

@@ -23,9 +23,19 @@ PACK = 4
 PASS = P * PACK
 BANK = 512
 CHUNK = 256
-CHUNKS = T // CHUNK
+STRIP = 128
 LISTS = 2
+PAIRS = 2
 PER_COLUMN = 16
+
+UNIT = PACK * CHUNK * 4
+REACH = 512
+AT_LAST_TERMS = 0
+AT_Z12 = LISTS * UNIT
+AT_TERMS1_2 = AT_Z12 + UNIT
+AT_EARLY_TERMS = AT_TERMS1_2 + UNIT
+AT_SHARED = AT_Z12 - REACH
+AT_A0_2 = AT_TERMS1_2 + REACH // 2
 
 
 def tile_picked_wdime_none_l_kernel(
@@ -35,12 +45,16 @@ def tile_picked_wdime_none_l_kernel(
     with ExitStack() as ctx:
         keep = ctx.enter_context(tc.tile_pool(name="keep", bufs=1))
         psum = ctx.enter_context(tc.psum_pool(name="psum", bufs=1))
+        turns = ctx.enter_context(tc.tile_pool(name="turns", bufs=1))
 
         def new_bank(number):
             return psum.tile([P, BANK], F32, name="bank%d" % number, tag="bank%d" % number)
 
-        def held(shape, dtype, name, takes_over=None):
-            return keep.tile(shape, dtype, name=name, tag=takes_over or name, align_bytes=64)
+        def held(shape, dtype, name):
+            return keep.tile(shape, dtype, name=name, tag=name, align_bytes=64)
+
+        def placed(shape, dtype, name, offset):
+            return turns.tile(shape, dtype, name=name, offset=offset, align_bytes=64)
 
         w1_raw = [held([P, PACK, H], F32, "w1_raw%d" % g) for g in range(K // PASS)]
         x_codes = [held([P, 2 * T], U8, "x_codes%d" % g) for g in range(K // PASS)]
@@ -53,9 +67,9 @@ def tile_picked_wdime_none_l_kernel(
         def load_rows(tile, rows):
             nc.sync.dma_start(out=tile[:], in_=rows.rearrange("(p j) n -> p j n", j=PACK))
 
-        def load_a(d, v0, width):
-            a_raw[(d, v0)] = held([P, PACK, width], F32, "a_raw%d_%d" % (d, v0))
-            load_rows(a_raw[(d, v0)], aT[:, d * T + v0:d * T + v0 + width])
+        def load_a(d, c, chunks):
+            a_raw[(d, c)] = held([P, PACK, chunks * CHUNK], F32, "a_raw%d_%d" % (d, c))
+            load_rows(a_raw[(d, c)], aT[:, d * T + c * CHUNK:d * T + (c + chunks) * CHUNK])
 
         def load_w1(g):
             load_rows(w1_raw[g], w1[g * PASS:(g + 1) * PASS, :])
@@ -78,52 +92,38 @@ def tile_picked_wdime_none_l_kernel(
         load_x(1)
         nc.sync.dma_start(lists[0][:], pos1)
         nc.sync.dma_start(lists[1][:], pos2)
-        load_a(0, 0, CHUNK)
+        load_a(0, 0, 1)
         load_rows(w3_raw, w3)
-        load_a(1, 0, BANK)
-        load_a(0, CHUNK, CHUNK)
-        load_a(0, BANK, BANK)
-        load_a(1, BANK + CHUNK, CHUNK)
+        load_a(1, 0, 2)
+        load_a(0, 1, 1)
+        load_a(1, 2, 1)
+        load_a(0, 2, 2)
+        load_a(1, 3, 1)
         w2_rows = w2.rearrange("(q t r) n -> r q t n", t=PACK, r=4)
         for r in range(4):
             nc.sync.dma_start(out=w2_raw[r:P:4, :, :], in_=w2_rows[r])
-        load_a(1, BANK, CHUNK)
 
-
-        copy = {"vector": nc.vector.tensor_copy, "scalar": nc.scalar.copy}
-
-        def round_weights(engine, raw, t0, tiles, grouped):
-            copy[engine](
+        def round_weights(copy, raw, t0, tiles, grouped):
+            copy(
                 out=grouped.rearrange("p (t q r) j -> p t q j r", t=tiles, r=4),
                 in_=raw[:].rearrange("p j (q t r) -> p t q j r", t=PACK, r=4)[:, t0:t0 + tiles],
             )
 
-        def round_columns(engine, raw, grouped):
-            copy[engine](
+        def round_on_vector(raw, grouped):
+            nc.vector.tensor_copy(
                 out=grouped.rearrange("p (c e) j -> p c j e", e=2),
                 in_=raw[:].rearrange("p j (c e) -> p c j e", e=2),
             )
 
         def round_on_gpsimd(raw, grouped):
-            nc.gpsimd.tensor_scalar(
-                grouped,
-                raw[:].rearrange("p j c -> p c j"),
-                1.0, 0.0, MULT, ADD,
-            )
+            nc.gpsimd.tensor_scalar(grouped, raw[:].rearrange("p j c -> p c j"), 1.0, 0.0, MULT, ADD)
 
-        def quantise_into(codes, plane, grouped):
-            nc.vector.quantize_mx(out=codes.bitcast(FP8X4), scales=plane, in_=grouped.rearrange("p w j -> p (w j)"))
-
-        def quantise(grouped, name, takes_over=None):
-            width = grouped.shape[1]
-            codes = held([P, width], U32, name + "_codes", takes_over)
-            plane = held([P, width], U8, name + "_plane")
-            quantise_into(codes[:], plane[:], grouped)
-            return codes, plane
-
-        def parts(operand, width):
-            codes, plane = operand
-            return [(codes[:, at:at + width], plane[:, at:at + width]) for at in range(0, codes.shape[1], width)]
+        def quantise(grouped, name, width):
+            columns = grouped.shape[1]
+            codes = held([P, columns], U32, name + "_codes")
+            plane = held([P, columns], U8, name + "_plane")
+            nc.vector.quantize_mx(out=codes[:].bitcast(FP8X4), scales=plane[:], in_=grouped.rearrange("p w j -> p (w j)"))
+            return [(codes[:, at:at + width], plane[:, at:at + width]) for at in range(0, columns, width)]
 
         def multiply(result, stationary, moving):
             nc.tensor.matmul_mx(
@@ -138,117 +138,86 @@ def tile_picked_wdime_none_l_kernel(
 
         a_bf = {}
         a_q = {}
-        a_codes = [held([P, T], U32, "a_codes%d" % d) for d in range(LISTS)]
-        a_plane = [held([P, T], U8, "a_plane%d" % d) for d in range(LISTS)]
 
-        def round_piece(engine, d, v0, takes_over=None):
-            width = a_raw[(d, v0)].shape[2]
-            a_bf[(d, v0)] = held([P, width, PACK], BF16, "a%d_%d_bf" % (d, v0), takes_over)
-            round_columns(engine, a_raw[(d, v0)], a_bf[(d, v0)][:])
+        def round_piece(d, c):
+            a_bf[(d, c)] = held([P, a_raw[(d, c)].shape[2], PACK], BF16, "a_bf%d_%d" % (d, c))
+            round_on_vector(a_raw[(d, c)], a_bf[(d, c)][:])
 
-        def quantise_piece(d, v0):
-            width = a_bf[(d, v0)].shape[1]
-            quantise_into(a_codes[d][:, v0:v0 + width], a_plane[d][:, v0:v0 + width], a_bf[(d, v0)][:])
+        def quantise_piece(d, c):
+            for n, part in enumerate(quantise(a_bf[(d, c)][:], "a%d_%d" % (d, c), CHUNK)):
+                a_q[(d, c + n)] = part
 
         h = [held([P, T], F32, "h%d" % t) for t in range(PACK)]
-        h_banks = {}
         w3_q = []
         f = {}
-        picked = [held([P, BANK], F32, "picked%d" % t) for t in range(PACK)]
-        wide = held([P, PACK, BANK], F32, "wide")
-        found = {(0, 0): wide[:, :, 0:CHUNK], (1, 0): wide[:, :, CHUNK:]}
-        for c, d in ((0, 1), (1, 1), (2, 0), (2, 1)):
-            found[(c, d)] = held([P, PACK, CHUNK], F32, "found%d_%d" % (c, d))[:]
-        woven = {}
         terms = {}
+        wide = held([P, PACK, 2 * CHUNK], F32, "wide")
+        found = {(0, c): wide[:, :, c * CHUNK:(c + 1) * CHUNK] for c in range(2)}
+        for d, c in ((1, 0), (1, 1), (0, 2), (1, 2), (0, 3)):
+            found[(d, c)] = held([P, PACK, CHUNK], F32, "found%d_%d" % (d, c))[:]
+        found[(1, 3)] = held([P, 2, CHUNK], F32, "found1_3")[:]
+        found_strip = [held([P, 2, STRIP], F32, "found_strip%d" % b) for b in range(2)]
 
-        def activate(t):
-            for half in range(2):
-                nc.scalar.activation(h[t][:, half * BANK:(half + 1) * BANK], h_banks[t][half][:], SILU)
+        def window(d, t, v0, width):
+            return h[t][:].indirect(lists[d][:, v0 // PER_COLUMN:(v0 + width) // PER_COLUMN])
 
-        def filters(c, t, role):
-            f[(c, t)] = new_bank(role)
-            for e in range(LISTS):
-                d = 1 - e if c == 0 else e
-                v0 = c * CHUNK
-                multiply(f[(c, t)][:, e * CHUNK:(e + 1) * CHUNK], w3_q[t], a_q.get((d, v0)) or (a_codes[d][:, v0:v0 + CHUNK], a_plane[d][:, v0:v0 + CHUNK]))
+        def gather_on_scalar(d, t, v0, into):
+            nc.scalar.activation(into, window(d, t, v0, into.shape[1]), COPY)
 
-        def gather(engine, d, v0, width, t, into):
-            window = h[t][:].indirect(lists[d][:, v0 // PER_COLUMN:(v0 + width) // PER_COLUMN])
-            if engine == "vector":
-                nc.vector.tensor_copy(out=into, in_=window)
-            else:
-                nc.scalar.activation(into, window, COPY)
+        def gather_on_vector(d, t, v0, into):
+            nc.vector.tensor_copy(out=into, in_=window(d, t, v0, into.shape[1]))
 
-        def weigh(c, t, takes_over=None):
-            if c not in terms:
-                terms[c] = held([P, LISTS, PACK, CHUNK], F32, "term%d" % c, takes_over)[:]
+        def filters(d, c):
+            for u in range(PAIRS):
+                f[(d, c, u)] = new_bank(LISTS * PAIRS * (c % 2) + PAIRS * d + u)
+                for e in range(2):
+                    multiply(f[(d, c, u)][:, e * CHUNK:(e + 1) * CHUNK], w3_q[2 * u + e], a_q[(d, c)])
+
+        def weigh_values(d, c, u, v0, values):
+            width = values.shape[2]
             nc.vector.tensor_tensor(
-                terms[c][:, :, t, :],
-                f[(c, t)][:].rearrange("p (e v) -> p e v", e=LISTS),
-                picked[t][:].rearrange("p (e v) -> p e v", e=LISTS),
+                terms[(d, c)][:, u, v0:v0 + width, :],
+                f[(d, c, u)][:].rearrange("p (e v) -> p v e", e=2)[:, v0:v0 + width, :],
+                values.rearrange("p e v -> p v e"),
                 MULT,
             )
 
-        def add(engine, z, c, v0, width):
-            engine.tensor_tensor(
-                z.rearrange("p (c e) t -> p c t e", e=2),
-                terms[c][:, 0, :, v0:v0 + width].rearrange("p t (c e) -> p c t e", e=2),
-                terms[c][:, 1, :, v0:v0 + width].rearrange("p t (c e) -> p c t e", e=2),
-                ADD,
-            )
+        def weigh(d, c, u):
+            weigh_values(d, c, u, 0, found[(d, c)][:, 2 * u:2 * u + 2, :])
 
-        def add_on_gpsimd(z, c, width=CHUNK):
-            nc.gpsimd.tensor_tensor(z, woven[c][:, 0, 0:width, :], woven[c][:, 1, 0:width, :], ADD)
+        def add(engine, z, c, v0):
+            width = z.shape[1]
+            first, second = (terms[(d, c)][:, :, v0:v0 + width, :].rearrange("p u v e -> p v u e") for d in range(LISTS))
+            engine.tensor_tensor(z.rearrange("p v (u e) -> p v u e", e=2), first, second, ADD)
 
-        def strip_filters(c, d, b, role):
-            f[(c, d, b)] = new_bank(role)
-            v0 = c * CHUNK
-            codes, plane = a_q.get((d, v0)) or (a_codes[d][:, v0:v0 + CHUNK], a_plane[d][:, v0:v0 + CHUNK])
-            for t in range(PACK):
-                multiply(f[(c, d, b)][:, t * P:(t + 1) * P], w3_q[t], (codes[:, b * P:(b + 1) * P], plane[:, b * P:(b + 1) * P]))
+        def project(z_q, number):
+            bank = new_bank(number)[:, 0:z_q[0].shape[1]]
+            multiply(bank, w2_q, z_q)
+            return bank
 
-        def chunk_filters(c, role):
-            for d in range(LISTS):
-                for b in range(2):
-                    strip_filters(c, d, b, role + 2 * d + b)
-
-        def weave(c, d, b):
-            nc.vector.tensor_tensor(
-                woven[c][:, d, b * P:(b + 1) * P, :].rearrange("p (c e) t -> p c t e", e=2),
-                f[(c, d, b)][:].rearrange("p (t c e) -> p c t e", t=PACK, e=2),
-                found[(c, d)][:, :, b * P:(b + 1) * P].rearrange("p t (c e) -> p c t e", e=2),
-                MULT,
-            )
-
-        banks = {}
-
-        def project(v0, z_q, role):
-            banks[v0] = new_bank(role)
-            width = z_q[0].shape[1]
-            multiply(banks[v0][:, 0:width], w2_q, z_q)
-
-        def store(v0, width):
+        def store(bank, v0):
+            width = bank.shape[1]
             result = held([P, width], F32, "result%d" % v0)
-            nc.scalar.copy(out=result[:], in_=banks[v0][:, 0:width])
+            nc.scalar.copy(out=result[:], in_=bank)
             nc.sync.dma_start(out=out[:, v0:v0 + width], in_=result[:])
 
-        low = held([P, 2 * P, PACK], BF16, "w1_0a_bf")
-        round_weights("vector", w1_raw[0], 0, 2, low[:])
-        high = held([P, 4 * P, PACK], BF16, "w1_high_bf")
-        round_weights("scalar", w1_raw[0], 2, 2, high[:, 0:2 * P, :])
-        w1_q = [parts(quantise(low[:], "w1_0a"), P), []]
-        low = held([P, 2 * P, PACK], BF16, "w1_1a_bf")
+        low0_bf = held([P, 2 * P, PACK], BF16, "w1_low0_bf")
+        round_weights(nc.vector.tensor_copy, w1_raw[0], 0, 2, low0_bf[:])
+        high_bf = held([P, 4 * P, PACK], BF16, "w1_high_bf")
+        round_weights(nc.scalar.copy, w1_raw[0], 2, 2, high_bf[:, 0:2 * P, :])
+        w1_q = [quantise(low0_bf[:], "w1_low0", P), []]
+        low1_bf = held([P, 2 * P, PACK], BF16, "w1_low1_bf")
         for t in range(2):
-            round_weights("vector", w1_raw[1], t, 1, low[:, t * P:(t + 1) * P, :])
-        round_weights("scalar", w1_raw[1], 2, 2, high[:, 2 * P:4 * P, :])
+            round_weights(nc.vector.tensor_copy, w1_raw[1], t, 1, low1_bf[:, t * P:(t + 1) * P, :])
+        round_weights(nc.scalar.copy, w1_raw[1], 2, 2, high_bf[:, 2 * P:4 * P, :])
         for t in range(2):
-            w1_q[1].extend(parts(quantise(low[:, t * P:(t + 1) * P, :], "w1_1_%d" % t), P))
-        high_q = parts(quantise(high[:], "w1_high"), P)
+            w1_q[1].extend(quantise(low1_bf[:, t * P:(t + 1) * P, :], "w1_low1_%d" % t, P))
+        high_q = quantise(high_bf[:], "w1_high", P)
         for g in range(K // PASS):
             w1_q[g].extend(high_q[2 * g:2 * g + 2])
+        h_banks = []
         for t in range(PACK):
-            h_banks[t] = [new_bank(2 * t + half) for half in range(2)]
+            h_banks.append([new_bank(2 * t + half) for half in range(2)])
             for g in range(K // PASS):
                 for half in range(2):
                     nc.tensor.matmul_mx(
@@ -261,83 +230,89 @@ def tile_picked_wdime_none_l_kernel(
                         stop=(g == K // PASS - 1),
                     )
 
-        round_piece("vector", 0, 0)
+        round_piece(0, 0)
         quantise_piece(0, 0)
         for t in range(PACK):
-            activate(t)
-        gather("vector", 0, 0, BANK, 0, wide[:, 0, :])
-        gather("vector", 1, 0, CHUNK, 0, found[(0, 1)][:, 0, :])
-        w3_bf = [held([P, 2 * P, PACK], BF16, "w3_%d_bf" % u) for u in range(2)]
-        for u in range(2):
-            round_weights("vector", w3_raw, 2 * u, 2, w3_bf[u][:])
-        for u in range(2):
-            w3_q.extend(parts(quantise(w3_bf[u][:], "w3_%d" % u), P))
+            for half in range(2):
+                nc.scalar.activation(h[t][:, half * BANK:(half + 1) * BANK], h_banks[t][half][:], SILU)
+
+        gather_on_vector(0, 0, 0, wide[:, 0, :])
+        gather_on_vector(1, 0, 0, found[(1, 0)][:, 0, :])
+        w3_bf = [held([P, 2 * P, PACK], BF16, "w3_bf%d" % u) for u in range(PAIRS)]
+        for u in range(PAIRS):
+            round_weights(nc.vector.tensor_copy, w3_raw, 2 * u, 2, w3_bf[u][:])
+        for u in range(PAIRS):
+            w3_q.extend(quantise(w3_bf[u][:], "w3_%d" % u, P))
         for t in range(1, PACK):
-            gather("scalar", 0, 0, BANK, t, wide[:, t, :])
-        for c, d in ((0, 1), (1, 1), (2, 0), (2, 1)):
-            for t in range(1 if c == 0 else 0, PACK):
-                gather("scalar", d, c * CHUNK, CHUNK, t, found[(c, d)][:, t, :])
-        for t in range(PACK):
-            for d in range(LISTS):
-                gather("scalar", d, 3 * CHUNK, CHUNK, t, picked[t][:, d * CHUNK:(d + 1) * CHUNK])
-        round_piece("vector", 1, 0)
-        round_piece("vector", 0, CHUNK)
+            gather_on_scalar(0, t, 0, wide[:, t, :])
+        for t in range(1, PACK):
+            gather_on_scalar(1, t, 0, found[(1, 0)][:, t, :])
+        for d, c in ((1, 1), (0, 2), (1, 2), (0, 3), (1, 3)):
+            for t in range(found[(d, c)].shape[1]):
+                gather_on_scalar(d, t, c * CHUNK, found[(d, c)][:, t, :])
+        for b in range(2):
+            for e in range(2):
+                gather_on_scalar(1, 2 + e, 3 * CHUNK + b * STRIP, found_strip[b][:, e, :])
+
+        round_piece(1, 0)
+        round_piece(0, 1)
         quantise_piece(1, 0)
-        quantise_piece(0, CHUNK)
+        quantise_piece(0, 1)
         for c in range(2):
-            chunk_filters(c, PACK * c)
-        round_piece("vector", 0, BANK)
-        early = held([P, 2, LISTS, CHUNK, PACK], F32, "early", "a_raw0_512")
-        woven[0] = early[:, 0]
-        woven[1] = early[:, 1]
-        weave(0, 0, 0)
-        quantise_piece(0, BANK)
-        late_bf = held([P, CHUNK + N, PACK], BF16, "late_bf", "a0_512_bf")
-        round_on_gpsimd(a_raw[(1, BANK + CHUNK)], late_bf[:, 0:CHUNK, :])
-        round_on_gpsimd(w2_raw, late_bf[:, CHUNK:, :])
-        for d, b in ((0, 1), (1, 0), (1, 1)):
-            weave(0, d, b)
-        mixed_bf = held([P, 2 * CHUNK, PACK], BF16, "mixed_bf")
-        add_on_gpsimd(mixed_bf[:, 0:CHUNK, :], 0)
-        for d in range(LISTS):
-            for b in range(2):
-                weave(1, d, b)
-        round_columns("vector", a_raw[(1, BANK)], mixed_bf[:, CHUNK:, :])
-        z0_q, a_q[(1, BANK)] = parts(quantise(mixed_bf[:], "mixed"), CHUNK)
-        chunk_filters(2, 0)
-        late_codes, late_plane = quantise(late_bf[:], "late", "mixed_bf")
-        a_q[(1, BANK + CHUNK)] = (late_codes[:, 0:CHUNK], late_plane[:, 0:CHUNK])
-        w2_q = (late_codes[:, CHUNK:], late_plane[:, CHUNK:])
-        for t in range(PACK):
-            filters(3, t, PACK + t)
-        z_codes = held([P, T], U32, "z_codes")
-        z_plane = held([P, T], U8, "z_plane")
+            for d in range(LISTS):
+                filters(d, c)
+        round_piece(1, 2)
+        a_bf[(0, 2)] = placed([P, 2 * CHUNK, PACK], BF16, "a_bf0_2", AT_A0_2)
+        round_on_vector(a_raw[(0, 2)], a_bf[(0, 2)][:])
+        quantise_piece(1, 2)
+        quantise_piece(0, 2)
 
-        def quantise_z(z, v0, width):
-            quantise_into(z_codes[:, v0:v0 + width], z_plane[:, v0:v0 + width], z)
-
-        z = held([P, 2 * CHUNK, PACK], BF16, "z12", "a0_512_bf")
-        add_on_gpsimd(z[:, 0:CHUNK, :], 1)
-        woven[2] = held([P, LISTS, CHUNK, PACK], F32, "woven2", "w1_raw0")[:]
+        early_terms = placed([P, 2, LISTS, PAIRS, CHUNK, 2], F32, "early_terms", AT_EARLY_TERMS)
+        for c in range(2):
+            for d in range(LISTS):
+                terms[(d, c)] = early_terms[:, c, d]
+        shared_bf = placed([P, 2 * CHUNK + N, PACK], BF16, "shared_bf", AT_SHARED)
+        round_on_gpsimd(a_raw[(1, 3)], shared_bf[:, CHUNK:2 * CHUNK, :])
+        round_on_gpsimd(w2_raw, shared_bf[:, 2 * CHUNK:, :])
         for d in range(LISTS):
-            for b in range(2):
-                weave(2, d, b)
-        add_on_gpsimd(z[:, CHUNK:CHUNK + P, :], 2, P)
-        for t in range(2):
-            weigh(3, t, "w1_raw1")
-        nc.vector.tensor_tensor(z[:, CHUNK + P:, :], woven[2][:, 0, P:, :], woven[2][:, 1, P:, :], ADD)
-        weigh(3, 2)
-        quantise_z(z[:], CHUNK, 2 * CHUNK)
-        weigh(3, PACK - 1)
-        project(0, z0_q, 0)
-        project(CHUNK, (z_codes[:, CHUNK:CHUNK + BANK], z_plane[:, CHUNK:CHUNK + BANK]), 1)
-        store(0, CHUNK)
-        store(CHUNK, BANK)
-        last = held([P, CHUNK, PACK], BF16, "last")
-        for b in range(2):
-            add(nc.vector, last[:, b * P:(b + 1) * P, :], 3, b * P, P)
-        for b in range(2):
-            v0 = BANK + CHUNK + b * P
-            quantise_z(last[:, b * P:(b + 1) * P, :], v0, P)
-            project(v0, (z_codes[:, v0:v0 + P], z_plane[:, v0:v0 + P]), 2 + b)
-            store(v0, P)
+            for u in range(PAIRS):
+                weigh(d, 0, u)
+        for d in range(LISTS):
+            filters(d, 2)
+        add(nc.gpsimd, shared_bf[:, 0:CHUNK, :], 0, 0)
+        for d in range(LISTS):
+            for u in range(PAIRS):
+                weigh(d, 1, u)
+        filters(0, 3)
+        terms[(0, 2)] = held([P, PAIRS, CHUNK, 2], F32, "terms0_2")[:]
+        weigh(0, 2, 0)
+        z0_q, a_q[(1, 3)] = quantise(shared_bf[:, 0:2 * CHUNK, :], "z0_a1_3", CHUNK)
+        w2_q = quantise(shared_bf[:, 2 * CHUNK:, :], "w2", N)[0]
+        filters(1, 3)
+
+        z12_bf = placed([P, 2 * CHUNK, PACK], BF16, "z12_bf", AT_Z12)
+        add(nc.gpsimd, z12_bf[:, 0:CHUNK, :], 1, 0)
+        weigh(0, 2, 1)
+        terms[(1, 2)] = placed([P, PAIRS, CHUNK, 2], F32, "terms1_2", AT_TERMS1_2)[:]
+        for u in range(PAIRS):
+            weigh(1, 2, u)
+        last_terms = placed([P, LISTS, PAIRS, CHUNK, 2], F32, "last_terms", AT_LAST_TERMS)
+        for d in range(LISTS):
+            terms[(d, 3)] = last_terms[:, d]
+        weigh(0, 3, 0)
+        add(nc.vector, z12_bf[:, CHUNK:, :], 2, 0)
+        weigh(0, 3, 1)
+        z12_q = quantise(z12_bf[:], "z12", 2 * CHUNK)[0]
+        weigh(1, 3, 0)
+        bank0 = project(z0_q, 0)
+        bank12 = project(z12_q, 1)
+        store(bank0, 0)
+        store(bank12, CHUNK)
+
+        z3_bf = held([P, CHUNK, PACK], BF16, "z3_bf")
+        weigh_values(1, 3, 1, 0, found_strip[0][:])
+        add(nc.vector, z3_bf[:, 0:STRIP, :], 3, 0)
+        weigh_values(1, 3, 1, STRIP, found_strip[1][:])
+        store(project(quantise(z3_bf[:, 0:STRIP, :], "z3_0", STRIP)[0], 2), 3 * CHUNK)
+        add(nc.vector, z3_bf[:, STRIP:, :], 3, STRIP)
+        store(project(quantise(z3_bf[:, STRIP:, :], "z3_1", STRIP)[0], 3), 3 * CHUNK + STRIP)

@@ -151,10 +151,13 @@ def tile_picked_wdime_none_l_kernel(
         w3_q = []
         f = {}
         terms = {}
-        wide = held([P, PACK, 2 * CHUNK], F32, "wide")
-        found = {(0, c): wide[:, :, c * CHUNK:(c + 1) * CHUNK] for c in range(2)}
-        for d, c in ((1, 0), (1, 1), (0, 2), (1, 2), (0, 3)):
-            found[(d, c)] = held([P, PACK, CHUNK], F32, "found%d_%d" % (d, c))[:]
+        wide = {}
+        found = {}
+        for d, c in ((0, 0), (1, 0), (0, 2)):
+            wide[(d, c)] = held([P, PACK, 2 * CHUNK], F32, "wide%d_%d" % (d, c))
+            for n in range(2):
+                found[(d, c + n)] = wide[(d, c)][:, :, n * CHUNK:(n + 1) * CHUNK]
+        found[(1, 2)] = held([P, PACK, CHUNK], F32, "found1_2")[:]
         found[(1, 3)] = held([P, 2, CHUNK], F32, "found1_3")[:]
         found_strip = [held([P, 2, STRIP], F32, "found_strip%d" % b) for b in range(2)]
 
@@ -236,7 +239,7 @@ def tile_picked_wdime_none_l_kernel(
             for half in range(2):
                 nc.scalar.activation(h[t][:, half * BANK:(half + 1) * BANK], h_banks[t][half][:], SILU)
 
-        gather_on_vector(0, 0, 0, wide[:, 0, :])
+        gather_on_vector(0, 0, 0, wide[(0, 0)][:, 0, :])
         gather_on_vector(1, 0, 0, found[(1, 0)][:, 0, :])
         w3_bf = [held([P, 2 * P, PACK], BF16, "w3_bf%d" % u) for u in range(PAIRS)]
         for u in range(PAIRS):
@@ -244,10 +247,13 @@ def tile_picked_wdime_none_l_kernel(
         for u in range(PAIRS):
             w3_q.extend(quantise(w3_bf[u][:], "w3_%d" % u, P))
         for t in range(1, PACK):
-            gather_on_scalar(0, t, 0, wide[:, t, :])
+            gather_on_scalar(0, t, 0, wide[(0, 0)][:, t, :])
+        gather_on_scalar(1, 0, CHUNK, found[(1, 1)][:, 0, :])
         for t in range(1, PACK):
-            gather_on_scalar(1, t, 0, found[(1, 0)][:, t, :])
-        for d, c in ((1, 1), (0, 2), (1, 2), (0, 3), (1, 3)):
+            gather_on_scalar(1, t, 0, wide[(1, 0)][:, t, :])
+        for t in range(PACK):
+            gather_on_scalar(0, t, 2 * CHUNK, wide[(0, 2)][:, t, :])
+        for d, c in ((1, 2), (1, 3)):
             for t in range(found[(d, c)].shape[1]):
                 gather_on_scalar(d, t, c * CHUNK, found[(d, c)][:, t, :])
         for b in range(2):
@@ -293,17 +299,17 @@ def tile_picked_wdime_none_l_kernel(
         z12_bf = placed([P, 2 * CHUNK, PACK], BF16, "z12_bf", AT_Z12)
         add(nc.gpsimd, z12_bf[:, 0:CHUNK, :], 1, 0)
         weigh(0, 2, 1)
-        terms[(1, 2)] = placed([P, PAIRS, CHUNK, 2], F32, "terms1_2", AT_TERMS1_2)[:]
-        for u in range(PAIRS):
-            weigh(1, 2, u)
         last_terms = placed([P, LISTS, PAIRS, CHUNK, 2], F32, "last_terms", AT_LAST_TERMS)
         for d in range(LISTS):
             terms[(d, 3)] = last_terms[:, d]
         weigh(0, 3, 0)
-        add(nc.vector, z12_bf[:, CHUNK:, :], 2, 0)
+        terms[(1, 2)] = placed([P, PAIRS, CHUNK, 2], F32, "terms1_2", AT_TERMS1_2)[:]
+        for u in range(PAIRS):
+            weigh(1, 2, u)
         weigh(0, 3, 1)
-        z12_q = quantise(z12_bf[:], "z12", 2 * CHUNK)[0]
+        add(nc.vector, z12_bf[:, CHUNK:, :], 2, 0)
         weigh(1, 3, 0)
+        z12_q = quantise(z12_bf[:], "z12", 2 * CHUNK)[0]
         bank0 = project(z0_q, 0)
         bank12 = project(z12_q, 1)
         store(bank0, 0)

@@ -30,12 +30,12 @@ PER_COLUMN = 16
 
 UNIT = PACK * CHUNK * 4
 REACH = 512
-AT_LAST_TERMS = 0
-AT_Z12 = LISTS * UNIT
-AT_TERMS1_2 = AT_Z12 + UNIT
-AT_EARLY_TERMS = AT_TERMS1_2 + UNIT
-AT_SHARED = AT_Z12 - REACH
-AT_A0_2 = AT_TERMS1_2 + REACH // 2
+AT_TERMS = 0
+AT_A_LAST = LISTS * UNIT - UNIT // 2
+AT_A_BF = 4 * UNIT
+AT_LAST_BF = AT_A_BF
+AT_LAST_CODES = LISTS * UNIT
+AT_Z23 = AT_LAST_CODES + UNIT // 2
 
 
 def tile_picked_wdime_none_l_kernel(
@@ -67,8 +67,9 @@ def tile_picked_wdime_none_l_kernel(
         def load_rows(tile, rows):
             nc.sync.dma_start(out=tile[:], in_=rows.rearrange("(p j) n -> p j n", j=PACK))
 
-        def load_a(d, c, chunks):
-            a_raw[(d, c)] = held([P, PACK, chunks * CHUNK], F32, "a_raw%d_%d" % (d, c))
+        def load_a(d, c, chunks, offset=None):
+            shape, name = [P, PACK, chunks * CHUNK], "a_raw%d_%d" % (d, c)
+            a_raw[(d, c)] = held(shape, F32, name) if offset is None else placed(shape, F32, name, offset)
             load_rows(a_raw[(d, c)], aT[:, d * T + c * CHUNK:d * T + (c + chunks) * CHUNK])
 
         def load_w1(g):
@@ -94,10 +95,9 @@ def tile_picked_wdime_none_l_kernel(
         nc.sync.dma_start(lists[1][:], pos2)
         load_a(0, 0, 1)
         load_rows(w3_raw, w3)
+        load_a(0, 1, 3)
         load_a(1, 0, 2)
-        load_a(0, 1, 1)
-        load_a(1, 2, 1)
-        load_a(0, 2, 2)
+        load_a(1, 2, 1, AT_A_LAST)
         load_a(1, 3, 1)
         w2_rows = w2.rearrange("(q t r) n -> r q t n", t=PACK, r=4)
         for r in range(4):
@@ -112,18 +112,24 @@ def tile_picked_wdime_none_l_kernel(
         def round_on_vector(raw, grouped):
             nc.vector.tensor_copy(
                 out=grouped.rearrange("p (c e) j -> p c j e", e=2),
-                in_=raw[:].rearrange("p j (c e) -> p c j e", e=2),
+                in_=raw.rearrange("p j (c e) -> p c j e", e=2),
             )
 
         def round_on_gpsimd(raw, grouped):
             nc.gpsimd.tensor_scalar(grouped, raw[:].rearrange("p j c -> p c j"), 1.0, 0.0, MULT, ADD)
 
-        def quantise(grouped, name, width):
-            columns = grouped.shape[1]
-            codes = held([P, columns], U32, name + "_codes")
-            plane = held([P, columns], U8, name + "_plane")
-            nc.vector.quantize_mx(out=codes[:].bitcast(FP8X4), scales=plane[:], in_=grouped.rearrange("p w j -> p (w j)"))
-            return [(codes[:, at:at + width], plane[:, at:at + width]) for at in range(0, columns, width)]
+        def quantise_into(codes, plane, grouped):
+            nc.vector.quantize_mx(out=codes.bitcast(FP8X4), scales=plane, in_=grouped.rearrange("p w j -> p (w j)"))
+
+        def runs(codes, plane, width):
+            return [(codes[:, at:at + width], plane[:, at:at + width]) for at in range(0, codes.shape[1], width)]
+
+        def quantise(grouped, name, width, offset=None):
+            shape = [P, grouped.shape[1]]
+            codes = held(shape, U32, name + "_codes") if offset is None else placed(shape, U32, name + "_codes", offset)
+            plane = held(shape, U8, name + "_plane")
+            quantise_into(codes[:], plane[:], grouped)
+            return runs(codes[:], plane[:], width)
 
         def multiply(result, stationary, moving):
             nc.tensor.matmul_mx(
@@ -136,16 +142,7 @@ def tile_picked_wdime_none_l_kernel(
                 stop=True,
             )
 
-        a_bf = {}
         a_q = {}
-
-        def round_piece(d, c):
-            a_bf[(d, c)] = held([P, a_raw[(d, c)].shape[2], PACK], BF16, "a_bf%d_%d" % (d, c))
-            round_on_vector(a_raw[(d, c)], a_bf[(d, c)][:])
-
-        def quantise_piece(d, c):
-            for n, part in enumerate(quantise(a_bf[(d, c)][:], "a%d_%d" % (d, c), CHUNK)):
-                a_q[(d, c + n)] = part
 
         h = [held([P, T], F32, "h%d" % t) for t in range(PACK)]
         w3_q = []
@@ -170,9 +167,9 @@ def tile_picked_wdime_none_l_kernel(
         def gather_on_vector(d, t, v0, into):
             nc.vector.tensor_copy(out=into, in_=window(d, t, v0, into.shape[1]))
 
-        def filters(d, c):
+        def filters(d, c, banks):
             for u in range(PAIRS):
-                f[(d, c, u)] = new_bank(LISTS * PAIRS * (c % 2) + PAIRS * d + u)
+                f[(d, c, u)] = new_bank(banks[u])
                 for e in range(2):
                     multiply(f[(d, c, u)][:, e * CHUNK:(e + 1) * CHUNK], w3_q[2 * u + e], a_q[(d, c)])
 
@@ -193,10 +190,13 @@ def tile_picked_wdime_none_l_kernel(
             first, second = (terms[(d, c)][:, :, v0:v0 + width, :].rearrange("p u v e -> p v u e") for d in range(LISTS))
             engine.tensor_tensor(z.rearrange("p v (u e) -> p v u e", e=2), first, second, ADD)
 
-        def project(z_q, number):
-            bank = new_bank(number)[:, 0:z_q[0].shape[1]]
-            multiply(bank, w2_q, z_q)
-            return bank
+        def project(parts, number):
+            bank = new_bank(number)
+            at = 0
+            for part in parts:
+                multiply(bank[:, at:at + part[0].shape[1]], w2_q, part)
+                at = at + part[0].shape[1]
+            return bank[:, 0:at]
 
         def store(bank, v0):
             width = bank.shape[1]
@@ -233,14 +233,15 @@ def tile_picked_wdime_none_l_kernel(
                         stop=(g == K // PASS - 1),
                     )
 
-        round_piece(0, 0)
-        quantise_piece(0, 0)
+        first_bf = held([P, CHUNK, PACK], BF16, "first_bf")
+        round_on_vector(a_raw[(0, 0)][:], first_bf[:])
+        a_q[(0, 0)] = quantise(first_bf[:], "a0_0", CHUNK)[0]
         for t in range(PACK):
             for half in range(2):
                 nc.scalar.activation(h[t][:, half * BANK:(half + 1) * BANK], h_banks[t][half][:], SILU)
 
         gather_on_vector(0, 0, 0, wide[(0, 0)][:, 0, :])
-        gather_on_vector(1, 0, 0, found[(1, 0)][:, 0, :])
+        gather_on_vector(0, 0, 2 * CHUNK, wide[(0, 2)][:, 0, :])
         w3_bf = [held([P, 2 * P, PACK], BF16, "w3_bf%d" % u) for u in range(PAIRS)]
         for u in range(PAIRS):
             round_weights(nc.vector.tensor_copy, w3_raw, 2 * u, 2, w3_bf[u][:])
@@ -248,10 +249,9 @@ def tile_picked_wdime_none_l_kernel(
             w3_q.extend(quantise(w3_bf[u][:], "w3_%d" % u, P))
         for t in range(1, PACK):
             gather_on_scalar(0, t, 0, wide[(0, 0)][:, t, :])
-        gather_on_scalar(1, 0, CHUNK, found[(1, 1)][:, 0, :])
-        for t in range(1, PACK):
-            gather_on_scalar(1, t, 0, wide[(1, 0)][:, t, :])
         for t in range(PACK):
+            gather_on_scalar(1, t, 0, wide[(1, 0)][:, t, :])
+        for t in range(1, PACK):
             gather_on_scalar(0, t, 2 * CHUNK, wide[(0, 2)][:, t, :])
         for d, c in ((1, 2), (1, 3)):
             for t in range(found[(d, c)].shape[1]):
@@ -260,65 +260,66 @@ def tile_picked_wdime_none_l_kernel(
             for e in range(2):
                 gather_on_scalar(1, 2 + e, 3 * CHUNK + b * STRIP, found_strip[b][:, e, :])
 
-        round_piece(1, 0)
-        round_piece(0, 1)
-        quantise_piece(1, 0)
-        quantise_piece(0, 1)
-        for c in range(2):
-            for d in range(LISTS):
-                filters(d, c)
-        round_piece(1, 2)
-        a_bf[(0, 2)] = placed([P, 2 * CHUNK, PACK], BF16, "a_bf0_2", AT_A0_2)
-        round_on_vector(a_raw[(0, 2)], a_bf[(0, 2)][:])
-        quantise_piece(1, 2)
-        quantise_piece(0, 2)
+        def round_halves(raw, grouped):
+            half = raw.shape[2] // 2
+            for at in (0, half):
+                round_on_vector(raw[:, :, at:at + half], grouped[:, at:at + half, :])
 
-        early_terms = placed([P, 2, LISTS, PAIRS, CHUNK, 2], F32, "early_terms", AT_EARLY_TERMS)
-        for c in range(2):
-            for d in range(LISTS):
-                terms[(d, c)] = early_terms[:, c, d]
-        shared_bf = placed([P, 2 * CHUNK + N, PACK], BF16, "shared_bf", AT_SHARED)
-        round_on_gpsimd(a_raw[(1, 3)], shared_bf[:, CHUNK:2 * CHUNK, :])
-        round_on_gpsimd(w2_raw, shared_bf[:, 2 * CHUNK:, :])
-        for d in range(LISTS):
-            for u in range(PAIRS):
-                weigh(d, 0, u)
-        for d in range(LISTS):
-            filters(d, 2)
-        add(nc.gpsimd, shared_bf[:, 0:CHUNK, :], 0, 0)
-        for d in range(LISTS):
-            for u in range(PAIRS):
-                weigh(d, 1, u)
-        filters(0, 3)
-        terms[(0, 2)] = held([P, PAIRS, CHUNK, 2], F32, "terms0_2")[:]
-        weigh(0, 2, 0)
-        z0_q, a_q[(1, 3)] = quantise(shared_bf[:, 0:2 * CHUNK, :], "z0_a1_3", CHUNK)
-        w2_q = quantise(shared_bf[:, 2 * CHUNK:, :], "w2", N)[0]
-        filters(1, 3)
+        def quantise_parts(grouped, name, ends):
+            codes = held([P, ends[-1]], U32, name + "_codes")
+            plane = held([P, ends[-1]], U8, name + "_plane")
+            for at, end in zip([0] + ends[:-1], ends):
+                quantise_into(codes[:, at:end], plane[:, at:end], grouped[:, at:end, :])
+            return runs(codes[:], plane[:], CHUNK)
 
-        z12_bf = placed([P, 2 * CHUNK, PACK], BF16, "z12_bf", AT_Z12)
-        add(nc.gpsimd, z12_bf[:, 0:CHUNK, :], 1, 0)
-        weigh(0, 2, 1)
-        last_terms = placed([P, LISTS, PAIRS, CHUNK, 2], F32, "last_terms", AT_LAST_TERMS)
+        rest_bf = held([P, 3 * CHUNK, PACK], BF16, "rest_bf")
+        round_halves(a_raw[(0, 1)][:], rest_bf[:])
+        a_q[(0, 1)], a_q[(0, 2)], a_q[(0, 3)] = quantise_parts(rest_bf, "rest", [3 * STRIP, 6 * STRIP])
+        a_bf = placed([P, 3 * CHUNK, PACK], BF16, "a_bf", AT_A_BF)
+        round_halves(a_raw[(1, 0)][:], a_bf[:, 0:2 * CHUNK, :])
+        round_halves(a_raw[(1, 2)][:], a_bf[:, 2 * CHUNK:, :])
+        a_q[(1, 0)], a_q[(1, 1)], a_q[(1, 2)] = quantise_parts(a_bf, "second", [2 * STRIP, 5 * STRIP, 6 * STRIP])
         for d in range(LISTS):
-            terms[(d, 3)] = last_terms[:, d]
-        weigh(0, 3, 0)
-        terms[(1, 2)] = placed([P, PAIRS, CHUNK, 2], F32, "terms1_2", AT_TERMS1_2)[:]
-        for u in range(PAIRS):
-            weigh(1, 2, u)
-        weigh(0, 3, 1)
-        add(nc.vector, z12_bf[:, CHUNK:, :], 2, 0)
+            for c in range(2):
+                filters(d, c, [LISTS * PAIRS * c + PAIRS * d + u for u in range(PAIRS)])
+
+        for c in range(2):
+            early_terms = placed([P, LISTS, PAIRS, CHUNK, 2], F32, "early_terms%d" % c, AT_TERMS + c * LISTS * UNIT)
+            for d in range(LISTS):
+                terms[(d, c)] = early_terms[:, d]
+        for c in range(2, 4):
+            for d in range(LISTS):
+                terms[(d, c)] = held([P, PAIRS, CHUNK, 2], F32, "terms%d_%d" % (d, c))[:]
+        last_bf = placed([P, CHUNK + N, PACK], BF16, "last_bf", AT_LAST_BF)
+        z01_bf = held([P, 2 * CHUNK, PACK], BF16, "z01_bf")
+        round_on_gpsimd(a_raw[(1, 3)], last_bf[:, 0:CHUNK, :])
+        round_on_gpsimd(w2_raw, last_bf[:, CHUNK:, :])
+        for d, c, u in ((0, 1, 1), (0, 0, 0), (0, 0, 1), (1, 0, 1), (1, 0, 0)):
+            weigh(d, c, u)
+        add(nc.gpsimd, z01_bf[:, 0:CHUNK, :], 0, 0)
+        for d, c, u in ((0, 1, 0), (1, 1, 1), (1, 1, 0)):
+            weigh(d, c, u)
+        add(nc.gpsimd, z01_bf[:, CHUNK:, :], 1, 0)
+        filters(0, 3, (5, 1))
+        filters(0, 2, (0, 3))
+        filters(1, 2, (2, 4))
+        for d, c, u in ((0, 2, 0), (0, 3, 0), (0, 2, 1), (0, 3, 1), (1, 2, 0), (1, 2, 1)):
+            weigh(d, c, u)
+
+        last_codes, last_plane = quantise(last_bf[:], "last", CHUNK + N, AT_LAST_CODES)[0]
+        a_q[(1, 3)] = (last_codes[:, 0:CHUNK], last_plane[:, 0:CHUNK])
+        w2_q = (last_codes[:, CHUNK:], last_plane[:, CHUNK:])
+        filters(1, 3, (7, 6))
+        z23_bf = placed([P, 2 * CHUNK, PACK], BF16, "z23_bf", AT_Z23)
+        add(nc.vector, z23_bf[:, 0:CHUNK, :], 2, 0)
+        store(project(quantise(z01_bf[:], "z01", 2 * CHUNK), 5), 0)
         weigh(1, 3, 0)
-        z12_q = quantise(z12_bf[:], "z12", 2 * CHUNK)[0]
-        bank0 = project(z0_q, 0)
-        bank12 = project(z12_q, 1)
-        store(bank0, 0)
-        store(bank12, CHUNK)
+        store(project(quantise(z23_bf[:, 0:CHUNK, :], "z2", CHUNK), 3), 2 * CHUNK)
 
-        z3_bf = held([P, CHUNK, PACK], BF16, "z3_bf")
+        z3_bf = z23_bf[:, CHUNK:, :]
         weigh_values(1, 3, 1, 0, found_strip[0][:])
         add(nc.vector, z3_bf[:, 0:STRIP, :], 3, 0)
         weigh_values(1, 3, 1, STRIP, found_strip[1][:])
-        store(project(quantise(z3_bf[:, 0:STRIP, :], "z3_0", STRIP)[0], 2), 3 * CHUNK)
+        store(project(quantise(z3_bf[:, 0:STRIP, :], "z3_0", STRIP), 0), 3 * CHUNK)
         add(nc.vector, z3_bf[:, STRIP:, :], 3, STRIP)
-        store(project(quantise(z3_bf[:, STRIP:, :], "z3_1", STRIP)[0], 3), 3 * CHUNK + STRIP)
+        store(project(quantise(z3_bf[:, STRIP:, :], "z3_1", STRIP), 1), 3 * CHUNK + STRIP)

@@ -35,6 +35,7 @@ AT_A_LAST = LISTS * UNIT - UNIT // 2
 AT_A_BF = 4 * UNIT
 AT_LAST_BF = AT_A_BF
 AT_LAST_CODES = LISTS * UNIT
+AT_W2_CODES = AT_LAST_CODES + UNIT // 4
 AT_Z23 = AT_LAST_CODES + UNIT // 2
 
 
@@ -65,15 +66,15 @@ def tile_picked_wdime_none_l_kernel(
         a_raw = {}
 
         def load_rows(tile, rows):
-            nc.sync.dma_start(out=tile[:], in_=rows.rearrange("(p j) n -> p j n", j=PACK))
+            nc.sync.dma_start(out=tile, in_=rows.rearrange("(p j) n -> p j n", j=PACK))
 
         def load_a(d, c, chunks, offset=None):
             shape, name = [P, PACK, chunks * CHUNK], "a_raw%d_%d" % (d, c)
             a_raw[(d, c)] = held(shape, F32, name) if offset is None else placed(shape, F32, name, offset)
-            load_rows(a_raw[(d, c)], aT[:, d * T + c * CHUNK:d * T + (c + chunks) * CHUNK])
+            load_rows(a_raw[(d, c)][:], aT[:, d * T + c * CHUNK:d * T + (c + chunks) * CHUNK])
 
         def load_w1(g):
-            load_rows(w1_raw[g], w1[g * PASS:(g + 1) * PASS, :])
+            load_rows(w1_raw[g][:], w1[g * PASS:(g + 1) * PASS, :])
 
         def load_x(g):
             nc.sync.dma_start(out=x_codes[g][:].bitcast(I32), in_=x_words[g].bitcast(I32))
@@ -91,10 +92,10 @@ def tile_picked_wdime_none_l_kernel(
         load_x(0)
         load_w1(1)
         load_x(1)
+        load_a(0, 0, 1)
         nc.sync.dma_start(lists[0][:], pos1)
         nc.sync.dma_start(lists[1][:], pos2)
-        load_a(0, 0, 1)
-        load_rows(w3_raw, w3)
+        load_rows(w3_raw[:], w3)
         load_a(0, 1, 3)
         load_a(1, 0, 2)
         load_a(1, 2, 1, AT_A_LAST)
@@ -109,8 +110,8 @@ def tile_picked_wdime_none_l_kernel(
                 in_=raw[:].rearrange("p j (q t r) -> p t q j r", t=PACK, r=4)[:, t0:t0 + tiles],
             )
 
-        def round_on_vector(raw, grouped):
-            nc.vector.tensor_copy(
+        def round_columns(copy, raw, grouped):
+            copy(
                 out=grouped.rearrange("p (c e) j -> p c j e", e=2),
                 in_=raw.rearrange("p j (c e) -> p c j e", e=2),
             )
@@ -155,8 +156,7 @@ def tile_picked_wdime_none_l_kernel(
             for n in range(2):
                 found[(d, c + n)] = wide[(d, c)][:, :, n * CHUNK:(n + 1) * CHUNK]
         found[(1, 2)] = held([P, PACK, CHUNK], F32, "found1_2")[:]
-        found[(1, 3)] = held([P, 2, CHUNK], F32, "found1_3")[:]
-        found_strip = [held([P, 2, STRIP], F32, "found_strip%d" % b) for b in range(2)]
+        found[(1, 3)] = held([P, PACK, CHUNK], F32, "found1_3")[:]
 
         def window(d, t, v0, width):
             return h[t][:].indirect(lists[d][:, v0 // PER_COLUMN:(v0 + width) // PER_COLUMN])
@@ -173,17 +173,13 @@ def tile_picked_wdime_none_l_kernel(
                 for e in range(2):
                     multiply(f[(d, c, u)][:, e * CHUNK:(e + 1) * CHUNK], w3_q[2 * u + e], a_q[(d, c)])
 
-        def weigh_values(d, c, u, v0, values):
-            width = values.shape[2]
+        def weigh(d, c, u):
             nc.vector.tensor_tensor(
-                terms[(d, c)][:, u, v0:v0 + width, :],
-                f[(d, c, u)][:].rearrange("p (e v) -> p v e", e=2)[:, v0:v0 + width, :],
-                values.rearrange("p e v -> p v e"),
+                terms[(d, c)][:, u],
+                f[(d, c, u)][:].rearrange("p (e v) -> p v e", e=2),
+                found[(d, c)][:, 2 * u:2 * u + 2, :].rearrange("p e v -> p v e"),
                 MULT,
             )
-
-        def weigh(d, c, u):
-            weigh_values(d, c, u, 0, found[(d, c)][:, 2 * u:2 * u + 2, :])
 
         def add(engine, z, c, v0):
             width = z.shape[1]
@@ -204,37 +200,34 @@ def tile_picked_wdime_none_l_kernel(
             nc.scalar.copy(out=result[:], in_=bank)
             nc.sync.dma_start(out=out[:, v0:v0 + width], in_=result[:])
 
-        low0_bf = held([P, 2 * P, PACK], BF16, "w1_low0_bf")
-        round_weights(nc.vector.tensor_copy, w1_raw[0], 0, 2, low0_bf[:])
-        high_bf = held([P, 4 * P, PACK], BF16, "w1_high_bf")
-        round_weights(nc.scalar.copy, w1_raw[0], 2, 2, high_bf[:, 0:2 * P, :])
-        w1_q = [quantise(low0_bf[:], "w1_low0", P), []]
-        low1_bf = held([P, 2 * P, PACK], BF16, "w1_low1_bf")
+        w1_bf = [[held([P, 2 * P, PACK], BF16, "w1_bf%d_%d" % (g, u)) for u in range(PAIRS)] for g in range(K // PASS)]
+        round_weights(nc.vector.tensor_copy, w1_raw[0], 0, 2, w1_bf[0][0][:])
+        round_weights(nc.scalar.copy, w1_raw[0], 2, 2, w1_bf[0][1][:])
+        w1_q = [quantise(w1_bf[0][0][:], "w1_0_0", P) + quantise(w1_bf[0][1][:], "w1_0_1", P), []]
         for t in range(2):
-            round_weights(nc.vector.tensor_copy, w1_raw[1], t, 1, low1_bf[:, t * P:(t + 1) * P, :])
-        round_weights(nc.scalar.copy, w1_raw[1], 2, 2, high_bf[:, 2 * P:4 * P, :])
+            round_weights(nc.vector.tensor_copy, w1_raw[1], t, 1, w1_bf[1][0][:, t * P:(t + 1) * P, :])
+        round_weights(nc.scalar.copy, w1_raw[1], 2, 2, w1_bf[1][1][:])
         for t in range(2):
-            w1_q[1].extend(quantise(low1_bf[:, t * P:(t + 1) * P, :], "w1_low1_%d" % t, P))
-        high_q = quantise(high_bf[:], "w1_high", P)
-        for g in range(K // PASS):
-            w1_q[g].extend(high_q[2 * g:2 * g + 2])
+            w1_q[1].extend(quantise(w1_bf[1][0][:, t * P:(t + 1) * P, :], "w1_1_tile%d" % t, P))
+        w1_q[1].extend(quantise(w1_bf[1][1][:], "w1_1_1", P))
         h_banks = []
         for t in range(PACK):
             h_banks.append([new_bank(2 * t + half) for half in range(2)])
-            for g in range(K // PASS):
-                for half in range(2):
+            passes = (0, 1) if t < 2 else (1, 0)
+            for half in range(2):
+                for g in passes:
                     nc.tensor.matmul_mx(
                         out=h_banks[t][half][:],
                         lhsT=w1_q[g][t][0].bitcast(FP8X4),
                         lhsT_scale=w1_q[g][t][1],
                         rhs=x_codes[g][:, 2 * half * BANK:2 * (half + 1) * BANK].bitcast(FP4X4),
                         rhs_scale=x_plane[:, g, half * BANK:(half + 1) * BANK],
-                        start=(g == 0),
-                        stop=(g == K // PASS - 1),
+                        start=(g == passes[0]),
+                        stop=(g == passes[-1]),
                     )
 
         first_bf = held([P, CHUNK, PACK], BF16, "first_bf")
-        round_on_vector(a_raw[(0, 0)][:], first_bf[:])
+        round_columns(nc.vector.tensor_copy, a_raw[(0, 0)][:], first_bf[:])
         a_q[(0, 0)] = quantise(first_bf[:], "a0_0", CHUNK)[0]
         for t in range(PACK):
             for half in range(2):
@@ -242,6 +235,7 @@ def tile_picked_wdime_none_l_kernel(
 
         gather_on_vector(0, 0, 0, wide[(0, 0)][:, 0, :])
         gather_on_vector(0, 0, 2 * CHUNK, wide[(0, 2)][:, 0, :])
+        gather_on_vector(1, 0, 2 * CHUNK, found[(1, 2)][:, 0, :])
         w3_bf = [held([P, 2 * P, PACK], BF16, "w3_bf%d" % u) for u in range(PAIRS)]
         for u in range(PAIRS):
             round_weights(nc.vector.tensor_copy, w3_raw, 2 * u, 2, w3_bf[u][:])
@@ -253,17 +247,17 @@ def tile_picked_wdime_none_l_kernel(
             gather_on_scalar(1, t, 0, wide[(1, 0)][:, t, :])
         for t in range(1, PACK):
             gather_on_scalar(0, t, 2 * CHUNK, wide[(0, 2)][:, t, :])
-        for d, c in ((1, 2), (1, 3)):
-            for t in range(found[(d, c)].shape[1]):
-                gather_on_scalar(d, t, c * CHUNK, found[(d, c)][:, t, :])
-        for b in range(2):
-            for e in range(2):
-                gather_on_scalar(1, 2 + e, 3 * CHUNK + b * STRIP, found_strip[b][:, e, :])
+        for c, tiles in ((2, range(1, PACK)), (3, range(PACK))):
+            for t in tiles:
+                gather_on_scalar(1, t, c * CHUNK, found[(1, c)][:, t, :])
+
+        w2_bf = held([P, N, PACK], BF16, "w2_bf")
+        round_columns(nc.scalar.copy, w2_raw[:], w2_bf[:])
 
         def round_halves(raw, grouped):
             half = raw.shape[2] // 2
             for at in (0, half):
-                round_on_vector(raw[:, :, at:at + half], grouped[:, at:at + half, :])
+                round_columns(nc.vector.tensor_copy, raw[:, :, at:at + half], grouped[:, at:at + half, :])
 
         def quantise_parts(grouped, name, ends):
             codes = held([P, ends[-1]], U32, name + "_codes")
@@ -279,8 +273,8 @@ def tile_picked_wdime_none_l_kernel(
         round_halves(a_raw[(1, 0)][:], a_bf[:, 0:2 * CHUNK, :])
         round_halves(a_raw[(1, 2)][:], a_bf[:, 2 * CHUNK:, :])
         a_q[(1, 0)], a_q[(1, 1)], a_q[(1, 2)] = quantise_parts(a_bf, "second", [2 * STRIP, 5 * STRIP, 6 * STRIP])
-        for d in range(LISTS):
-            for c in range(2):
+        for c in range(2):
+            for d in range(LISTS):
                 filters(d, c, [LISTS * PAIRS * c + PAIRS * d + u for u in range(PAIRS)])
 
         for c in range(2):
@@ -290,36 +284,33 @@ def tile_picked_wdime_none_l_kernel(
         for c in range(2, 4):
             for d in range(LISTS):
                 terms[(d, c)] = held([P, PAIRS, CHUNK, 2], F32, "terms%d_%d" % (d, c))[:]
-        last_bf = placed([P, CHUNK + N, PACK], BF16, "last_bf", AT_LAST_BF)
+        last_bf = placed([P, CHUNK, PACK], BF16, "last_bf", AT_LAST_BF)
         z01_bf = held([P, 2 * CHUNK, PACK], BF16, "z01_bf")
-        round_on_gpsimd(a_raw[(1, 3)], last_bf[:, 0:CHUNK, :])
-        round_on_gpsimd(w2_raw, last_bf[:, CHUNK:, :])
-        for d, c, u in ((0, 1, 1), (0, 0, 0), (0, 0, 1), (1, 0, 1), (1, 0, 0)):
+        round_on_gpsimd(a_raw[(1, 3)], last_bf[:])
+        for d, c, u in ((0, 0, 1), (0, 0, 0), (1, 0, 1), (1, 0, 0)):
             weigh(d, c, u)
         add(nc.gpsimd, z01_bf[:, 0:CHUNK, :], 0, 0)
-        for d, c, u in ((0, 1, 0), (1, 1, 1), (1, 1, 0)):
+        for d, c, u in ((0, 1, 1), (0, 1, 0), (1, 1, 1), (1, 1, 0)):
             weigh(d, c, u)
         add(nc.gpsimd, z01_bf[:, CHUNK:, :], 1, 0)
-        filters(0, 3, (5, 1))
-        filters(0, 2, (0, 3))
-        filters(1, 2, (2, 4))
+        filters(0, 3, (1, 3))
+        filters(1, 2, (2, 5))
+        filters(0, 2, (0, 4))
         for d, c, u in ((0, 2, 0), (0, 3, 0), (0, 2, 1), (0, 3, 1), (1, 2, 0), (1, 2, 1)):
             weigh(d, c, u)
 
-        last_codes, last_plane = quantise(last_bf[:], "last", CHUNK + N, AT_LAST_CODES)[0]
-        a_q[(1, 3)] = (last_codes[:, 0:CHUNK], last_plane[:, 0:CHUNK])
-        w2_q = (last_codes[:, CHUNK:], last_plane[:, CHUNK:])
+        a_q[(1, 3)] = quantise(last_bf[:], "last", CHUNK, AT_LAST_CODES)[0]
         filters(1, 3, (7, 6))
         z23_bf = placed([P, 2 * CHUNK, PACK], BF16, "z23_bf", AT_Z23)
         add(nc.vector, z23_bf[:, 0:CHUNK, :], 2, 0)
-        store(project(quantise(z01_bf[:], "z01", 2 * CHUNK), 5), 0)
+        z01_q = quantise(z01_bf[:], "z01", 2 * CHUNK)
         weigh(1, 3, 0)
+        w2_q = quantise(w2_bf[:], "w2", N, AT_W2_CODES)[0]
+        store(project(z01_q, 4), 0)
+        weigh(1, 3, 1)
         store(project(quantise(z23_bf[:, 0:CHUNK, :], "z2", CHUNK), 3), 2 * CHUNK)
-
         z3_bf = z23_bf[:, CHUNK:, :]
-        weigh_values(1, 3, 1, 0, found_strip[0][:])
-        add(nc.vector, z3_bf[:, 0:STRIP, :], 3, 0)
-        weigh_values(1, 3, 1, STRIP, found_strip[1][:])
-        store(project(quantise(z3_bf[:, 0:STRIP, :], "z3_0", STRIP), 0), 3 * CHUNK)
-        add(nc.vector, z3_bf[:, STRIP:, :], 3, STRIP)
-        store(project(quantise(z3_bf[:, STRIP:, :], "z3_1", STRIP), 1), 3 * CHUNK + STRIP)
+        for v0 in (0, STRIP):
+            add(nc.vector, z3_bf[:, v0:v0 + STRIP, :], 3, v0)
+        for b in range(2):
+            store(project(quantise(z3_bf[:, b * STRIP:(b + 1) * STRIP, :], "z3_%d" % b, STRIP), b), 3 * CHUNK + b * STRIP)

@@ -234,18 +234,17 @@ def tile_picked_wdime_none_l_kernel(
                 nc.scalar.activation(h[t][:, half * BANK:(half + 1) * BANK], h_banks[t][half][:], SILU)
 
         gather_on_vector(0, 0, 0, wide[(0, 0)][:, 0, :])
-        gather_on_vector(0, 0, 2 * CHUNK, wide[(0, 2)][:, 0, :])
+        gather_on_vector(1, 0, 0, wide[(1, 0)][:, 0, :])
         gather_on_vector(1, 0, 2 * CHUNK, found[(1, 2)][:, 0, :])
         w3_bf = [held([P, 2 * P, PACK], BF16, "w3_bf%d" % u) for u in range(PAIRS)]
         for u in range(PAIRS):
             round_weights(nc.vector.tensor_copy, w3_raw, 2 * u, 2, w3_bf[u][:])
         for u in range(PAIRS):
             w3_q.extend(quantise(w3_bf[u][:], "w3_%d" % u, P))
-        for t in range(1, PACK):
-            gather_on_scalar(0, t, 0, wide[(0, 0)][:, t, :])
+        for d in range(LISTS):
+            for t in range(1, PACK):
+                gather_on_scalar(d, t, 0, wide[(d, 0)][:, t, :])
         for t in range(PACK):
-            gather_on_scalar(1, t, 0, wide[(1, 0)][:, t, :])
-        for t in range(1, PACK):
             gather_on_scalar(0, t, 2 * CHUNK, wide[(0, 2)][:, t, :])
         for c, tiles in ((2, range(1, PACK)), (3, range(PACK))):
             for t in tiles:

from contextlib import ExitStack

import concourse.mybir as mybir

K, T, H, N, J, U = 1024, 1024, 512, 128, 512, 2048
FLOPS = 2 * (K * H * T + J * H * U + H * N * T)

F32 = mybir.dt.float32
BF16 = mybir.dt.bfloat16
I32 = mybir.dt.int32
U32 = mybir.dt.uint32
U16 = mybir.dt.uint16
U8 = mybir.dt.uint8
FP8X4 = mybir.dt.float8_e4m3fn_x4
FP4X4 = mybir.dt.float4_e2m1fn_x4
COPY = mybir.ActivationFunctionType.Copy
SILU = mybir.ActivationFunctionType.Silu
MULT = mybir.AluOpType.mult
ADD = mybir.AluOpType.add

P = 128
PACK = 4
PASS = P * PACK
BANK = 512
CHUNK = 256
STRIP = 128
LISTS = 2
PAIRS = 2
PER_COLUMN = 16

UNIT = PACK * CHUNK * 4
REACH = 512
AT_TERMS = 0
AT_A_LAST = LISTS * UNIT - UNIT // 2
AT_A_BF = 4 * UNIT
AT_LAST_BF = AT_A_BF
AT_LAST_CODES = LISTS * UNIT
AT_W2_CODES = AT_LAST_CODES + UNIT // 4
AT_Z23 = AT_LAST_CODES + UNIT // 2


def tile_picked_wdime_none_l_kernel(
    tc, x_words, x_scales, aT, w1, w3, w2, pos1, pos2, out
):
    nc = tc.nc
    with ExitStack() as ctx:
        keep = ctx.enter_context(tc.tile_pool(name="keep", bufs=1))
        psum = ctx.enter_context(tc.psum_pool(name="psum", bufs=1))
        turns = ctx.enter_context(tc.tile_pool(name="turns", bufs=1))

        def new_bank(number):
            return psum.tile([P, BANK], F32, name="bank%d" % number, tag="bank%d" % number)

        def held(shape, dtype, name):
            return keep.tile(shape, dtype, name=name, tag=name, align_bytes=64)

        def placed(shape, dtype, name, offset):
            return turns.tile(shape, dtype, name=name, offset=offset, align_bytes=64)

        w1_raw = [held([P, PACK, H], F32, "w1_raw%d" % g) for g in range(K // PASS)]
        x_codes = [held([P, 2 * T], U8, "x_codes%d" % g) for g in range(K // PASS)]
        x_plane = held([P, K // PASS, T], U8, "x_plane")
        w3_raw = held([P, PACK, H], F32, "w3_raw")
        w2_raw = held([P, PACK, N], F32, "w2_raw")
        lists = [keep.tile([P, T // PER_COLUMN], U16, name="list%d" % d) for d in range(LISTS)]
        a_raw = {}

        def load_rows(tile, rows):
            nc.sync.dma_start(out=tile, in_=rows.rearrange("(p j) n -> p j n", j=PACK))

        def load_a(d, c, chunks, offset=None):
            shape, name = [P, PACK, chunks * CHUNK], "a_raw%d_%d" % (d, c)
            a_raw[(d, c)] = held(shape, F32, name) if offset is None else placed(shape, F32, name, offset)
            load_rows(a_raw[(d, c)][:], aT[:, d * T + c * CHUNK:d * T + (c + chunks) * CHUNK])

        def load_w1(g):
            load_rows(w1_raw[g][:], w1[g * PASS:(g + 1) * PASS, :])

        def load_x(g):
            nc.sync.dma_start(out=x_codes[g][:].bitcast(I32), in_=x_words[g].bitcast(I32))

        nc.gpsimd.memset(x_plane[:].bitcast(I32), 0)
        warm_in = held([P, 1], F32, "warm_in")
        warm_out = held([P, 1], F32, "warm_out")
        nc.vector.memset(warm_in[:], 0.0)
        nc.scalar.activation(warm_out[:], warm_in[:], SILU)

        load_w1(0)
        scale_rows = x_scales.rearrange("g (quad r) n -> r quad g n", r=4)
        for r in range(4):
            nc.sync.dma_start(out=x_plane[r:P:32, :, :].bitcast(I32), in_=scale_rows[r].bitcast(I32))
        load_x(0)
        load_w1(1)
        load_x(1)
        load_a(0, 0, 1)
        nc.sync.dma_start(lists[0][:], pos1)
        nc.sync.dma_start(lists[1][:], pos2)
        load_rows(w3_raw[:], w3)
        load_a(0, 1, 3)
        load_a(1, 0, 2)
        load_a(1, 2, 1, AT_A_LAST)
        load_a(1, 3, 1)
        w2_rows = w2.rearrange("(q t r) n -> r q t n", t=PACK, r=4)
        for r in range(4):
            nc.sync.dma_start(out=w2_raw[r:P:4, :, :], in_=w2_rows[r])

        def round_weights(copy, raw, t0, tiles, grouped):
            copy(
                out=grouped.rearrange("p (t q r) j -> p t q j r", t=tiles, r=4),
                in_=raw[:].rearrange("p j (q t r) -> p t q j r", t=PACK, r=4)[:, t0:t0 + tiles],
            )

        def round_columns(copy, raw, grouped):
            copy(
                out=grouped.rearrange("p (c e) j -> p c j e", e=2),
                in_=raw.rearrange("p j (c e) -> p c j e", e=2),
            )

        def round_on_gpsimd(raw, grouped):
            nc.gpsimd.tensor_scalar(grouped, raw[:].rearrange("p j c -> p c j"), 1.0, 0.0, MULT, ADD)

        def quantise_into(codes, plane, grouped):
            nc.vector.quantize_mx(out=codes.bitcast(FP8X4), scales=plane, in_=grouped.rearrange("p w j -> p (w j)"))

        def runs(codes, plane, width):
            return [(codes[:, at:at + width], plane[:, at:at + width]) for at in range(0, codes.shape[1], width)]

        def quantise(grouped, name, width, offset=None):
            shape = [P, grouped.shape[1]]
            codes = held(shape, U32, name + "_codes") if offset is None else placed(shape, U32, name + "_codes", offset)
            plane = held(shape, U8, name + "_plane")
            quantise_into(codes[:], plane[:], grouped)
            return runs(codes[:], plane[:], width)

        def multiply(result, stationary, moving):
            nc.tensor.matmul_mx(
                out=result,
                lhsT=stationary[0].bitcast(FP8X4),
                lhsT_scale=stationary[1],
                rhs=moving[0].bitcast(FP8X4),
                rhs_scale=moving[1],
                start=True,
                stop=True,
            )

        a_q = {}

        h = [held([P, T], F32, "h%d" % t) for t in range(PACK)]
        w3_q = []
        f = {}
        terms = {}
        wide = {}
        found = {}
        for d, c in ((0, 0), (1, 0), (0, 2)):
            wide[(d, c)] = held([P, PACK, 2 * CHUNK], F32, "wide%d_%d" % (d, c))
            for n in range(2):
                found[(d, c + n)] = wide[(d, c)][:, :, n * CHUNK:(n + 1) * CHUNK]
        found[(1, 2)] = held([P, PACK, CHUNK], F32, "found1_2")[:]
        found[(1, 3)] = held([P, PACK, CHUNK], F32, "found1_3")[:]

        def window(d, t, v0, width):
            return h[t][:].indirect(lists[d][:, v0 // PER_COLUMN:(v0 + width) // PER_COLUMN])

        def gather_on_scalar(d, t, v0, into):
            nc.scalar.activation(into, window(d, t, v0, into.shape[1]), COPY)

        def gather_on_vector(d, t, v0, into):
            nc.vector.tensor_copy(out=into, in_=window(d, t, v0, into.shape[1]))

        def filters(d, c, banks):
            for u in range(PAIRS):
                f[(d, c, u)] = new_bank(banks[u])
                for e in range(2):
                    multiply(f[(d, c, u)][:, e * CHUNK:(e + 1) * CHUNK], w3_q[2 * u + e], a_q[(d, c)])

        def weigh(d, c, u):
            nc.vector.tensor_tensor(
                terms[(d, c)][:, u],
                f[(d, c, u)][:].rearrange("p (e v) -> p v e", e=2),
                found[(d, c)][:, 2 * u:2 * u + 2, :].rearrange("p e v -> p v e"),
                MULT,
            )

        def add(engine, z, c, v0):
            width = z.shape[1]
            first, second = (terms[(d, c)][:, :, v0:v0 + width, :].rearrange("p u v e -> p v u e") for d in range(LISTS))
            engine.tensor_tensor(z.rearrange("p v (u e) -> p v u e", e=2), first, second, ADD)

        def project(parts, number):
            bank = new_bank(number)
            at = 0
            for part in parts:
                multiply(bank[:, at:at + part[0].shape[1]], w2_q, part)
                at = at + part[0].shape[1]
            return bank[:, 0:at]

        def store(bank, v0):
            width = bank.shape[1]
            result = held([P, width], F32, "result%d" % v0)
            nc.scalar.copy(out=result[:], in_=bank)
            nc.sync.dma_start(out=out[:, v0:v0 + width], in_=result[:])

        w1_bf = [[held([P, 2 * P, PACK], BF16, "w1_bf%d_%d" % (g, u)) for u in range(PAIRS)] for g in range(K // PASS)]
        round_weights(nc.vector.tensor_copy, w1_raw[0], 0, 2, w1_bf[0][0][:])
        round_weights(nc.scalar.copy, w1_raw[0], 2, 2, w1_bf[0][1][:])
        w1_q = [quantise(w1_bf[0][0][:], "w1_0_0", P) + quantise(w1_bf[0][1][:], "w1_0_1", P), []]
        for t in range(2):
            round_weights(nc.vector.tensor_copy, w1_raw[1], t, 1, w1_bf[1][0][:, t * P:(t + 1) * P, :])
        round_weights(nc.scalar.copy, w1_raw[1], 2, 2, w1_bf[1][1][:])
        for t in range(2):
            w1_q[1].extend(quantise(w1_bf[1][0][:, t * P:(t + 1) * P, :], "w1_1_tile%d" % t, P))
        w1_q[1].extend(quantise(w1_bf[1][1][:], "w1_1_1", P))
        h_banks = []
        for t in range(PACK):
            h_banks.append([new_bank(2 * t + half) for half in range(2)])
            passes = (0, 1) if t < 2 else (1, 0)
            for half in range(2):
                for g in passes:
                    nc.tensor.matmul_mx(
                        out=h_banks[t][half][:],
                        lhsT=w1_q[g][t][0].bitcast(FP8X4),
                        lhsT_scale=w1_q[g][t][1],
                        rhs=x_codes[g][:, 2 * half * BANK:2 * (half + 1) * BANK].bitcast(FP4X4),
                        rhs_scale=x_plane[:, g, half * BANK:(half + 1) * BANK],
                        start=(g == passes[0]),
                        stop=(g == passes[-1]),
                    )

        first_bf = held([P, CHUNK, PACK], BF16, "first_bf")
        round_columns(nc.vector.tensor_copy, a_raw[(0, 0)][:], first_bf[:])
        a_q[(0, 0)] = quantise(first_bf[:], "a0_0", CHUNK)[0]
        for t in range(PACK):
            for half in range(2):
                nc.scalar.activation(h[t][:, half * BANK:(half + 1) * BANK], h_banks[t][half][:], SILU)

        gather_on_vector(0, 0, 0, wide[(0, 0)][:, 0, :])
        gather_on_vector(1, 0, 0, wide[(1, 0)][:, 0, :])
        gather_on_vector(1, 0, 2 * CHUNK, found[(1, 2)][:, 0, :])
        w3_bf = [held([P, 2 * P, PACK], BF16, "w3_bf%d" % u) for u in range(PAIRS)]
        for u in range(PAIRS):
            round_weights(nc.vector.tensor_copy, w3_raw, 2 * u, 2, w3_bf[u][:])
        for u in range(PAIRS):
            w3_q.extend(quantise(w3_bf[u][:], "w3_%d" % u, P))
        for d in range(LISTS):
            for t in range(1, PACK):
                gather_on_scalar(d, t, 0, wide[(d, 0)][:, t, :])
        for t in range(PACK):
            gather_on_scalar(0, t, 2 * CHUNK, wide[(0, 2)][:, t, :])
        for c, tiles in ((2, range(1, PACK)), (3, range(PACK))):
            for t in tiles:
                gather_on_scalar(1, t, c * CHUNK, found[(1, c)][:, t, :])

        w2_bf = held([P, N, PACK], BF16, "w2_bf")
        round_columns(nc.scalar.copy, w2_raw[:], w2_bf[:])

        def round_halves(raw, grouped):
            half = raw.shape[2] // 2
            for at in (0, half):
                round_columns(nc.vector.tensor_copy, raw[:, :, at:at + half], grouped[:, at:at + half, :])

        def quantise_parts(grouped, name, ends):
            codes = held([P, ends[-1]], U32, name + "_codes")
            plane = held([P, ends[-1]], U8, name + "_plane")
            for at, end in zip([0] + ends[:-1], ends):
                quantise_into(codes[:, at:end], plane[:, at:end], grouped[:, at:end, :])
            return runs(codes[:], plane[:], CHUNK)

        rest_bf = held([P, 3 * CHUNK, PACK], BF16, "rest_bf")
        round_halves(a_raw[(0, 1)][:], rest_bf[:])
        a_q[(0, 1)], a_q[(0, 2)], a_q[(0, 3)] = quantise_parts(rest_bf, "rest", [3 * STRIP, 6 * STRIP])
        a_bf = placed([P, 3 * CHUNK, PACK], BF16, "a_bf", AT_A_BF)
        round_halves(a_raw[(1, 0)][:], a_bf[:, 0:2 * CHUNK, :])
        round_halves(a_raw[(1, 2)][:], a_bf[:, 2 * CHUNK:, :])
        a_q[(1, 0)], a_q[(1, 1)], a_q[(1, 2)] = quantise_parts(a_bf, "second", [2 * STRIP, 5 * STRIP, 6 * STRIP])
        for c in range(2):
            for d in range(LISTS):
                filters(d, c, [LISTS * PAIRS * c + PAIRS * d + u for u in range(PAIRS)])

        for c in range(2):
            early_terms = placed([P, LISTS, PAIRS, CHUNK, 2], F32, "early_terms%d" % c, AT_TERMS + c * LISTS * UNIT)
            for d in range(LISTS):
                terms[(d, c)] = early_terms[:, d]
        for c in range(2, 4):
            for d in range(LISTS):
                terms[(d, c)] = held([P, PAIRS, CHUNK, 2], F32, "terms%d_%d" % (d, c))[:]
        last_bf = placed([P, CHUNK, PACK], BF16, "last_bf", AT_LAST_BF)
        z01_bf = held([P, 2 * CHUNK, PACK], BF16, "z01_bf")
        round_on_gpsimd(a_raw[(1, 3)], last_bf[:])
        for d, c, u in ((0, 0, 1), (0, 0, 0), (1, 0, 1), (1, 0, 0)):
            weigh(d, c, u)
        add(nc.gpsimd, z01_bf[:, 0:CHUNK, :], 0, 0)
        for d, c, u in ((0, 1, 1), (0, 1, 0), (1, 1, 1), (1, 1, 0)):
            weigh(d, c, u)
        add(nc.gpsimd, z01_bf[:, CHUNK:, :], 1, 0)
        filters(0, 3, (1, 3))
        filters(1, 2, (2, 5))
        filters(0, 2, (0, 4))
        for d, c, u in ((0, 2, 0), (0, 3, 0), (0, 2, 1), (0, 3, 1), (1, 2, 0), (1, 2, 1)):
            weigh(d, c, u)

        a_q[(1, 3)] = quantise(last_bf[:], "last", CHUNK, AT_LAST_CODES)[0]
        filters(1, 3, (7, 6))
        z23_bf = placed([P, 2 * CHUNK, PACK], BF16, "z23_bf", AT_Z23)
        add(nc.vector, z23_bf[:, 0:CHUNK, :], 2, 0)
        z01_q = quantise(z01_bf[:], "z01", 2 * CHUNK)
        weigh(1, 3, 0)
        w2_q = quantise(w2_bf[:], "w2", N, AT_W2_CODES)[0]
        store(project(z01_q, 4), 0)
        weigh(1, 3, 1)
        store(project(quantise(z23_bf[:, 0:CHUNK, :], "z2", CHUNK), 3), 2 * CHUNK)
        z3_bf = z23_bf[:, CHUNK:, :]
        for v0 in (0, STRIP):
            add(nc.vector, z3_bf[:, v0:v0 + STRIP, :], 3, v0)
        for b in range(2):
            store(project(quantise(z3_bf[:, b * STRIP:(b + 1) * STRIP, :], "z3_%d" % b, STRIP), b), 3 * CHUNK + b * STRIP)
